import numpy as np
import ml_dtypes


def mxq(x, axis, fmt="e4m3"):
    dtype, down = {"e4m3": (ml_dtypes.float8_e4m3fn, 7), "e5m2": (ml_dtypes.float8_e5m2, 14)}[fmt]
    v = np.moveaxis(np.asarray(x, np.float32).astype(ml_dtypes.bfloat16).astype(np.float64), axis, -1)
    blocks = v.reshape(v.shape[:-1] + (-1, 32))
    amax = np.abs(blocks).max(-1, keepdims=True)
    byte = np.maximum(np.where(amax > 0, np.frexp(amax)[1] - 1 + 127, 0) - down, 1)
    scale = np.exp2(byte - 127.0)
    codes = (blocks / scale).astype(np.float32).astype(dtype).astype(np.float64)
    return np.moveaxis((codes * scale).reshape(v.shape), -1, axis)


WIDE = False


def mx_kscale(k):
    if not WIDE:
        return np.ones(k)
    levels = np.array([10, -10, 5, -5, 0])
    if k % 512:
        return np.exp2(np.random.permutation(np.resize(levels, k // 32))).repeat(32)
    a = np.empty((k // 512, 16))
    for p in range(k // 512):
        a[p, :8] = np.random.permutation(np.resize(levels, 8))
        for g in range(8):
            far = levels[np.abs(levels - a[p, g]) >= 10]
            a[p, g + 8] = far[np.random.randint(len(far))]
    return np.exp2(a.ravel()).repeat(32)


BF16 = ml_dtypes.bfloat16


def bf(x):
    return np.asarray(x, np.float32).astype(BF16)


def f64(x):
    return np.asarray(x).astype(np.float64)

def planes(Y):
    n, m = Y.shape
    b = f64(bf(Y)).reshape(n // 32, 32, m)
    amax = np.abs(b).max(1)
    byte = np.clip(np.where(amax > 0, np.frexp(amax)[1] - 1 + 127 - 7, 1), 1, 254)
    codes = (b * np.exp2(127.0 - byte)[:, None, :]).reshape(n, m).astype(np.float32).astype(ml_dtypes.float8_e4m3fn).view(np.uint8)
    words = codes.reshape(n // 512, 128, 4, m).transpose(0, 1, 3, 2)
    return np.ascontiguousarray(words), np.ascontiguousarray(byte.astype(np.uint8).reshape(n // 512, 16, m))


N, M, P = 1024, 1024, 512


def dress_left(t, g, b):
    y = mxq(t, 1, "e4m3") @ mxq(g[:, None] * b, 0, "e4m3")
    return b + y


def dress_right(t, g, b):
    y = mxq(t, 0, "e4m3").T @ mxq(g[:, None] * b, 0, "e4m3")
    return b + y


def setup_inputs():
    s, u, t = mx_kscale(N), mx_kscale(M), mx_kscale(P)
    return {
        "ta": bf(np.random.standard_normal((N, N)) / np.sqrt(N) / s[None, :]),
        "tb": bf(np.random.standard_normal((M, M)) / np.sqrt(M) / u[:, None]),
        "ba": bf(np.random.standard_normal((N, P)) * P ** -0.25 * t[None, :]),
        "bb": bf(np.random.standard_normal((M, P)) * P ** -0.25 / t[None, :]),
        "ga": bf((1.0 + 0.1 * np.random.standard_normal(N)) * s),
        "gb": bf((1.0 + 0.1 * np.random.standard_normal(M)) * u),
        "delta": bf(np.random.uniform(0.5, 1.5, (N, M))),
    }


def core(ta, tb, ba, bb, ga, gb, delta):
    xa = dress_left(f64(ta), f64(ga), f64(ba))
    xb = dress_right(f64(tb), f64(gb), f64(bb))
    r = mxq(xa, 1, "e4m3") @ mxq(xb, 1, "e4m3").T
    tab = -r / f64(delta)
    return tab


def reference(ta, tb, ba, bb, ga, gb, delta):
    R_out = core(ta, tb, ba, bb, ga, gb, delta)
    words, scales = planes(R_out.T)
    return R_out, words, scales

@@ -1,0 +1,441 @@
+from contextlib import ExitStack
+
+import concourse.mybir as mybir
+from concourse.masks import make_identity
+
+F32 = mybir.dt.float32
+BF16 = mybir.dt.bfloat16
+I32 = mybir.dt.int32
+U32 = mybir.dt.uint32
+U8 = mybir.dt.uint8
+FP8X4 = mybir.dt.float8_e4m3fn_x4
+ALU = mybir.AluOpType
+ACT = mybir.ActivationFunctionType
+
+N, M, P = 1024, 1024, 512
+FLOPS = 2 * N * N * P + 2 * M * M * P + 2 * N * M * P
+BLOCKS = N // 128
+NS = (2, 5, 6)
+
+
+def tile_opposedspindirectringamplitudeupdate_x1_kernel(tc, ta, tb, ba, bb, ga, gb, delta, out_0, out_1, out_2):
+    nc = tc.nc
+    with ExitStack() as ctx:
+        keep = ctx.enter_context(tc.tile_pool(name="keep", bufs=1))
+        pool = ctx.enter_context(tc.tile_pool(name="work", bufs=2))
+        psum = ctx.enter_context(tc.psum_pool(name="psum", bufs=2))
+
+        def keep_tile(shape, dtype, name):
+            return keep.tile(shape, dtype, name=name, align_bytes=64)
+
+        ident = keep_tile([128, 128], F32, "ident")
+        graw, gf, raw, btr, gcodes, gscale = {}, {}, {}, {}, {}, {}
+        for s in ("b", "a"):
+            graw[s] = keep_tile([128, 2, 4], BF16, "graw" + s)
+            gf[s] = keep_tile([128, 2, 4], F32, "gf" + s)
+            btr[s] = keep_tile([128, 1024, 4], BF16, "btr" + s)
+            for c in range(2):
+                raw[s, c] = keep_tile([128, 4, P], BF16, "raw%s%d" % (s, c))
+                gcodes[s, c] = keep_tile([128, P], U32, "gcodes%s%d" % (s, c))
+                gscale[s, c] = keep_tile([128, P], U8, "gscale%s%d" % (s, c))
+        tbr = [pool.tile([128, 4, M], BF16, name="tbr%d" % c, tag="big", bufs=4, align_bytes=64) for c in range(2)]
+        tar = [keep_tile([128, 2, N], BF16, "tar%d" % i) for i in range(4)]
+        dr = [keep_tile([128, M], BF16, "dr%d" % b) for b in range(8)]
+        tbcodes = [keep_tile([128, M], U32, "tbcodes%d" % c) for c in range(2)]
+        tbscale = [keep_tile([128, M], U8, "tbscale%d" % c) for c in range(2)]
+        xbcodes = keep_tile([128, M], U32, "xbcodes")
+        xbscale = keep_tile([128, M], U8, "xbscale")
+        pcodes = keep_tile([128, 2, N], U32, "pcodes")
+        pscale = keep_tile([128, 2, N], U8, "pscale")
+        warm = keep.tile([128, 1], F32, name="warm")
+        spare = psum.tile([128, 512], F32, name="spare", bufs=1)
+
+        make_identity(nc, ident[:])
+        with tc.manual_schedule():
+            nc.scalar.dma_start(out=graw["b"][:], in_=gb.rearrange("(c p j) -> p c j", p=128, j=4))
+            nc.scalar.dma_start(out=graw["a"][:], in_=ga.rearrange("(c p j) -> p c j", p=128, j=4))
+            def load_raw(s, x, c):
+                nc.sync.dma_start(out=raw[s, c][:], in_=x[512 * c : 512 * (c + 1), :].rearrange("(p j) w -> p j w", j=4))
+
+            def load_delta(b):
+                nc.sync.dma_start(out=dr[b][:], in_=delta[128 * b : 128 * (b + 1), :])
+
+            def load_ta(q):
+                nc.sync.dma_start(out=tar[q][:], in_=ta[256 * q : 256 * (q + 1), :].rearrange("(b p) k -> p b k", p=128))
+
+            load_raw("b", bb, 0)
+            load_raw("b", bb, 1)
+            for c in range(2):
+                nc.sync.dma_start(out=tbr[c][:], in_=tb[512 * c : 512 * (c + 1), :].rearrange("(p j) w -> p j w", j=4))
+            load_delta(0)
+            load_raw("a", ba, 0)
+            load_ta(0)
+            load_raw("a", ba, 1)
+            load_delta(1)
+            load_ta(1)
+            load_delta(2)
+            load_ta(2)
+            load_delta(3)
+            load_ta(3)
+            for b in range(4, 8):
+                load_delta(b)
+
+            gm = {}
+            gi = {}
+
+            def factor_mult(s, c, engine="v"):
+                gm[s, c] = pool.tile([128, 4, P], BF16, name="gm", align_bytes=64)
+                for j in range(4):
+                    if engine == "v":
+                        nc.vector.tensor_scalar(
+                            out=gm[s, c][:, j, :], in0=raw[s, c][:, j, :], scalar1=gf[s][:, c, j : j + 1], scalar2=None, op0=ALU.mult
+                        )
+                    else:
+                        nc.scalar.activation(
+                            out=gm[s, c][:, j, :], in_=raw[s, c][:, j, :], func=ACT.Copy, scale=gf[s][:, c, j : j + 1]
+                        )
+
+            def interleave(engine, dst, src):
+                copy = nc.vector.tensor_copy if engine == "v" else nc.scalar.copy
+                copy(out=dst, in_=src.rearrange("p j w -> p w j"))
+
+            def factor_copy(s, c):
+                gi[s, c] = pool.tile([128, 4, 128, 4], BF16, name="gi", align_bytes=64)
+                nc.vector.tensor_copy(out=gi[s, c][:], in_=gm[s, c][:].rearrange("p j (m t) -> p t m j", t=4))
+
+            def turn_b(s, c, h):
+                words = raw[s, c][:].rearrange("p j w -> p (j w)").bitcast(F32)
+                bank = psum.tile([128, 4, 128], F32, name="turn", bufs=3)
+                for jj in range(2):
+                    for u in range(2):
+                        j = 2 * h + jj
+                        nc.tensor.transpose(bank[:, 2 * jj + u, :], words[:, 256 * j + u : 256 * (j + 1) : 2], ident[:])
+                dst = btr[s][:].rearrange("p n f -> p (n f)").bitcast(F32)
+                dst = dst[:, 1024 * c : 1024 * (c + 1)].rearrange("p (q r) -> p q r", r=8)[:, :, 4 * h : 4 * h + 4]
+                nc.scalar.copy(out=dst, in_=bank[:].rearrange("p r q -> p q r"))
+
+            def factor_quantise(s, c):
+                nc.vector.quantize_mx(
+                    out=gcodes[s, c][:].bitcast(FP8X4), scales=gscale[s, c][:], in_=gi[s, c][:].rearrange("p t m j -> p (t m j)")
+                )
+
+            ti = {}
+
+            def tb_copy(c, h, engine):
+                ti[c, h] = pool.tile([128, 512, 4], BF16, name="ti", bufs=4, align_bytes=64)
+                interleave(engine, ti[c, h][:], tbr[c][:, :, 512 * h : 512 * (h + 1)])
+
+            def tb_quantise(c, h):
+                cols = slice(512 * h, 512 * (h + 1))
+                nc.vector.quantize_mx(
+                    out=tbcodes[c][:, cols].bitcast(FP8X4), scales=tbscale[c][:, cols], in_=ti[c, h][:].rearrange("p w j -> p (w j)")
+                )
+
+            def busy(n):
+                for i in range(n):
+                    nc.tensor.matmul_mx(
+                        out=spare[:],
+                        lhsT=gcodes["b", 0][:, 0:128].bitcast(FP8X4),
+                        lhsT_scale=gscale["b", 0][:, 0:128],
+                        rhs=gcodes["b", 0][:].bitcast(FP8X4),
+                        rhs_scale=gscale["b", 0][:],
+                        start=True,
+                        stop=True,
+                    )
+
+            def word_view(tile_ap):
+                return tile_ap.rearrange("p c n f -> p (c n f)").bitcast(F32).rearrange("p (c n u) -> p c n u", c=2, u=2)
+
+            tat, tac = {}, {}
+
+            def turn_ta(b):
+                words = tar[b // 2][:, b % 2, :].bitcast(F32)
+                bank = psum.tile([128, 4, 128], F32, name="turn", bufs=3)
+                for c in range(2):
+                    for u in range(2):
+                        nc.tensor.transpose(bank[:, 2 * c + u, :], words[:, 256 * c + u : 256 * (c + 1) : 2], ident[:])
+                half = slice(128 * (b % 2), 128 * (b % 2) + 128)
+                if b % 2 == 0:
+                    tat[b // 2] = pool.tile([128, 2, 256, 4], BF16, name="tat", bufs=4, align_bytes=64)
+                nc.scalar.copy(out=word_view(tat[b // 2][:])[:, :, half, :], in_=bank[:].rearrange("p (c u) n -> p c n u", c=2))
+
+            def ta_quantise(q):
+                codes = pool.tile([128, 2, 256], U32, name="tacodes", bufs=4, align_bytes=64)
+                scale = pool.tile([128, 2, 256], U8, name="tascale", bufs=4, align_bytes=64)
+                nc.vector.quantize_mx(
+                    out=codes[:].rearrange("p c n -> p (c n)").bitcast(FP8X4),
+                    scales=scale[:].rearrange("p c n -> p (c n)"),
+                    in_=tat[q][:].rearrange("p c n f -> p (c n f)"),
+                )
+                tac[q] = codes, scale
+
+            bank_of = {}
+            xt = {}
+
+            def dress_mm(s, b):
+                bank = psum.tile([128, 4, 128], F32, name="dress", tag="mm", bufs=4)
+                for t in range(4):
+                    cols = slice(128 * t, 128 * (t + 1))
+                    for c in range(2):
+                        if s == "b":
+                            own = slice(128 * b, 128 * (b + 1))
+                            codes, scale = tbcodes[c][:, own], tbscale[c][:, own]
+                        else:
+                            own = slice(128 * (b % 2), 128 * (b % 2) + 128)
+                            codes, scale = tac[b // 2][0][:, c, own], tac[b // 2][1][:, c, own]
+                        nc.tensor.matmul_mx(
+                            out=bank[:, t, :],
+                            lhsT=gcodes[s, c][:, cols].bitcast(FP8X4),
+                            lhsT_scale=gscale[s, c][:, cols],
+                            rhs=codes.bitcast(FP8X4),
+                            rhs_scale=scale,
+                            start=(c == 0),
+                            stop=(c == 1),
+                        )
+                bank_of[s, b] = bank
+
+            def dress_add(s, b):
+                if s == "b":
+                    if b % 4 == 0:
+                        xt[s, b // 4] = pool.tile([128, 512, 4], BF16, name="xtb", bufs=2, align_bytes=64)
+                    out = xt[s, b // 4][:, 128 * (b % 4) : 128 * (b % 4) + 128, :]
+                else:
+                    xt[s, b] = pool.tile([128, 128, 4], BF16, name="xta", bufs=3, align_bytes=64)
+                    out = xt[s, b][:]
+                nc.vector.tensor_tensor(
+                    out=out,
+                    in0=bank_of[s, b][:].rearrange("p t n -> p n t"),
+                    in1=btr[s][:, 128 * b : 128 * (b + 1), :],
+                    op=ALU.add,
+                )
+
+            def xb_quantise(h):
+                cols = slice(512 * h, 512 * (h + 1))
+                nc.vector.quantize_mx(
+                    out=xbcodes[:, cols].bitcast(FP8X4), scales=xbscale[:, cols], in_=xt["b", h][:].rearrange("p n f -> p (n f)")
+                )
+
+            xac = {}
+
+            def xa_quantise(b):
+                codes = pool.tile([128, 128], U32, name="xacodes", bufs=3, align_bytes=64)
+                scale = pool.tile([128, 128], U8, name="xascale", bufs=3, align_bytes=64)
+                nc.vector.quantize_mx(out=codes[:].bitcast(FP8X4), scales=scale[:], in_=xt["a", b][:].rearrange("p n f -> p (n f)"))
+                xac[b] = codes, scale
+
+            recs = {}
+
+            def root(b):
+                if b % 2 == 0:
+                    recs[b // 2] = pool.tile([128, 2, M], F32, name="recs", tag="big", bufs=4, align_bytes=64)
+                nc.scalar.activation(out=recs[b // 2][:, b % 2, :], in_=dr[b][:], func=ACT.Abs_reciprocal_sqrt)
+
+            def square(b):
+                rec = recs[b // 2][:, b % 2, :]
+                nc.scalar.activation(out=rec, in_=rec, func=ACT.Square)
+
+            prod = {}
+
+            def product(b, h):
+                cols = slice(512 * h, 512 * (h + 1))
+                bank = psum.tile([128, 512], F32, name="prod", tag="mm", bufs=4)
+                nc.tensor.matmul_mx(
+                    out=bank[:],
+                    lhsT=xac[b][0][:].bitcast(FP8X4),
+                    lhsT_scale=xac[b][1][:],
+                    rhs=xbcodes[:, cols].bitcast(FP8X4),
+                    rhs_scale=xbscale[:, cols],
+                    start=True,
+                    stop=True,
+                )
+                prod[b, h] = bank
+
+            r, rb = {}, {}
+
+            def divide(b, h):
+                cols = slice(512 * h, 512 * (h + 1))
+                if h == 0:
+                    r[b] = pool.tile([128, M], F32, name="r", bufs=3)
+                    rb[b] = pool.tile([128, M], BF16, name="rb", bufs=2)
+                nc.vector.scalar_tensor_tensor(
+                    out=r[b][:, cols], in0=prod[b, h][:], scalar=-1.0, in1=recs[b // 2][:, b % 2, cols], op0=ALU.mult, op1=ALU.mult
+                )
+
+            def narrow(b, g0, g1, engine="v"):
+                pairs = slice(128 * g0, 128 * g1)
+                copy = nc.vector.tensor_copy if engine == "v" else nc.scalar.copy
+                copy(
+                    out=rb[b][:].rearrange("p (u w e) -> p u w e", u=2, e=2)[:, :, pairs, :],
+                    in_=r[b][:].rearrange("p (w u e) -> p u w e", u=2, e=2)[:, :, pairs, :],
+                )
+
+            pb, pt = {}, {}
+
+            def turn_p(b, g):
+                words = rb[b][:].bitcast(F32)
+                if g == 0:
+                    pb[b] = psum.tile([128, 4, 128], F32, name="turn", bufs=3)
+                for u in range(2):
+                    first = 256 * u + 128 * g
+                    nc.tensor.transpose(pb[b][:, 2 * g + u, :], words[:, first : first + 128], ident[:])
+
+            def p_words(b, g0, g1):
+                half = slice(128 * (b % 2), 128 * (b % 2) + 128)
+                if b % 2 == 0 and g0 == 0:
+                    pt[b // 2] = pool.tile([128, 2, 256, 4], BF16, name="pt", bufs=2, align_bytes=64)
+                nc.scalar.copy(
+                    out=word_view(pt[b // 2][:])[:, g0:g1, half, :],
+                    in_=pb[b][:, 2 * g0 : 2 * g1, :].rearrange("p (c u) n -> p c n u", u=2),
+                )
+
+            def p_quantise(b0, b1, g):
+                cols = slice(128 * b0, 128 * b1)
+                own = slice(128 * (b0 % 2), 128 * (b0 % 2) + 128 * (b1 - b0))
+                nc.vector.quantize_mx(
+                    out=pcodes[:, g, cols].bitcast(FP8X4),
+                    scales=pscale[:, g, cols],
+                    in_=pt[b0 // 2][:, g, own, :].rearrange("p n f -> p (n f)"),
+                )
+
+            def store_r(b, c0, c1):
+                nc.sync.dma_start(out=out_0[128 * b : 128 * (b + 1), c0:c1], in_=r[b][:, c0:c1])
+
+            def store_codes(b0, b1):
+                cols = slice(128 * b0, 128 * b1)
+                nc.sync.dma_start(
+                    out=out_1[:, :, cols, :].rearrange("g p n f -> p g (n f)").bitcast(I32), in_=pcodes[:, :, cols].bitcast(I32)
+                )
+
+            def store_scales(b0, b1, queues):
+                cols = slice(128 * b0, 128 * b1)
+                for quad in range(4):
+                    queues[quad % 2].dma_start(
+                        out=out_2[:, 4 * quad : 4 * quad + 4, cols].rearrange("g r n -> r g n").bitcast(I32),
+                        in_=pscale[32 * quad : 32 * quad + 4, :, cols].bitcast(I32),
+                    )
+
+            def p_pair(q):
+                p_quantise(2 * q, 2 * q + 2, 0)
+                p_quantise(2 * q, 2 * q + 2, 1)
+                store_codes(2 * q, 2 * q + 2)
+                if q == 2:
+                    store_scales(0, 6, (nc.sync, nc.sync))
+
+
+            nc.vector.memset(warm[:], 1.0)
+            nc.scalar.activation(out=warm[:], in_=warm[:], func=ACT.Abs_reciprocal_sqrt)
+            nc.vector.tensor_copy(out=gf["b"][:], in_=graw["b"][:])
+            turn_b("b", 0, 0)
+            turn_b("b", 0, 1)
+            turn_b("b", 1, 0)
+            turn_b("b", 1, 1)
+            factor_mult("b", 0)
+            factor_mult("b", 1)
+            factor_copy("b", 0)
+            tb_copy(0, 1, "s")
+            tb_copy(1, 0, "s")
+            factor_quantise("b", 0)
+            busy(3)
+            tb_copy(0, 0, "v")
+            tb_copy(1, 1, "s")
+            factor_copy("b", 1)
+            nc.vector.tensor_copy(out=gf["a"][:], in_=graw["a"][:])
+            turn_b("a", 0, 1)
+            tb_quantise(0, 0)
+            factor_quantise("b", 1)
+            factor_mult("a", 0)
+            busy(1)
+            turn_ta(0)
+            turn_ta(1)
+            tb_quantise(0, 1)
+            root(0)
+            tb_quantise(1, 0)
+            for b in range(4): dress_mm("b", b)
+            factor_copy("a", 0)
+            factor_mult("a", 1)
+            factor_quantise("a", 0)
+            turn_b("a", 0, 0)
+            root(1)
+            dress_add("b", 0)
+            dress_add("b", 1)
+            factor_copy("a", 1)
+            square(0)
+            tb_quantise(1, 1)
+            factor_quantise("a", 1)
+            ta_quantise(0)
+            turn_b("a", 1, 1)
+            turn_ta(2)
+            turn_ta(3)
+            root(2)
+            root(3)
+            dress_mm("b", 4)
+            dress_mm("b", 5)
+            dress_add("b", 2)
+            dress_add("b", 3)
+            square(2)
+            dress_mm("a", 0)
+            dress_add("b", 4)
+            dress_mm("b", 6)
+            dress_mm("b", 7)
+            xb_quantise(0)
+            turn_ta(4)
+            turn_b("a", 1, 0)
+            dress_add("a", 0)
+            dress_add("b", 5)
+            dress_add("b", 6)
+            turn_ta(5)
+            dress_add("b", 7)
+            dress_mm("a", 1)
+            xa_quantise(0)
+            xb_quantise(1)
+            ta_quantise(1)
+            dress_add("a", 1)
+            product(0, 0)
+            product(0, 1)
+            dress_mm("a", 2)
+            busy(1)
+            square(1)
+            last = BLOCKS - 1
+            for i in range(BLOCKS):
+                if i < 4:
+                    root(i + 4)
+                divide(i, 0)
+                if i < 2:
+                    turn_ta(i + 6)
+                if i < last:
+                    xa_quantise(i + 1)
+                if i in (3, 5, 7):
+                    p_pair(i // 2 - 1)
+                if i >= 1:
+                    turn_p(i - 1, 0)
+                if i >= 1:
+                    turn_p(i - 1, 1)
+                if i < last:
+                    product(i + 1, 0)
+                divide(i, 1)
+                if i >= 1:
+                    p_words(i - 1, 0, 2)
+                if i < 6:
+                    dress_add("a", i + 2)
+                store_r(i, 0, M)
+                if i < last:
+                    product(i + 1, 1)
+                if i < 5:
+                    dress_mm("a", i + 3)
+                narrow(i, 0, 2, "s" if i in NS else "v")
+                if i < 5:
+                    square(i + 3)
+                busy(1 if i < 5 else 2)
+                if i in (0, 2):
+                    ta_quantise(2 + i // 2)
+            p_quantise(6, 7, 0)
+            p_quantise(6, 7, 1)
+            store_codes(6, 7)
+            turn_p(last, 0)
+            turn_p(last, 1)
+            p_words(last, 0, 1)
+            p_quantise(7, 8, 0)
+            p_words(last, 1, 2)
+            p_quantise(7, 8, 1)
+            store_codes(7, 8)
+            store_scales(6, 8, (nc.sync, nc.scalar))

@@ -48,7 +48,6 @@ def tile_opposedspindirectringamplitudeupdate_x1_kernel(tc, ta, tb, ba, bb, ga, 
         pcodes = keep_tile([128, 2, N], U32, "pcodes")
         pscale = keep_tile([128, 2, N], U8, "pscale")
         warm = keep.tile([128, 1], F32, name="warm")
-        spare = psum.tile([128, 512], F32, name="spare", bufs=1)
 
         make_identity(nc, ident[:])
         with tc.manual_schedule():
@@ -130,18 +129,6 @@ def tile_opposedspindirectringamplitudeupdate_x1_kernel(tc, ta, tb, ba, bb, ga, 
                 nc.vector.quantize_mx(
                     out=tbcodes[c][:, cols].bitcast(FP8X4), scales=tbscale[c][:, cols], in_=ti[c, h][:].rearrange("p w j -> p (w j)")
                 )
-
-            def busy(n):
-                for i in range(n):
-                    nc.tensor.matmul_mx(
-                        out=spare[:],
-                        lhsT=gcodes["b", 0][:, 0:128].bitcast(FP8X4),
-                        lhsT_scale=gscale["b", 0][:, 0:128],
-                        rhs=gcodes["b", 0][:].bitcast(FP8X4),
-                        rhs_scale=gscale["b", 0][:],
-                        start=True,
-                        stop=True,
-                    )
 
             def word_view(tile_ap):
                 return tile_ap.rearrange("p c n f -> p (c n f)").bitcast(F32).rearrange("p (c n u) -> p c n u", c=2, u=2)
@@ -335,7 +322,6 @@ def tile_opposedspindirectringamplitudeupdate_x1_kernel(tc, ta, tb, ba, bb, ga, 
             tb_copy(0, 1, "s")
             tb_copy(1, 0, "s")
             factor_quantise("b", 0)
-            busy(3)
             tb_copy(0, 0, "v")
             tb_copy(1, 1, "s")
             factor_copy("b", 1)
@@ -344,7 +330,6 @@ def tile_opposedspindirectringamplitudeupdate_x1_kernel(tc, ta, tb, ba, bb, ga, 
             tb_quantise(0, 0)
             factor_quantise("b", 1)
             factor_mult("a", 0)
-            busy(1)
             turn_ta(0)
             turn_ta(1)
             tb_quantise(0, 1)
@@ -393,7 +378,6 @@ def tile_opposedspindirectringamplitudeupdate_x1_kernel(tc, ta, tb, ba, bb, ga, 
             product(0, 0)
             product(0, 1)
             dress_mm("a", 2)
-            busy(1)
             square(1)
             last = BLOCKS - 1
             for i in range(BLOCKS):
@@ -425,7 +409,6 @@ def tile_opposedspindirectringamplitudeupdate_x1_kernel(tc, ta, tb, ba, bb, ga, 
                 narrow(i, 0, 2, "s" if i in NS else "v")
                 if i < 5:
                     square(i + 3)
-                busy(1 if i < 5 else 2)
                 if i in (0, 2):
                     ta_quantise(2 + i // 2)
             p_quantise(6, 7, 0)

@@ -15,7 +15,6 @@ ACT = mybir.ActivationFunctionType
 N, M, P = 1024, 1024, 512
 FLOPS = 2 * N * N * P + 2 * M * M * P + 2 * N * M * P
 BLOCKS = N // 128
-NS = (2, 5, 6)
 
 
 def tile_opposedspindirectringamplitudeupdate_x1_kernel(tc, ta, tb, ba, bb, ga, gb, delta, out_0, out_1, out_2):
@@ -29,32 +28,42 @@ def tile_opposedspindirectringamplitudeupdate_x1_kernel(tc, ta, tb, ba, bb, ga, 
             return keep.tile(shape, dtype, name=name, align_bytes=64)
 
         ident = keep_tile([128, 128], F32, "ident")
-        graw, gf, raw, btr, gcodes, gscale = {}, {}, {}, {}, {}, {}
+        gain, rows4, rows1, gcodes, gscale = {}, {}, {}, {}, {}
         for s in ("b", "a"):
-            graw[s] = keep_tile([128, 2, 4], BF16, "graw" + s)
-            gf[s] = keep_tile([128, 2, 4], F32, "gf" + s)
-            btr[s] = keep_tile([128, 1024, 4], BF16, "btr" + s)
+            gain[s] = keep_tile([128, 2, 4], BF16, "gain" + s)
             for c in range(2):
-                raw[s, c] = keep_tile([128, 4, P], BF16, "raw%s%d" % (s, c))
+                rows4[s, c] = keep_tile([128, 4, P], BF16, "rows4%s%d" % (s, c))
+                rows1[s, c] = keep_tile([128, 4, P], BF16, "rows1%s%d" % (s, c))
                 gcodes[s, c] = keep_tile([128, P], U32, "gcodes%s%d" % (s, c))
                 gscale[s, c] = keep_tile([128, P], U8, "gscale%s%d" % (s, c))
-        tbr = [pool.tile([128, 4, M], BF16, name="tbr%d" % c, tag="big", bufs=4, align_bytes=64) for c in range(2)]
-        tar = [keep_tile([128, 2, N], BF16, "tar%d" % i) for i in range(4)]
-        dr = [keep_tile([128, M], BF16, "dr%d" % b) for b in range(8)]
+        tbr = [keep_tile([128, 4, M], BF16, "tbr%d" % c) for c in range(2)]
+        tar = [keep_tile([128, 2, N], BF16, "tar%d" % q) for q in range(4)]
+        dr = [keep_tile([128, M], BF16, "dr%d" % b) for b in range(BLOCKS)]
+        rec = [keep_tile([128, M], F32, "rec%d" % b) for b in range(BLOCKS)]
         tbcodes = [keep_tile([128, M], U32, "tbcodes%d" % c) for c in range(2)]
         tbscale = [keep_tile([128, M], U8, "tbscale%d" % c) for c in range(2)]
-        xbcodes = keep_tile([128, M], U32, "xbcodes")
-        xbscale = keep_tile([128, M], U8, "xbscale")
+        tacodes = [keep_tile([128, 2, 256], U32, "tacodes%d" % q) for q in range(4)]
+        tascale = [keep_tile([128, 2, 256], U8, "tascale%d" % q) for q in range(4)]
+        xcodes = {s: keep_tile([128, M], U32, "xcodes" + s) for s in ("b", "a")}
+        xscale = {s: keep_tile([128, M], U8, "xscale" + s) for s in ("b", "a")}
         pcodes = keep_tile([128, 2, N], U32, "pcodes")
         pscale = keep_tile([128, 2, N], U8, "pscale")
-        warm = keep.tile([128, 1], F32, name="warm")
 
         make_identity(nc, ident[:])
         with tc.manual_schedule():
-            nc.scalar.dma_start(out=graw["b"][:], in_=gb.rearrange("(c p j) -> p c j", p=128, j=4))
-            nc.scalar.dma_start(out=graw["a"][:], in_=ga.rearrange("(c p j) -> p c j", p=128, j=4))
-            def load_raw(s, x, c):
-                nc.sync.dma_start(out=raw[s, c][:], in_=x[512 * c : 512 * (c + 1), :].rearrange("(p j) w -> p j w", j=4))
+            factor = {"a": ba, "b": bb}
+
+            def load_gain(s, g):
+                nc.scalar.dma_start(out=gain[s][:], in_=g.rearrange("(c p j) -> p c j", p=128, j=4))
+
+            def load_rows4(s, c):
+                nc.sync.dma_start(out=rows4[s, c][:], in_=factor[s][512 * c : 512 * (c + 1), :].rearrange("(p j) w -> p j w", j=4))
+
+            def load_rows1(s, c):
+                nc.sync.dma_start(out=rows1[s, c][:], in_=factor[s][512 * c : 512 * (c + 1), :].rearrange("(b p) w -> p b w", p=128))
+
+            def load_tb(c):
+                nc.sync.dma_start(out=tbr[c][:], in_=tb[512 * c : 512 * (c + 1), :].rearrange("(p j) w -> p j w", j=4))
 
             def load_delta(b):
                 nc.sync.dma_start(out=dr[b][:], in_=delta[128 * b : 128 * (b + 1), :])
@@ -62,180 +71,132 @@ def tile_opposedspindirectringamplitudeupdate_x1_kernel(tc, ta, tb, ba, bb, ga, 
             def load_ta(q):
                 nc.sync.dma_start(out=tar[q][:], in_=ta[256 * q : 256 * (q + 1), :].rearrange("(b p) k -> p b k", p=128))
 
-            load_raw("b", bb, 0)
-            load_raw("b", bb, 1)
-            for c in range(2):
-                nc.sync.dma_start(out=tbr[c][:], in_=tb[512 * c : 512 * (c + 1), :].rearrange("(p j) w -> p j w", j=4))
-            load_delta(0)
-            load_raw("a", ba, 0)
-            load_ta(0)
-            load_raw("a", ba, 1)
-            load_delta(1)
-            load_ta(1)
-            load_delta(2)
-            load_ta(2)
-            load_delta(3)
-            load_ta(3)
-            for b in range(4, 8):
-                load_delta(b)
+            def copy_on(engine):
+                return nc.vector.tensor_copy if engine == "v" else nc.scalar.copy
 
-            gm = {}
-            gi = {}
+            def quantise(codes, scale, values):
+                nc.vector.quantize_mx(out=codes.bitcast(FP8X4), scales=scale, in_=values)
 
-            def factor_mult(s, c, engine="v"):
-                gm[s, c] = pool.tile([128, 4, P], BF16, name="gm", align_bytes=64)
+            scaled, grouped = {}, {}
+
+            def factor_mult(s, c):
+                scaled[s, c] = pool.tile([128, 4, P], BF16, name="scaled", align_bytes=64)
                 for j in range(4):
-                    if engine == "v":
-                        nc.vector.tensor_scalar(
-                            out=gm[s, c][:, j, :], in0=raw[s, c][:, j, :], scalar1=gf[s][:, c, j : j + 1], scalar2=None, op0=ALU.mult
-                        )
-                    else:
-                        nc.scalar.activation(
-                            out=gm[s, c][:, j, :], in_=raw[s, c][:, j, :], func=ACT.Copy, scale=gf[s][:, c, j : j + 1]
-                        )
+                    nc.vector.tensor_scalar(
+                        out=scaled[s, c][:, j, :], in0=rows4[s, c][:, j, :], scalar1=gain[s][:, c, j : j + 1], scalar2=None, op0=ALU.mult
+                    )
 
-            def interleave(engine, dst, src):
-                copy = nc.vector.tensor_copy if engine == "v" else nc.scalar.copy
-                copy(out=dst, in_=src.rearrange("p j w -> p w j"))
+            def interleave(engine, name, src):
+                grouped[name] = pool.tile([128, 512, 4], BF16, name="grouped", bufs=4, align_bytes=64)
+                copy_on(engine)(out=grouped[name][:], in_=src.rearrange("p j w -> p w j"))
 
-            def factor_copy(s, c):
-                gi[s, c] = pool.tile([128, 4, 128, 4], BF16, name="gi", align_bytes=64)
-                nc.vector.tensor_copy(out=gi[s, c][:], in_=gm[s, c][:].rearrange("p j (m t) -> p t m j", t=4))
-
-            def turn_b(s, c, h):
-                words = raw[s, c][:].rearrange("p j w -> p (j w)").bitcast(F32)
-                bank = psum.tile([128, 4, 128], F32, name="turn", bufs=3)
-                for jj in range(2):
-                    for u in range(2):
-                        j = 2 * h + jj
-                        nc.tensor.transpose(bank[:, 2 * jj + u, :], words[:, 256 * j + u : 256 * (j + 1) : 2], ident[:])
-                dst = btr[s][:].rearrange("p n f -> p (n f)").bitcast(F32)
-                dst = dst[:, 1024 * c : 1024 * (c + 1)].rearrange("p (q r) -> p q r", r=8)[:, :, 4 * h : 4 * h + 4]
-                nc.scalar.copy(out=dst, in_=bank[:].rearrange("p r q -> p q r"))
+            def factor_group(s, c, engine="v"):
+                interleave(engine, (s, c), scaled[s, c][:])
 
             def factor_quantise(s, c):
-                nc.vector.quantize_mx(
-                    out=gcodes[s, c][:].bitcast(FP8X4), scales=gscale[s, c][:], in_=gi[s, c][:].rearrange("p t m j -> p (t m j)")
-                )
+                quantise(gcodes[s, c][:], gscale[s, c][:], grouped[s, c][:].rearrange("p w j -> p (w j)"))
 
-            ti = {}
-
-            def tb_copy(c, h, engine):
-                ti[c, h] = pool.tile([128, 512, 4], BF16, name="ti", bufs=4, align_bytes=64)
-                interleave(engine, ti[c, h][:], tbr[c][:, :, 512 * h : 512 * (h + 1)])
+            def tb_group(c, h, engine):
+                interleave(engine, ("t", c, h), tbr[c][:, :, 512 * h : 512 * (h + 1)])
 
             def tb_quantise(c, h):
                 cols = slice(512 * h, 512 * (h + 1))
-                nc.vector.quantize_mx(
-                    out=tbcodes[c][:, cols].bitcast(FP8X4), scales=tbscale[c][:, cols], in_=ti[c, h][:].rearrange("p w j -> p (w j)")
-                )
+                quantise(tbcodes[c][:, cols], tbscale[c][:, cols], grouped["t", c, h][:].rearrange("p w j -> p (w j)"))
+
+            def turn_bank():
+                return psum.tile([128, 4, 128], F32, name="turn", bufs=3)
 
             def word_view(tile_ap):
                 return tile_ap.rearrange("p c n f -> p (c n f)").bitcast(F32).rearrange("p (c n u) -> p c n u", c=2, u=2)
 
-            tat, tac = {}, {}
+            tabank, tat = {}, {}
 
-            def turn_ta(b):
+            def ta_turn(b):
                 words = tar[b // 2][:, b % 2, :].bitcast(F32)
-                bank = psum.tile([128, 4, 128], F32, name="turn", bufs=3)
+                tabank[b] = turn_bank()
                 for c in range(2):
                     for u in range(2):
-                        nc.tensor.transpose(bank[:, 2 * c + u, :], words[:, 256 * c + u : 256 * (c + 1) : 2], ident[:])
+                        nc.tensor.transpose(tabank[b][:, 2 * c + u, :], words[:, 256 * c + u : 256 * (c + 1) : 2], ident[:])
+
+            def ta_words(b):
                 half = slice(128 * (b % 2), 128 * (b % 2) + 128)
                 if b % 2 == 0:
-                    tat[b // 2] = pool.tile([128, 2, 256, 4], BF16, name="tat", bufs=4, align_bytes=64)
-                nc.scalar.copy(out=word_view(tat[b // 2][:])[:, :, half, :], in_=bank[:].rearrange("p (c u) n -> p c n u", c=2))
+                    tat[b // 2] = pool.tile([128, 2, 256, 4], BF16, name="tat", bufs=2, align_bytes=64)
+                nc.scalar.copy(out=word_view(tat[b // 2][:])[:, :, half, :], in_=tabank[b][:].rearrange("p (c u) n -> p c n u", c=2))
 
             def ta_quantise(q):
-                codes = pool.tile([128, 2, 256], U32, name="tacodes", bufs=4, align_bytes=64)
-                scale = pool.tile([128, 2, 256], U8, name="tascale", bufs=4, align_bytes=64)
-                nc.vector.quantize_mx(
-                    out=codes[:].rearrange("p c n -> p (c n)").bitcast(FP8X4),
-                    scales=scale[:].rearrange("p c n -> p (c n)"),
-                    in_=tat[q][:].rearrange("p c n f -> p (c n f)"),
+                quantise(
+                    tacodes[q][:].rearrange("p c n -> p (c n)"),
+                    tascale[q][:].rearrange("p c n -> p (c n)"),
+                    tat[q][:].rearrange("p c n f -> p (c n f)"),
                 )
-                tac[q] = codes, scale
 
-            bank_of = {}
-            xt = {}
+            ybank, xrows, xbank, xt = {}, {}, {}, {}
 
             def dress_mm(s, b):
-                bank = psum.tile([128, 4, 128], F32, name="dress", tag="mm", bufs=4)
-                for t in range(4):
-                    cols = slice(128 * t, 128 * (t + 1))
-                    for c in range(2):
-                        if s == "b":
-                            own = slice(128 * b, 128 * (b + 1))
-                            codes, scale = tbcodes[c][:, own], tbscale[c][:, own]
-                        else:
-                            own = slice(128 * (b % 2), 128 * (b % 2) + 128)
-                            codes, scale = tac[b // 2][0][:, c, own], tac[b // 2][1][:, c, own]
-                        nc.tensor.matmul_mx(
-                            out=bank[:, t, :],
-                            lhsT=gcodes[s, c][:, cols].bitcast(FP8X4),
-                            lhsT_scale=gscale[s, c][:, cols],
-                            rhs=codes.bitcast(FP8X4),
-                            rhs_scale=scale,
-                            start=(c == 0),
-                            stop=(c == 1),
-                        )
-                bank_of[s, b] = bank
+                ybank[s, b] = psum.tile([128, P], F32, name="dress", tag="mm", bufs=5)
+                for c in range(2):
+                    if s == "b":
+                        own = slice(128 * b, 128 * (b + 1))
+                        codes, scale = tbcodes[c][:, own], tbscale[c][:, own]
+                    else:
+                        own = slice(128 * (b % 2), 128 * (b % 2) + 128)
+                        codes, scale = tacodes[b // 2][:, c, own], tascale[b // 2][:, c, own]
+                    nc.tensor.matmul_mx(
+                        out=ybank[s, b][:],
+                        lhsT=codes.bitcast(FP8X4),
+                        lhsT_scale=scale,
+                        rhs=gcodes[s, c][:].bitcast(FP8X4),
+                        rhs_scale=gscale[s, c][:],
+                        start=(c == 0),
+                        stop=(c == 1),
+                    )
 
             def dress_add(s, b):
-                if s == "b":
-                    if b % 4 == 0:
-                        xt[s, b // 4] = pool.tile([128, 512, 4], BF16, name="xtb", bufs=2, align_bytes=64)
-                    out = xt[s, b // 4][:, 128 * (b % 4) : 128 * (b % 4) + 128, :]
-                else:
-                    xt[s, b] = pool.tile([128, 128, 4], BF16, name="xta", bufs=3, align_bytes=64)
-                    out = xt[s, b][:]
+                xrows[s, b] = pool.tile([128, P], BF16, name="xrows", bufs=4, align_bytes=64)
                 nc.vector.tensor_tensor(
-                    out=out,
-                    in0=bank_of[s, b][:].rearrange("p t n -> p n t"),
-                    in1=btr[s][:, 128 * b : 128 * (b + 1), :],
+                    out=xrows[s, b][:].rearrange("p (u w e) -> p u w e", u=2, e=2),
+                    in0=ybank[s, b][:].rearrange("p (w u e) -> p u w e", u=2, e=2),
+                    in1=rows1[s, b // 4][:, b % 4, :].rearrange("p (w u e) -> p u w e", u=2, e=2),
                     op=ALU.add,
                 )
 
-            def xb_quantise(h):
-                cols = slice(512 * h, 512 * (h + 1))
-                nc.vector.quantize_mx(
-                    out=xbcodes[:, cols].bitcast(FP8X4), scales=xbscale[:, cols], in_=xt["b", h][:].rearrange("p n f -> p (n f)")
-                )
+            def x_turn(s, q):
+                xbank[s, q] = turn_bank()
+                for k in range(2):
+                    words = xrows[s, 2 * q + k][:].bitcast(F32)
+                    for u in range(2):
+                        nc.tensor.transpose(xbank[s, q][:, 2 * k + u, :], words[:, 128 * u : 128 * (u + 1)], ident[:])
 
-            xac = {}
+            def x_words(s, q):
+                xt[s, q] = pool.tile([128, 2, 128, 4], BF16, name="xt", bufs=3, align_bytes=64)
+                nc.scalar.copy(out=word_view(xt[s, q][:]), in_=xbank[s, q][:].rearrange("p (k u) n -> p k n u", u=2))
 
-            def xa_quantise(b):
-                codes = pool.tile([128, 128], U32, name="xacodes", bufs=3, align_bytes=64)
-                scale = pool.tile([128, 128], U8, name="xascale", bufs=3, align_bytes=64)
-                nc.vector.quantize_mx(out=codes[:].bitcast(FP8X4), scales=scale[:], in_=xt["a", b][:].rearrange("p n f -> p (n f)"))
-                xac[b] = codes, scale
-
-            recs = {}
+            def x_quantise(s, q):
+                cols = slice(256 * q, 256 * (q + 1))
+                quantise(xcodes[s][:, cols], xscale[s][:, cols], xt[s, q][:].rearrange("p k n f -> p (k n f)"))
 
             def root(b):
-                if b % 2 == 0:
-                    recs[b // 2] = pool.tile([128, 2, M], F32, name="recs", tag="big", bufs=4, align_bytes=64)
-                nc.scalar.activation(out=recs[b // 2][:, b % 2, :], in_=dr[b][:], func=ACT.Abs_reciprocal_sqrt)
+                nc.scalar.activation(out=rec[b][:], in_=dr[b][:], func=ACT.Abs_reciprocal_sqrt)
 
             def square(b):
-                rec = recs[b // 2][:, b % 2, :]
-                nc.scalar.activation(out=rec, in_=rec, func=ACT.Square)
+                nc.scalar.activation(out=rec[b][:], in_=rec[b][:], func=ACT.Square)
 
             prod = {}
 
             def product(b, h):
+                own = slice(128 * b, 128 * (b + 1))
                 cols = slice(512 * h, 512 * (h + 1))
-                bank = psum.tile([128, 512], F32, name="prod", tag="mm", bufs=4)
+                prod[b, h] = psum.tile([128, 512], F32, name="prod", tag="mm", bufs=5)
                 nc.tensor.matmul_mx(
-                    out=bank[:],
-                    lhsT=xac[b][0][:].bitcast(FP8X4),
-                    lhsT_scale=xac[b][1][:],
-                    rhs=xbcodes[:, cols].bitcast(FP8X4),
-                    rhs_scale=xbscale[:, cols],
+                    out=prod[b, h][:],
+                    lhsT=xcodes["a"][:, own].bitcast(FP8X4),
+                    lhsT_scale=xscale["a"][:, own],
+                    rhs=xcodes["b"][:, cols].bitcast(FP8X4),
+                    rhs_scale=xscale["b"][:, cols],
                     start=True,
                     stop=True,
                 )
-                prod[b, h] = bank
 
             r, rb = {}, {}
 
@@ -243,48 +204,46 @@ def tile_opposedspindirectringamplitudeupdate_x1_kernel(tc, ta, tb, ba, bb, ga, 
                 cols = slice(512 * h, 512 * (h + 1))
                 if h == 0:
                     r[b] = pool.tile([128, M], F32, name="r", bufs=3)
-                    rb[b] = pool.tile([128, M], BF16, name="rb", bufs=2)
                 nc.vector.scalar_tensor_tensor(
-                    out=r[b][:, cols], in0=prod[b, h][:], scalar=-1.0, in1=recs[b // 2][:, b % 2, cols], op0=ALU.mult, op1=ALU.mult
+                    out=r[b][:, cols], in0=prod[b, h][:], scalar=-1.0, in1=rec[b][:, cols], op0=ALU.mult, op1=ALU.mult
                 )
 
-            def narrow(b, g0, g1, engine="v"):
-                pairs = slice(128 * g0, 128 * g1)
-                copy = nc.vector.tensor_copy if engine == "v" else nc.scalar.copy
-                copy(
-                    out=rb[b][:].rearrange("p (u w e) -> p u w e", u=2, e=2)[:, :, pairs, :],
-                    in_=r[b][:].rearrange("p (w u e) -> p u w e", u=2, e=2)[:, :, pairs, :],
-                )
+            def narrow(b, g0, g1, engine):
+                if g0 == 0:
+                    rb[b] = pool.tile([128, 2, 512], BF16, name="rb", bufs=3)
+                for g in range(g0, g1):
+                    out = rb[b][:, g, :].rearrange("p (u w e) -> p u w e", u=2, e=2)
+                    src = r[b][:, 512 * g : 512 * (g + 1)].rearrange("p (w u e) -> p u w e", u=2, e=2)
+                    if engine == "g":
+                        nc.gpsimd.tensor_scalar(out=out, in0=src, scalar1=1.0, scalar2=0.0, op0=ALU.mult, op1=ALU.add)
+                    else:
+                        copy_on(engine)(out=out, in_=src)
 
             pb, pt = {}, {}
 
-            def turn_p(b, g):
-                words = rb[b][:].bitcast(F32)
-                if g == 0:
-                    pb[b] = psum.tile([128, 4, 128], F32, name="turn", bufs=3)
-                for u in range(2):
-                    first = 256 * u + 128 * g
-                    nc.tensor.transpose(pb[b][:, 2 * g + u, :], words[:, first : first + 128], ident[:])
+            def p_turn(b, g0=0, g1=2):
+                bank = turn_bank()
+                for g in range(g0, g1):
+                    pb[b, g] = bank
+                    words = rb[b][:, g, :].bitcast(F32)
+                    for u in range(2):
+                        nc.tensor.transpose(bank[:, 2 * g + u, :], words[:, 128 * u : 128 * (u + 1)], ident[:])
 
-            def p_words(b, g0, g1):
+            def p_words(b, g0=0, g1=2, engine="s"):
                 half = slice(128 * (b % 2), 128 * (b % 2) + 128)
                 if b % 2 == 0 and g0 == 0:
                     pt[b // 2] = pool.tile([128, 2, 256, 4], BF16, name="pt", bufs=2, align_bytes=64)
-                nc.scalar.copy(
+                copy_on(engine)(
                     out=word_view(pt[b // 2][:])[:, g0:g1, half, :],
-                    in_=pb[b][:, 2 * g0 : 2 * g1, :].rearrange("p (c u) n -> p c n u", u=2),
+                    in_=pb[b, g0][:, 2 * g0 : 2 * g1, :].rearrange("p (c u) n -> p c n u", u=2),
                 )
 
             def p_quantise(b0, b1, g):
                 cols = slice(128 * b0, 128 * b1)
                 own = slice(128 * (b0 % 2), 128 * (b0 % 2) + 128 * (b1 - b0))
-                nc.vector.quantize_mx(
-                    out=pcodes[:, g, cols].bitcast(FP8X4),
-                    scales=pscale[:, g, cols],
-                    in_=pt[b0 // 2][:, g, own, :].rearrange("p n f -> p (n f)"),
-                )
+                quantise(pcodes[:, g, cols], pscale[:, g, cols], pt[b0 // 2][:, g, own, :].rearrange("p n f -> p (n f)"))
 
-            def store_r(b, c0, c1):
+            def store_r(b, c0=0, c1=M):
                 nc.sync.dma_start(out=out_0[128 * b : 128 * (b + 1), c0:c1], in_=r[b][:, c0:c1])
 
             def store_codes(b0, b1):
@@ -301,124 +260,187 @@ def tile_opposedspindirectringamplitudeupdate_x1_kernel(tc, ta, tb, ba, bb, ga, 
                         in_=pscale[32 * quad : 32 * quad + 4, :, cols].bitcast(I32),
                     )
 
-            def p_pair(q):
-                p_quantise(2 * q, 2 * q + 2, 0)
-                p_quantise(2 * q, 2 * q + 2, 1)
-                store_codes(2 * q, 2 * q + 2)
-                if q == 2:
-                    store_scales(0, 6, (nc.sync, nc.sync))
+            load_gain("b", gb)
+            load_gain("a", ga)
+            load_rows4("b", 0)
+            load_rows4("b", 1)
+            load_delta(0)
+            load_tb(0)
+            load_tb(1)
+            load_delta(1)
+            load_rows4("a", 0)
+            load_delta(2)
+            load_rows1("b", 0)
+            load_rows4("a", 1)
+            load_ta(0)
+            load_delta(3)
+            load_ta(1)
+            load_rows1("b", 1)
+            load_rows1("a", 0)
+            load_delta(4)
+            load_ta(2)
+            load_delta(5)
+            load_ta(3)
+            load_rows1("a", 1)
+            load_delta(6)
+            load_delta(7)
 
-
-            nc.vector.memset(warm[:], 1.0)
-            nc.scalar.activation(out=warm[:], in_=warm[:], func=ACT.Abs_reciprocal_sqrt)
-            nc.vector.tensor_copy(out=gf["b"][:], in_=graw["b"][:])
-            turn_b("b", 0, 0)
-            turn_b("b", 0, 1)
-            turn_b("b", 1, 0)
-            turn_b("b", 1, 1)
             factor_mult("b", 0)
+            factor_group("b", 0)
             factor_mult("b", 1)
-            factor_copy("b", 0)
-            tb_copy(0, 1, "s")
-            tb_copy(1, 0, "s")
             factor_quantise("b", 0)
-            tb_copy(0, 0, "v")
-            tb_copy(1, 1, "s")
-            factor_copy("b", 1)
-            nc.vector.tensor_copy(out=gf["a"][:], in_=graw["a"][:])
-            turn_b("a", 0, 1)
-            tb_quantise(0, 0)
-            factor_quantise("b", 1)
-            factor_mult("a", 0)
-            turn_ta(0)
-            turn_ta(1)
-            tb_quantise(0, 1)
+            factor_group("b", 1)
             root(0)
+            square(0)
+            tb_group(0, 1, "s")
+            tb_group(0, 0, "v")
+            factor_quantise("b", 1)
+            tb_group(1, 0, "v")
+            tb_quantise(0, 0)
+            tb_group(1, 1, "s")
+            factor_mult("a", 0)
             tb_quantise(1, 0)
-            for b in range(4): dress_mm("b", b)
-            factor_copy("a", 0)
+            for b in range(4):
+                dress_mm("b", b)
+            root(1)
+            root(2)
+            square(1)
+            factor_group("a", 0)
+            tb_quantise(0, 1)
             factor_mult("a", 1)
             factor_quantise("a", 0)
-            turn_b("a", 0, 0)
-            root(1)
-            dress_add("b", 0)
-            dress_add("b", 1)
-            factor_copy("a", 1)
-            square(0)
-            tb_quantise(1, 1)
-            factor_quantise("a", 1)
-            ta_quantise(0)
-            turn_b("a", 1, 1)
-            turn_ta(2)
-            turn_ta(3)
-            root(2)
-            root(3)
-            dress_mm("b", 4)
-            dress_mm("b", 5)
-            dress_add("b", 2)
-            dress_add("b", 3)
+            factor_group("a", 1)
+            ta_turn(0)
+            ta_turn(1)
             square(2)
+            ta_words(0)
+            ta_words(1)
+            tb_quantise(1, 1)
+            ta_turn(2)
+            dress_mm("b", 4)
+            ta_turn(3)
+            factor_quantise("a", 1)
+            dress_add("b", 0)
+            ta_quantise(0)
+            root(3)
+            ta_words(2)
+            ta_words(3)
+            dress_add("b", 1)
             dress_mm("a", 0)
-            dress_add("b", 4)
-            dress_mm("b", 6)
-            dress_mm("b", 7)
-            xb_quantise(0)
-            turn_ta(4)
-            turn_b("a", 1, 0)
-            dress_add("a", 0)
-            dress_add("b", 5)
-            dress_add("b", 6)
-            turn_ta(5)
-            dress_add("b", 7)
             dress_mm("a", 1)
-            xa_quantise(0)
-            xb_quantise(1)
+            x_turn("b", 0)
+            square(3)
+            x_words("b", 0)
+            dress_add("b", 2)
+            dress_mm("b", 5)
+            dress_add("b", 3)
+            dress_mm("b", 6)
+            x_turn("b", 1)
+            ta_turn(4)
+            root(4)
+            x_words("b", 1)
+            ta_words(4)
             ta_quantise(1)
+            dress_add("b", 4)
+            dress_mm("b", 7)
+            dress_add("a", 0)
             dress_add("a", 1)
-            product(0, 0)
-            product(0, 1)
             dress_mm("a", 2)
-            square(1)
+            x_turn("a", 0)
+            ta_turn(5)
+            dress_mm("a", 3)
+            square(4)
+            x_words("a", 0)
+            ta_words(5)
+            x_quantise("b", 0)
+            dress_add("b", 5)
+            x_quantise("b", 1)
+            dress_add("b", 6)
+            dress_add("b", 7)
+            x_turn("b", 2)
+            x_turn("b", 3)
+            x_words("b", 2)
+            x_words("b", 3)
+            root(5)
+            x_quantise("a", 0)
+            product(0, 0)
+            ta_quantise(2)
+            dress_mm("a", 4)
+            dress_mm("a", 5)
+            dress_add("a", 2)
+            dress_add("a", 3)
+            x_turn("a", 1)
+            ta_turn(6)
+            x_quantise("b", 2)
+            x_quantise("b", 3)
+            product(0, 1)
+            x_words("a", 1)
+            ta_words(6)
+            square(5)
             last = BLOCKS - 1
             for i in range(BLOCKS):
-                if i < 4:
-                    root(i + 4)
+                by_vector = i < 3
                 divide(i, 0)
-                if i < 2:
-                    turn_ta(i + 6)
-                if i < last:
-                    xa_quantise(i + 1)
-                if i in (3, 5, 7):
-                    p_pair(i // 2 - 1)
-                if i >= 1:
-                    turn_p(i - 1, 0)
-                if i >= 1:
-                    turn_p(i - 1, 1)
+                if i in (2, 4):
+                    x_turn("a", i // 2 + 1)
+                if 1 <= i <= 3:
+                    p_turn(i - 1)
                 if i < last:
                     product(i + 1, 0)
-                divide(i, 1)
-                if i >= 1:
-                    p_words(i - 1, 0, 2)
-                if i < 6:
-                    dress_add("a", i + 2)
-                store_r(i, 0, M)
-                if i < last:
                     product(i + 1, 1)
-                if i < 5:
-                    dress_mm("a", i + 3)
-                narrow(i, 0, 2, "s" if i in NS else "v")
-                if i < 5:
-                    square(i + 3)
-                if i in (0, 2):
-                    ta_quantise(2 + i // 2)
+                if i == 0:
+                    ta_turn(7)
+                    ta_words(7)
+                if i > 3:
+                    p_turn(i - 1)
+                divide(i, 1)
+                store_r(i)
+                if i == last:
+                    break
+                if i < 4:
+                    dress_add("a", i + 4)
+                if i == 1:
+                    ta_quantise(3)
+                    dress_mm("a", 6)
+                    dress_mm("a", 7)
+                if i < 2:
+                    root(i + 6)
+                if i in (2, 4):
+                    x_words("a", i // 2 + 1)
+                if by_vector:
+                    if i >= 1:
+                        p_words(i - 1)
+                    narrow(i, 0, 2, "v")
+                    if i < 2:
+                        square(i + 6)
+                elif i == 3:
+                    p_words(i - 1)
+                    narrow(i, 0, 2, "s")
+                else:
+                    narrow(i, 0, 2, "s")
+                    p_words(i - 1)
+                if i in (0, 2, 4):
+                    x_quantise("a", (i + 2) // 2)
+                if i in (3, 6):
+                    q = i // 3 - 1
+                    p_quantise(2 * q, 2 * q + 2, 0)
+                    p_quantise(2 * q, 2 * q + 2, 1)
+                    store_codes(2 * q, 2 * q + 2)
+                if i == 6:
+                    store_scales(0, 4, (nc.sync, nc.sync))
+            narrow(last, 0, 1, "v")
+            p_words(6)
+            p_quantise(4, 6, 0)
+            narrow(last, 1, 2, "v")
+            p_quantise(4, 6, 1)
+            store_codes(4, 6)
+            p_turn(last, 0, 1)
+            p_turn(last, 1, 2)
             p_quantise(6, 7, 0)
             p_quantise(6, 7, 1)
-            store_codes(6, 7)
-            turn_p(last, 0)
-            turn_p(last, 1)
             p_words(last, 0, 1)
+            p_words(last, 1, 2, "v")
             p_quantise(7, 8, 0)
-            p_words(last, 1, 2)
             p_quantise(7, 8, 1)
-            store_codes(7, 8)
-            store_scales(6, 8, (nc.sync, nc.scalar))
+            store_codes(6, 8)
+            store_scales(4, 8, (nc.sync, nc.scalar))

@@ -33,9 +33,10 @@ def tile_opposedspindirectringamplitudeupdate_x1_kernel(tc, ta, tb, ba, bb, ga, 
             gain[s] = keep_tile([128, 2, 4], BF16, "gain" + s)
             for c in range(2):
                 rows4[s, c] = keep_tile([128, 4, P], BF16, "rows4%s%d" % (s, c))
-                rows1[s, c] = keep_tile([128, 4, P], BF16, "rows1%s%d" % (s, c))
                 gcodes[s, c] = keep_tile([128, P], U32, "gcodes%s%d" % (s, c))
                 gscale[s, c] = keep_tile([128, P], U8, "gscale%s%d" % (s, c))
+        rows1 = [keep_tile([128, 4, P], BF16, "rows1%d" % c) for c in range(2)]
+        bbt = keep_tile([128, M, 4], BF16, "bbt")
         tbr = [keep_tile([128, 4, M], BF16, "tbr%d" % c) for c in range(2)]
         tar = [keep_tile([128, 2, N], BF16, "tar%d" % q) for q in range(4)]
         dr = [keep_tile([128, M], BF16, "dr%d" % b) for b in range(BLOCKS)]
@@ -59,8 +60,8 @@ def tile_opposedspindirectringamplitudeupdate_x1_kernel(tc, ta, tb, ba, bb, ga, 
             def load_rows4(s, c):
                 nc.sync.dma_start(out=rows4[s, c][:], in_=factor[s][512 * c : 512 * (c + 1), :].rearrange("(p j) w -> p j w", j=4))
 
-            def load_rows1(s, c):
-                nc.sync.dma_start(out=rows1[s, c][:], in_=factor[s][512 * c : 512 * (c + 1), :].rearrange("(b p) w -> p b w", p=128))
+            def load_rows1(c):
+                nc.sync.dma_start(out=rows1[c][:], in_=ba[512 * c : 512 * (c + 1), :].rearrange("(b p) w -> p b w", p=128))
 
             def load_tb(c):
                 nc.sync.dma_start(out=tbr[c][:], in_=tb[512 * c : 512 * (c + 1), :].rearrange("(p j) w -> p j w", j=4))
@@ -91,7 +92,14 @@ def tile_opposedspindirectringamplitudeupdate_x1_kernel(tc, ta, tb, ba, bb, ga, 
                 copy_on(engine)(out=grouped[name][:], in_=src.rearrange("p j w -> p w j"))
 
             def factor_group(s, c, engine="v"):
-                interleave(engine, (s, c), scaled[s, c][:])
+                if s == "a":
+                    interleave(engine, (s, c), scaled[s, c][:])
+                else:
+                    grouped[s, c] = pool.tile([128, 512, 4], BF16, name="grouped", bufs=4, align_bytes=64)
+                    copy_on(engine)(
+                        out=grouped[s, c][:].rearrange("p (t m) j -> p t m j", t=4),
+                        in_=scaled[s, c][:].rearrange("p j (m t) -> p t m j", t=4),
+                    )
 
             def factor_quantise(s, c):
                 quantise(gcodes[s, c][:], gscale[s, c][:], grouped[s, c][:].rearrange("p w j -> p (w j)"))
@@ -133,48 +141,88 @@ def tile_opposedspindirectringamplitudeupdate_x1_kernel(tc, ta, tb, ba, bb, ga, 
 
             ybank, xrows, xbank, xt = {}, {}, {}, {}
 
-            def dress_mm(s, b):
-                ybank[s, b] = psum.tile([128, P], F32, name="dress", tag="mm", bufs=5)
+            bbank = {}
+
+            def bb_turn(c, h):
+                words = rows4["b", c][:].rearrange("p j w -> p (j w)").bitcast(F32)
+                bbank[c, h] = turn_bank()
+                for jj in range(2):
+                    for u in range(2):
+                        j = 2 * h + jj
+                        nc.tensor.transpose(bbank[c, h][:, 2 * jj + u, :], words[:, 256 * j + u : 256 * (j + 1) : 2], ident[:])
+
+            def bb_words(c, h):
+                dst = bbt[:].rearrange("p n f -> p (n f)").bitcast(F32)
+                dst = dst[:, 1024 * c : 1024 * (c + 1)].rearrange("p (q r) -> p q r", r=8)[:, :, 4 * h : 4 * h + 4]
+                nc.scalar.copy(out=dst, in_=bbank[c, h][:].rearrange("p r q -> p q r"))
+
+            def xb_mm(b):
+                ybank["b", b] = psum.tile([128, 4, 128], F32, name="dress", tag="mm", bufs=5)
+                own = slice(128 * b, 128 * (b + 1))
+                for t in range(4):
+                    cols = slice(128 * t, 128 * (t + 1))
+                    for c in range(2):
+                        nc.tensor.matmul_mx(
+                            out=ybank["b", b][:, t, :],
+                            lhsT=gcodes["b", c][:, cols].bitcast(FP8X4),
+                            lhsT_scale=gscale["b", c][:, cols],
+                            rhs=tbcodes[c][:, own].bitcast(FP8X4),
+                            rhs_scale=tbscale[c][:, own],
+                            start=(c == 0),
+                            stop=(c == 1),
+                        )
+
+            def xb_add(b):
+                if b % 4 == 0:
+                    xt["b", b // 4] = pool.tile([128, 512, 4], BF16, name="xbt", tag="scaled", bufs=2, align_bytes=64)
+                nc.vector.tensor_tensor(
+                    out=xt["b", b // 4][:, 128 * (b % 4) : 128 * (b % 4) + 128, :],
+                    in0=ybank["b", b][:].rearrange("p t n -> p n t"),
+                    in1=bbt[:, 128 * b : 128 * (b + 1), :],
+                    op=ALU.add,
+                )
+
+            def xb_quantise(h):
+                cols = slice(512 * h, 512 * (h + 1))
+                quantise(xcodes["b"][:, cols], xscale["b"][:, cols], xt["b", h][:].rearrange("p n f -> p (n f)"))
+
+            def xa_mm(b):
+                ybank["a", b] = psum.tile([128, P], F32, name="dress", tag="mm", bufs=5)
+                own = slice(128 * (b % 2), 128 * (b % 2) + 128)
                 for c in range(2):
-                    if s == "b":
-                        own = slice(128 * b, 128 * (b + 1))
-                        codes, scale = tbcodes[c][:, own], tbscale[c][:, own]
-                    else:
-                        own = slice(128 * (b % 2), 128 * (b % 2) + 128)
-                        codes, scale = tacodes[b // 2][:, c, own], tascale[b // 2][:, c, own]
                     nc.tensor.matmul_mx(
-                        out=ybank[s, b][:],
-                        lhsT=codes.bitcast(FP8X4),
-                        lhsT_scale=scale,
-                        rhs=gcodes[s, c][:].bitcast(FP8X4),
-                        rhs_scale=gscale[s, c][:],
+                        out=ybank["a", b][:],
+                        lhsT=tacodes[b // 2][:, c, own].bitcast(FP8X4),
+                        lhsT_scale=tascale[b // 2][:, c, own],
+                        rhs=gcodes["a", c][:].bitcast(FP8X4),
+                        rhs_scale=gscale["a", c][:],
                         start=(c == 0),
                         stop=(c == 1),
                     )
 
-            def dress_add(s, b):
-                xrows[s, b] = pool.tile([128, P], BF16, name="xrows", bufs=4, align_bytes=64)
+            def xa_add(b):
+                xrows[b] = pool.tile([128, P], BF16, name="xrows", bufs=4, align_bytes=64)
                 nc.vector.tensor_tensor(
-                    out=xrows[s, b][:].rearrange("p (u w e) -> p u w e", u=2, e=2),
-                    in0=ybank[s, b][:].rearrange("p (w u e) -> p u w e", u=2, e=2),
-                    in1=rows1[s, b // 4][:, b % 4, :].rearrange("p (w u e) -> p u w e", u=2, e=2),
+                    out=xrows[b][:].rearrange("p (u w e) -> p u w e", u=2, e=2),
+                    in0=ybank["a", b][:].rearrange("p (w u e) -> p u w e", u=2, e=2),
+                    in1=rows1[b // 4][:, b % 4, :].rearrange("p (w u e) -> p u w e", u=2, e=2),
                     op=ALU.add,
                 )
 
-            def x_turn(s, q):
-                xbank[s, q] = turn_bank()
+            def xa_turn(q):
+                xbank[q] = turn_bank()
                 for k in range(2):
-                    words = xrows[s, 2 * q + k][:].bitcast(F32)
+                    words = xrows[2 * q + k][:].bitcast(F32)
                     for u in range(2):
-                        nc.tensor.transpose(xbank[s, q][:, 2 * k + u, :], words[:, 128 * u : 128 * (u + 1)], ident[:])
+                        nc.tensor.transpose(xbank[q][:, 2 * k + u, :], words[:, 128 * u : 128 * (u + 1)], ident[:])
 
-            def x_words(s, q):
-                xt[s, q] = pool.tile([128, 2, 128, 4], BF16, name="xt", bufs=3, align_bytes=64)
-                nc.scalar.copy(out=word_view(xt[s, q][:]), in_=xbank[s, q][:].rearrange("p (k u) n -> p k n u", u=2))
+            def xa_words(q, engine="s"):
+                xt["a", q] = pool.tile([128, 2, 128, 4], BF16, name="xat", bufs=2, align_bytes=64)
+                copy_on(engine)(out=word_view(xt["a", q][:]), in_=xbank[q][:].rearrange("p (k u) n -> p k n u", u=2))
 
-            def x_quantise(s, q):
+            def xa_quantise(q):
                 cols = slice(256 * q, 256 * (q + 1))
-                quantise(xcodes[s][:, cols], xscale[s][:, cols], xt[s, q][:].rearrange("p k n f -> p (k n f)"))
+                quantise(xcodes["a"][:, cols], xscale["a"][:, cols], xt["a", q][:].rearrange("p k n f -> p (k n f)"))
 
             def root(b):
                 nc.scalar.activation(out=rec[b][:], in_=dr[b][:], func=ACT.Abs_reciprocal_sqrt)
@@ -210,14 +258,14 @@ def tile_opposedspindirectringamplitudeupdate_x1_kernel(tc, ta, tb, ba, bb, ga, 
 
             def narrow(b, g0, g1, engine):
                 if g0 == 0:
-                    rb[b] = pool.tile([128, 2, 512], BF16, name="rb", bufs=3)
-                for g in range(g0, g1):
-                    out = rb[b][:, g, :].rearrange("p (u w e) -> p u w e", u=2, e=2)
-                    src = r[b][:, 512 * g : 512 * (g + 1)].rearrange("p (w u e) -> p u w e", u=2, e=2)
-                    if engine == "g":
-                        nc.gpsimd.tensor_scalar(out=out, in0=src, scalar1=1.0, scalar2=0.0, op0=ALU.mult, op1=ALU.add)
-                    else:
-                        copy_on(engine)(out=out, in_=src)
+                    rb[b] = pool.tile([128, M], BF16, name="rb", bufs=3)
+                pairs = slice(128 * g0, 128 * g1)
+                out = rb[b][:].rearrange("p (u w e) -> p u w e", u=2, e=2)[:, :, pairs, :]
+                src = r[b][:].rearrange("p (w u e) -> p u w e", u=2, e=2)[:, :, pairs, :]
+                if engine == "g":
+                    nc.gpsimd.tensor_scalar(out=out, in0=src, scalar1=1.0, scalar2=-0.0, op0=ALU.mult, op1=ALU.add)
+                else:
+                    copy_on(engine)(out=out, in_=src)
 
             pb, pt = {}, {}
 
@@ -225,14 +273,15 @@ def tile_opposedspindirectringamplitudeupdate_x1_kernel(tc, ta, tb, ba, bb, ga, 
                 bank = turn_bank()
                 for g in range(g0, g1):
                     pb[b, g] = bank
-                    words = rb[b][:, g, :].bitcast(F32)
+                    words = rb[b][:].bitcast(F32)
                     for u in range(2):
-                        nc.tensor.transpose(bank[:, 2 * g + u, :], words[:, 128 * u : 128 * (u + 1)], ident[:])
+                        first = 256 * u + 128 * g
+                        nc.tensor.transpose(bank[:, 2 * g + u, :], words[:, first : first + 128], ident[:])
 
             def p_words(b, g0=0, g1=2, engine="s"):
                 half = slice(128 * (b % 2), 128 * (b % 2) + 128)
                 if b % 2 == 0 and g0 == 0:
-                    pt[b // 2] = pool.tile([128, 2, 256, 4], BF16, name="pt", bufs=2, align_bytes=64)
+                    pt[b // 2] = pool.tile([128, 2, 256, 4], BF16, name="pt", bufs=3, align_bytes=64)
                 copy_on(engine)(
                     out=word_view(pt[b // 2][:])[:, g0:g1, half, :],
                     in_=pb[b, g0][:, 2 * g0 : 2 * g1, :].rearrange("p (c u) n -> p c n u", u=2),
@@ -263,35 +312,38 @@ def tile_opposedspindirectringamplitudeupdate_x1_kernel(tc, ta, tb, ba, bb, ga, 
             load_gain("b", gb)
             load_gain("a", ga)
             load_rows4("b", 0)
-            load_rows4("b", 1)
             load_delta(0)
+            load_rows4("b", 1)
             load_tb(0)
             load_tb(1)
-            load_delta(1)
-            load_rows4("a", 0)
-            load_delta(2)
-            load_rows1("b", 0)
-            load_rows4("a", 1)
             load_ta(0)
-            load_delta(3)
+            load_rows4("a", 0)
             load_ta(1)
-            load_rows1("b", 1)
-            load_rows1("a", 0)
-            load_delta(4)
+            load_rows4("a", 1)
+            load_delta(1)
             load_ta(2)
-            load_delta(5)
+            load_delta(2)
+            load_rows1(0)
             load_ta(3)
-            load_rows1("a", 1)
+            load_delta(3)
+            load_delta(4)
+            load_rows1(1)
+            load_delta(5)
             load_delta(6)
             load_delta(7)
 
+            root(0)
+            for c in range(2):
+                for h in range(2):
+                    bb_turn(c, h)
+                    bb_words(c, h)
+                if c == 0:
+                    square(0)
             factor_mult("b", 0)
             factor_group("b", 0)
             factor_mult("b", 1)
             factor_quantise("b", 0)
             factor_group("b", 1)
-            root(0)
-            square(0)
             tb_group(0, 1, "s")
             tb_group(0, 0, "v")
             factor_quantise("b", 1)
@@ -300,147 +352,122 @@ def tile_opposedspindirectringamplitudeupdate_x1_kernel(tc, ta, tb, ba, bb, ga, 
             tb_group(1, 1, "s")
             factor_mult("a", 0)
             tb_quantise(1, 0)
+            ta_turn(0)
+            ta_turn(1)
+            ta_words(0)
+            ta_words(1)
             for b in range(4):
-                dress_mm("b", b)
-            root(1)
-            root(2)
-            square(1)
+                xb_mm(b)
             factor_group("a", 0)
             tb_quantise(0, 1)
             factor_mult("a", 1)
-            factor_quantise("a", 0)
-            factor_group("a", 1)
-            ta_turn(0)
-            ta_turn(1)
-            square(2)
-            ta_words(0)
-            ta_words(1)
             tb_quantise(1, 1)
+            root(1)
+            factor_group("a", 1, "s")
             ta_turn(2)
-            dress_mm("b", 4)
             ta_turn(3)
-            factor_quantise("a", 1)
-            dress_add("b", 0)
+            xb_mm(4)
+            xb_add(0)
+            factor_quantise("a", 0)
+            xb_add(1)
+            xb_mm(5)
+            xb_mm(6)
             ta_quantise(0)
-            root(3)
+            xb_add(2)
+            xb_add(3)
+            xb_mm(7)
             ta_words(2)
             ta_words(3)
-            dress_add("b", 1)
-            dress_mm("a", 0)
-            dress_mm("a", 1)
-            x_turn("b", 0)
-            square(3)
-            x_words("b", 0)
-            dress_add("b", 2)
-            dress_mm("b", 5)
-            dress_add("b", 3)
-            dress_mm("b", 6)
-            x_turn("b", 1)
+            square(1)
+            factor_quantise("a", 1)
+            xa_mm(0)
             ta_turn(4)
-            root(4)
-            x_words("b", 1)
-            ta_words(4)
-            ta_quantise(1)
-            dress_add("b", 4)
-            dress_mm("b", 7)
-            dress_add("a", 0)
-            dress_add("a", 1)
-            dress_mm("a", 2)
-            x_turn("a", 0)
             ta_turn(5)
-            dress_mm("a", 3)
-            square(4)
-            x_words("a", 0)
+            xb_add(4)
+            xb_quantise(0)
+            xb_add(5)
+            xa_mm(1)
+            ta_quantise(1)
+            xb_add(6)
+            xb_add(7)
+            xa_mm(2)
+            xa_mm(3)
+            root(2)
+            root(3)
+            ta_words(4)
             ta_words(5)
-            x_quantise("b", 0)
-            dress_add("b", 5)
-            x_quantise("b", 1)
-            dress_add("b", 6)
-            dress_add("b", 7)
-            x_turn("b", 2)
-            x_turn("b", 3)
-            x_words("b", 2)
-            x_words("b", 3)
-            root(5)
-            x_quantise("a", 0)
-            product(0, 0)
-            ta_quantise(2)
-            dress_mm("a", 4)
-            dress_mm("a", 5)
-            dress_add("a", 2)
-            dress_add("a", 3)
-            x_turn("a", 1)
+            xa_add(0)
+            xa_add(1)
+            xa_turn(0)
             ta_turn(6)
-            x_quantise("b", 2)
-            x_quantise("b", 3)
-            product(0, 1)
-            x_words("a", 1)
+            ta_turn(7)
+            ta_quantise(2)
+            xa_mm(4)
+            xa_mm(5)
+            square(2)
+            xa_words(0)
             ta_words(6)
-            square(5)
+            ta_words(7)
+            xb_quantise(1)
+            xa_add(2)
+            xa_add(3)
+            xa_turn(1)
+            square(3)
+            xa_words(1)
+            root(4)
+            xa_quantise(0)
+            product(0, 0)
+            product(0, 1)
+            xa_add(4)
+            ta_quantise(3)
+            xa_add(5)
+            xa_turn(2)
+            root(5)
+            xa_words(2)
+            square(4)
             last = BLOCKS - 1
+            rest = [(root, 6), (square, 5), (root, 7), (square, 6), (square, 7)]
             for i in range(BLOCKS):
-                by_vector = i < 3
-                divide(i, 0)
-                if i in (2, 4):
-                    x_turn("a", i // 2 + 1)
-                if 1 <= i <= 3:
-                    p_turn(i - 1)
+                if i >= 2:
+                    p_turn(i - 2)
+                if i == 3:
+                    xa_turn(3)
                 if i < last:
                     product(i + 1, 0)
                     product(i + 1, 1)
-                if i == 0:
-                    ta_turn(7)
-                    ta_words(7)
-                if i > 3:
-                    p_turn(i - 1)
+                if i < 2:
+                    xa_mm(i + 6)
+                divide(i, 0)
                 divide(i, 1)
                 store_r(i)
-                if i == last:
-                    break
-                if i < 4:
-                    dress_add("a", i + 4)
-                if i == 1:
-                    ta_quantise(3)
-                    dress_mm("a", 6)
-                    dress_mm("a", 7)
-                if i < 2:
-                    root(i + 6)
-                if i in (2, 4):
-                    x_words("a", i // 2 + 1)
-                if by_vector:
-                    if i >= 1:
-                        p_words(i - 1)
-                    narrow(i, 0, 2, "v")
-                    if i < 2:
-                        square(i + 6)
-                elif i == 3:
-                    p_words(i - 1)
-                    narrow(i, 0, 2, "s")
-                else:
-                    narrow(i, 0, 2, "s")
-                    p_words(i - 1)
+                if i >= 2:
+                    p_words(i - 2)
+                if i == 3:
+                    xa_words(3, "v")
+                for step, b in rest[i : i + 1]:
+                    step(b)
                 if i in (0, 2, 4):
-                    x_quantise("a", (i + 2) // 2)
-                if i in (3, 6):
-                    q = i // 3 - 1
-                    p_quantise(2 * q, 2 * q + 2, 0)
-                    p_quantise(2 * q, 2 * q + 2, 1)
-                    store_codes(2 * q, 2 * q + 2)
-                if i == 6:
-                    store_scales(0, 4, (nc.sync, nc.sync))
+                    xa_quantise(i // 2 + 1)
+                if i == 5:
+                    p_quantise(0, 2, 0)
+                    p_quantise(0, 2, 1)
+                    store_codes(0, 2)
+                if i < last:
+                    narrow(i, 0, 2, "g")
+                if i in (1, 2):
+                    xa_add(i + 5)
             narrow(last, 0, 1, "v")
-            p_words(6)
-            p_quantise(4, 6, 0)
             narrow(last, 1, 2, "v")
-            p_quantise(4, 6, 1)
-            store_codes(4, 6)
-            p_turn(last, 0, 1)
-            p_turn(last, 1, 2)
-            p_quantise(6, 7, 0)
-            p_quantise(6, 7, 1)
-            p_words(last, 0, 1)
-            p_words(last, 1, 2, "v")
-            p_quantise(7, 8, 0)
-            p_quantise(7, 8, 1)
+            for q in (1, 2):
+                p_quantise(2 * q, 2 * q + 2, 0)
+                p_quantise(2 * q, 2 * q + 2, 1)
+            store_codes(2, 6)
+            p_turn(6)
+            p_words(6)
+            for g in range(2):
+                p_turn(last, g, g + 1)
+                p_words(last, g, g + 1)
+            p_quantise(6, 8, 0)
+            p_quantise(6, 8, 1)
             store_codes(6, 8)
-            store_scales(4, 8, (nc.sync, nc.scalar))
+            store_scales(0, 8, (nc.scalar, nc.sync))

@@ -37,10 +37,10 @@ def tile_opposedspindirectringamplitudeupdate_x1_kernel(tc, ta, tb, ba, bb, ga, 
                 gscale[s, c] = keep_tile([128, P], U8, "gscale%s%d" % (s, c))
         rows1 = [keep_tile([128, 4, P], BF16, "rows1%d" % c) for c in range(2)]
         bbt = keep_tile([128, M, 4], BF16, "bbt")
-        tbr = [keep_tile([128, 4, M], BF16, "tbr%d" % c) for c in range(2)]
+        tbr = [pool.tile([128, 4, M], BF16, name="tbr%d" % c, tag="big", align_bytes=64) for c in range(2)]
         tar = [keep_tile([128, 2, N], BF16, "tar%d" % q) for q in range(4)]
         dr = [keep_tile([128, M], BF16, "dr%d" % b) for b in range(BLOCKS)]
-        rec = [keep_tile([128, M], F32, "rec%d" % b) for b in range(BLOCKS)]
+        rec = {b: keep_tile([128, M], F32, "rec%d" % b) for b in (0, 3, 4, 5)}
         tbcodes = [keep_tile([128, M], U32, "tbcodes%d" % c) for c in range(2)]
         tbscale = [keep_tile([128, M], U8, "tbscale%d" % c) for c in range(2)]
         tacodes = [keep_tile([128, 2, 256], U32, "tacodes%d" % q) for q in range(4)]
@@ -87,25 +87,30 @@ def tile_opposedspindirectringamplitudeupdate_x1_kernel(tc, ta, tb, ba, bb, ga, 
                         out=scaled[s, c][:, j, :], in0=rows4[s, c][:, j, :], scalar1=gain[s][:, c, j : j + 1], scalar2=None, op0=ALU.mult
                     )
 
-            def interleave(engine, name, src):
-                grouped[name] = pool.tile([128, 512, 4], BF16, name="grouped", bufs=4, align_bytes=64)
-                copy_on(engine)(out=grouped[name][:], in_=src.rearrange("p j w -> p w j"))
-
-            def factor_group(s, c, engine="v"):
-                if s == "a":
-                    interleave(engine, (s, c), scaled[s, c][:])
+            def interleave(engine, name, src, tag="grouped", c0=0, c1=512):
+                if c0 == 0:
+                    grouped[name] = pool.tile([128, 512, 4], BF16, name="grouped", tag=tag, bufs=3 if tag == "grouped" else 1, align_bytes=64)
+                out, src = grouped[name][:, c0:c1, :], src[:, :, c0:c1].rearrange("p j w -> p w j")
+                if engine == "g":
+                    nc.gpsimd.tensor_scalar(out=out, in0=src, scalar1=1.0, scalar2=-0.0, op0=ALU.mult, op1=ALU.add)
                 else:
-                    grouped[s, c] = pool.tile([128, 512, 4], BF16, name="grouped", bufs=4, align_bytes=64)
+                    copy_on(engine)(out=out, in_=src)
+
+            def factor_group(s, c, engine="v", tag="grouped", c0=0, c1=512):
+                if s == "a":
+                    interleave(engine, (s, c), scaled[s, c][:], tag, c0, c1)
+                else:
+                    grouped[s, c] = pool.tile([128, 512, 4], BF16, name="grouped", bufs=3, align_bytes=64)
                     copy_on(engine)(
-                        out=grouped[s, c][:].rearrange("p (t m) j -> p t m j", t=4),
-                        in_=scaled[s, c][:].rearrange("p j (m t) -> p t m j", t=4),
+                        out=grouped[s, c][:].rearrange("p (t m e) j -> p m t e j", t=4, e=2),
+                        in_=scaled[s, c][:].rearrange("p j (m e t) -> p m t e j", t=4, e=2),
                     )
 
             def factor_quantise(s, c):
                 quantise(gcodes[s, c][:], gscale[s, c][:], grouped[s, c][:].rearrange("p w j -> p (w j)"))
 
-            def tb_group(c, h, engine):
-                interleave(engine, ("t", c, h), tbr[c][:, :, 512 * h : 512 * (h + 1)])
+            def tb_group(c, h, engine, tag="grouped"):
+                interleave(engine, ("t", c, h), tbr[c][:, :, 512 * h : 512 * (h + 1)], tag)
 
             def tb_quantise(c, h):
                 cols = slice(512 * h, 512 * (h + 1))
@@ -156,25 +161,29 @@ def tile_opposedspindirectringamplitudeupdate_x1_kernel(tc, ta, tb, ba, bb, ga, 
                 dst = dst[:, 1024 * c : 1024 * (c + 1)].rearrange("p (q r) -> p q r", r=8)[:, :, 4 * h : 4 * h + 4]
                 nc.scalar.copy(out=dst, in_=bbank[c, h][:].rearrange("p r q -> p q r"))
 
-            def xb_mm(b):
-                ybank["b", b] = psum.tile([128, 4, 128], F32, name="dress", tag="mm", bufs=5)
+            def xb_mm(b, c):
+                if c == 0:
+                    ybank["b", b] = psum.tile([128, 4, 128], F32, name="dress", tag="mm", bufs=5)
                 own = slice(128 * b, 128 * (b + 1))
                 for t in range(4):
                     cols = slice(128 * t, 128 * (t + 1))
-                    for c in range(2):
-                        nc.tensor.matmul_mx(
-                            out=ybank["b", b][:, t, :],
-                            lhsT=gcodes["b", c][:, cols].bitcast(FP8X4),
-                            lhsT_scale=gscale["b", c][:, cols],
-                            rhs=tbcodes[c][:, own].bitcast(FP8X4),
-                            rhs_scale=tbscale[c][:, own],
-                            start=(c == 0),
-                            stop=(c == 1),
-                        )
+                    nc.tensor.matmul_mx(
+                        out=ybank["b", b][:, t, :],
+                        lhsT=gcodes["b", c][:, cols].bitcast(FP8X4),
+                        lhsT_scale=gscale["b", c][:, cols],
+                        rhs=tbcodes[c][:, own].bitcast(FP8X4),
+                        rhs_scale=tbscale[c][:, own],
+                        start=(c == 0 and t == 0),
+                        stop=(c == 1 and t == 3),
+                    )
+
+            def xb_both(b):
+                xb_mm(b, 0)
+                xb_mm(b, 1)
 
             def xb_add(b):
                 if b % 4 == 0:
-                    xt["b", b // 4] = pool.tile([128, 512, 4], BF16, name="xbt", tag="scaled", bufs=2, align_bytes=64)
+                    xt["b", b // 4] = pool.tile([128, 512, 4], BF16, name="xbt", tag="xbt%d" % (b // 4), bufs=1, align_bytes=64)
                 nc.vector.tensor_tensor(
                     out=xt["b", b // 4][:, 128 * (b % 4) : 128 * (b % 4) + 128, :],
                     in0=ybank["b", b][:].rearrange("p t n -> p n t"),
@@ -186,19 +195,23 @@ def tile_opposedspindirectringamplitudeupdate_x1_kernel(tc, ta, tb, ba, bb, ga, 
                 cols = slice(512 * h, 512 * (h + 1))
                 quantise(xcodes["b"][:, cols], xscale["b"][:, cols], xt["b", h][:].rearrange("p n f -> p (n f)"))
 
-            def xa_mm(b):
-                ybank["a", b] = psum.tile([128, P], F32, name="dress", tag="mm", bufs=5)
+            def xa_pass(b, c):
+                if c == 0:
+                    ybank["a", b] = psum.tile([128, P], F32, name="dress", tag="mm", bufs=5)
                 own = slice(128 * (b % 2), 128 * (b % 2) + 128)
-                for c in range(2):
-                    nc.tensor.matmul_mx(
-                        out=ybank["a", b][:],
-                        lhsT=tacodes[b // 2][:, c, own].bitcast(FP8X4),
-                        lhsT_scale=tascale[b // 2][:, c, own],
-                        rhs=gcodes["a", c][:].bitcast(FP8X4),
-                        rhs_scale=gscale["a", c][:],
-                        start=(c == 0),
-                        stop=(c == 1),
-                    )
+                nc.tensor.matmul_mx(
+                    out=ybank["a", b][:],
+                    lhsT=tacodes[b // 2][:, c, own].bitcast(FP8X4),
+                    lhsT_scale=tascale[b // 2][:, c, own],
+                    rhs=gcodes["a", c][:].bitcast(FP8X4),
+                    rhs_scale=gscale["a", c][:],
+                    start=(c == 0),
+                    stop=(c == 1),
+                )
+
+            def xa_mm(b):
+                xa_pass(b, 0)
+                xa_pass(b, 1)
 
             def xa_add(b):
                 xrows[b] = pool.tile([128, P], BF16, name="xrows", bufs=4, align_bytes=64)
@@ -216,19 +229,28 @@ def tile_opposedspindirectringamplitudeupdate_x1_kernel(tc, ta, tb, ba, bb, ga, 
                     for u in range(2):
                         nc.tensor.transpose(xbank[q][:, 2 * k + u, :], words[:, 128 * u : 128 * (u + 1)], ident[:])
 
-            def xa_words(q, engine="s"):
-                xt["a", q] = pool.tile([128, 2, 128, 4], BF16, name="xat", bufs=2, align_bytes=64)
+            def xa_words(q, engine="s", tag="xat"):
+                xt["a", q] = pool.tile([128, 2, 128, 4], BF16, name="xat", tag=tag, bufs=2 if tag == "xat" else 1, align_bytes=64)
                 copy_on(engine)(out=word_view(xt["a", q][:]), in_=xbank[q][:].rearrange("p (k u) n -> p k n u", u=2))
 
             def xa_quantise(q):
                 cols = slice(256 * q, 256 * (q + 1))
                 quantise(xcodes["a"][:, cols], xscale["a"][:, cols], xt["a", q][:].rearrange("p k n f -> p (k n f)"))
 
+            roots = {}
+
             def root(b):
-                nc.scalar.activation(out=rec[b][:], in_=dr[b][:], func=ACT.Abs_reciprocal_sqrt)
+                if b not in rec:
+                    rec[b] = pool.tile([128, M], F32, name="rec%d" % b, tag="big", align_bytes=64)
+                roots[b] = rec[b]
+                nc.scalar.activation(out=roots[b][:], in_=dr[b][:], func=ACT.Abs_reciprocal_sqrt)
 
             def square(b):
-                nc.scalar.activation(out=rec[b][:], in_=rec[b][:], func=ACT.Square)
+                nc.scalar.activation(out=rec[b][:], in_=roots[b][:], func=ACT.Square)
+
+            def square_beside(b, tag):
+                rec[b] = pool.tile([128, M], F32, name="rec%d" % b, tag=tag, bufs=1, align_bytes=64)
+                nc.gpsimd.tensor_tensor(out=rec[b][:], in0=roots[b][:], in1=roots[b][:], op=ALU.mult)
 
             prod = {}
 
@@ -315,12 +337,12 @@ def tile_opposedspindirectringamplitudeupdate_x1_kernel(tc, ta, tb, ba, bb, ga, 
             load_delta(0)
             load_rows4("b", 1)
             load_tb(0)
-            load_tb(1)
             load_ta(0)
+            load_tb(1)
             load_rows4("a", 0)
-            load_ta(1)
-            load_rows4("a", 1)
             load_delta(1)
+            load_rows4("a", 1)
+            load_ta(1)
             load_ta(2)
             load_delta(2)
             load_rows1(0)
@@ -339,6 +361,8 @@ def tile_opposedspindirectringamplitudeupdate_x1_kernel(tc, ta, tb, ba, bb, ga, 
                     bb_words(c, h)
                 if c == 0:
                     square(0)
+            ta_turn(0)
+            ta_turn(1)
             factor_mult("b", 0)
             factor_group("b", 0)
             factor_mult("b", 1)
@@ -347,84 +371,80 @@ def tile_opposedspindirectringamplitudeupdate_x1_kernel(tc, ta, tb, ba, bb, ga, 
             tb_group(0, 1, "s")
             tb_group(0, 0, "v")
             factor_quantise("b", 1)
-            tb_group(1, 0, "v")
             tb_quantise(0, 0)
-            tb_group(1, 1, "s")
+            for b in range(4):
+                xb_mm(b, 0)
+            tb_group(1, 0, "v")
+            tb_group(1, 1, "s", "gate1")
             factor_mult("a", 0)
             tb_quantise(1, 0)
-            ta_turn(0)
-            ta_turn(1)
+            for b in range(4):
+                xb_mm(b, 1)
             ta_words(0)
             ta_words(1)
-            for b in range(4):
-                xb_mm(b)
-            factor_group("a", 0)
             tb_quantise(0, 1)
             factor_mult("a", 1)
             tb_quantise(1, 1)
-            root(1)
-            factor_group("a", 1, "s")
+            factor_group("a", 0, "g", "gate1")
+            factor_group("a", 1, "s", "gate2")
             ta_turn(2)
             ta_turn(3)
-            xb_mm(4)
-            xb_add(0)
-            factor_quantise("a", 0)
-            xb_add(1)
-            xb_mm(5)
-            xb_mm(6)
-            ta_quantise(0)
-            xb_add(2)
-            xb_add(3)
-            xb_mm(7)
+            xb_both(4)
+            for b in range(5):
+                xb_add(b)
+            xb_both(5)
+            xb_both(6)
             ta_words(2)
             ta_words(3)
-            square(1)
-            factor_quantise("a", 1)
-            xa_mm(0)
             ta_turn(4)
+            xb_both(7)
             ta_turn(5)
-            xb_add(4)
-            xb_quantise(0)
-            xb_add(5)
-            xa_mm(1)
-            ta_quantise(1)
-            xb_add(6)
-            xb_add(7)
-            xa_mm(2)
-            xa_mm(3)
-            root(2)
-            root(3)
+            root(1)
             ta_words(4)
             ta_words(5)
+            root(2)
+            ta_quantise(0)
+            factor_quantise("a", 0)
+            xb_quantise(0)
+            ta_quantise(1)
+            factor_quantise("a", 1)
+            square_beside(1, "gate2")
+            xa_mm(0)
+            xa_mm(1)
+            ta_turn(6)
+            xa_mm(2)
+            for b in range(5, 8):
+                xb_add(b)
+            xa_mm(3)
+            ta_turn(7)
+            root(3)
+            ta_words(6)
+            square(3)
+            ta_words(7)
             xa_add(0)
             xa_add(1)
             xa_turn(0)
-            ta_turn(6)
-            ta_turn(7)
             ta_quantise(2)
             xa_mm(4)
             xa_mm(5)
-            square(2)
-            xa_words(0)
-            ta_words(6)
-            ta_words(7)
+            xa_words(0, "s", "gate3")
+            root(4)
             xb_quantise(1)
             xa_add(2)
             xa_add(3)
             xa_turn(1)
-            square(3)
+            ta_quantise(3)
             xa_words(1)
-            root(4)
+            square(4)
             xa_quantise(0)
+            square_beside(2, "gate3")
             product(0, 0)
             product(0, 1)
             xa_add(4)
-            ta_quantise(3)
             xa_add(5)
             xa_turn(2)
             root(5)
             xa_words(2)
-            square(4)
             last = BLOCKS - 1
             rest = [(root, 6), (square, 5), (root, 7), (square, 6), (square, 7)]
             for i in range(BLOCKS):
@@ -443,7 +463,7 @@ def tile_opposedspindirectringamplitudeupdate_x1_kernel(tc, ta, tb, ba, bb, ga, 
                 if i >= 2:
                     p_words(i - 2)
                 if i == 3:
-                    xa_words(3, "v")
+                    xa_words(3)
                 for step, b in rest[i : i + 1]:
                     step(b)
                 if i in (0, 2, 4):
@@ -453,7 +473,7 @@ def tile_opposedspindirectringamplitudeupdate_x1_kernel(tc, ta, tb, ba, bb, ga, 
                     p_quantise(0, 2, 1)
                     store_codes(0, 2)
                 if i < last:
-                    narrow(i, 0, 2, "g")
+                    narrow(i, 0, 2, "g" if i < 6 else "s")
                 if i in (1, 2):
                     xa_add(i + 5)
             narrow(last, 0, 1, "v")
@@ -461,7 +481,7 @@ def tile_opposedspindirectringamplitudeupdate_x1_kernel(tc, ta, tb, ba, bb, ga, 
             for q in (1, 2):
                 p_quantise(2 * q, 2 * q + 2, 0)
                 p_quantise(2 * q, 2 * q + 2, 1)
-            store_codes(2, 6)
+                store_codes(2 * q, 2 * q + 2)
             p_turn(6)
             p_words(6)
             for g in range(2):

@@ -32,13 +32,12 @@ def tile_opposedspindirectringamplitudeupdate_x1_kernel(tc, ta, tb, ba, bb, ga, 
         for s in ("b", "a"):
             gain[s] = keep_tile([128, 2, 4], BF16, "gain" + s)
             for c in range(2):
-                rows4[s, c] = keep_tile([128, 4, P], BF16, "rows4%s%d" % (s, c))
                 gcodes[s, c] = keep_tile([128, P], U32, "gcodes%s%d" % (s, c))
                 gscale[s, c] = keep_tile([128, P], U8, "gscale%s%d" % (s, c))
         rows1 = [keep_tile([128, 4, P], BF16, "rows1%d" % c) for c in range(2)]
         bbt = keep_tile([128, M, 4], BF16, "bbt")
         tbr = [pool.tile([128, 4, M], BF16, name="tbr%d" % c, tag="big", align_bytes=64) for c in range(2)]
-        tar = [keep_tile([128, 2, N], BF16, "tar%d" % q) for q in range(4)]
+        tar = {}
         dr = [keep_tile([128, M], BF16, "dr%d" % b) for b in range(BLOCKS)]
         rec = {b: keep_tile([128, M], F32, "rec%d" % b) for b in (0, 3, 4, 5)}
         tbcodes = [keep_tile([128, M], U32, "tbcodes%d" % c) for c in range(2)]
@@ -54,11 +53,17 @@ def tile_opposedspindirectringamplitudeupdate_x1_kernel(tc, ta, tb, ba, bb, ga, 
         with tc.manual_schedule():
             factor = {"a": ba, "b": bb}
 
-            def load_gain(s, g):
-                nc.scalar.dma_start(out=gain[s][:], in_=g.rearrange("(c p j) -> p c j", p=128, j=4))
+            def load_gain(s, g, queue):
+                queue.dma_start(out=gain[s][:], in_=g.rearrange("(c p j) -> p c j", p=128, j=4))
 
-            def load_rows4(s, c):
-                nc.sync.dma_start(out=rows4[s, c][:], in_=factor[s][512 * c : 512 * (c + 1), :].rearrange("(p j) w -> p j w", j=4))
+            def load_rows4(s, c, pieces=1):
+                src = factor[s][512 * c : 512 * (c + 1), :].rearrange("(p j) w -> p j w", j=4)
+                step = 4 // pieces
+                for j0 in range(0, 4, step):
+                    piece = keep_tile([128, step, P], BF16, "rows4%s%d%d" % (s, c, j0))
+                    nc.sync.dma_start(out=piece[:], in_=src[:, j0 : j0 + step, :])
+                    for j in range(step):
+                        rows4[s, c, j0 + j] = piece[:, j, :]
 
             def load_rows1(c):
                 nc.sync.dma_start(out=rows1[c][:], in_=ba[512 * c : 512 * (c + 1), :].rearrange("(b p) w -> p b w", p=128))
@@ -69,8 +74,11 @@ def tile_opposedspindirectringamplitudeupdate_x1_kernel(tc, ta, tb, ba, bb, ga, 
             def load_delta(b):
                 nc.sync.dma_start(out=dr[b][:], in_=delta[128 * b : 128 * (b + 1), :])
 
-            def load_ta(q):
-                nc.sync.dma_start(out=tar[q][:], in_=ta[256 * q : 256 * (q + 1), :].rearrange("(b p) k -> p b k", p=128))
+            def load_ta(b0, b1):
+                rows = keep_tile([128, b1 - b0, N], BF16, "tar%d" % b0)
+                nc.sync.dma_start(out=rows[:], in_=ta[128 * b0 : 128 * b1, :].rearrange("(b p) k -> p b k", p=128))
+                for b in range(b0, b1):
+                    tar[b] = rows[:, b - b0, :]
 
             def copy_on(engine):
                 return nc.vector.tensor_copy if engine == "v" else nc.scalar.copy
@@ -84,7 +92,7 @@ def tile_opposedspindirectringamplitudeupdate_x1_kernel(tc, ta, tb, ba, bb, ga, 
                 scaled[s, c] = pool.tile([128, 4, P], BF16, name="scaled", align_bytes=64)
                 for j in range(4):
                     nc.vector.tensor_scalar(
-                        out=scaled[s, c][:, j, :], in0=rows4[s, c][:, j, :], scalar1=gain[s][:, c, j : j + 1], scalar2=None, op0=ALU.mult
+                        out=scaled[s, c][:, j, :], in0=rows4[s, c, j], scalar1=gain[s][:, c, j : j + 1], scalar2=None, op0=ALU.mult
                     )
 
             def interleave(engine, name, src, tag="grouped", c0=0, c1=512):
@@ -125,7 +133,7 @@ def tile_opposedspindirectringamplitudeupdate_x1_kernel(tc, ta, tb, ba, bb, ga, 
             tabank, tat = {}, {}
 
             def ta_turn(b):
-                words = tar[b // 2][:, b % 2, :].bitcast(F32)
+                words = tar[b].bitcast(F32)
                 tabank[b] = turn_bank()
                 for c in range(2):
                     for u in range(2):
@@ -149,12 +157,11 @@ def tile_opposedspindirectringamplitudeupdate_x1_kernel(tc, ta, tb, ba, bb, ga, 
             bbank = {}
 
             def bb_turn(c, h):
-                words = rows4["b", c][:].rearrange("p j w -> p (j w)").bitcast(F32)
                 bbank[c, h] = turn_bank()
                 for jj in range(2):
+                    words = rows4["b", c, 2 * h + jj].bitcast(F32)
                     for u in range(2):
-                        j = 2 * h + jj
-                        nc.tensor.transpose(bbank[c, h][:, 2 * jj + u, :], words[:, 256 * j + u : 256 * (j + 1) : 2], ident[:])
+                        nc.tensor.transpose(bbank[c, h][:, 2 * jj + u, :], words[:, u::2], ident[:])
 
             def bb_words(c, h):
                 dst = bbt[:].rearrange("p n f -> p (n f)").bitcast(F32)
@@ -331,22 +338,23 @@ def tile_opposedspindirectringamplitudeupdate_x1_kernel(tc, ta, tb, ba, bb, ga, 
                         in_=pscale[32 * quad : 32 * quad + 4, :, cols].bitcast(I32),
                     )
 
-            load_gain("b", gb)
-            load_gain("a", ga)
-            load_rows4("b", 0)
+            load_gain("b", gb, nc.scalar)
+            load_rows4("b", 0, 2)
             load_delta(0)
             load_rows4("b", 1)
             load_tb(0)
-            load_ta(0)
+            load_ta(0, 1)
             load_tb(1)
+            load_gain("a", ga, nc.sync)
             load_rows4("a", 0)
-            load_delta(1)
             load_rows4("a", 1)
-            load_ta(1)
-            load_ta(2)
+            load_delta(1)
+            load_ta(1, 2)
+            load_ta(2, 4)
+            load_ta(4, 6)
             load_delta(2)
             load_rows1(0)
-            load_ta(3)
+            load_ta(6, 8)
             load_delta(3)
             load_delta(4)
             load_rows1(1)
@@ -362,7 +370,6 @@ def tile_opposedspindirectringamplitudeupdate_x1_kernel(tc, ta, tb, ba, bb, ga, 
                 if c == 0:
                     square(0)
             ta_turn(0)
-            ta_turn(1)
             factor_mult("b", 0)
             factor_group("b", 0)
             factor_mult("b", 1)
@@ -381,65 +388,64 @@ def tile_opposedspindirectringamplitudeupdate_x1_kernel(tc, ta, tb, ba, bb, ga, 
             for b in range(4):
                 xb_mm(b, 1)
             ta_words(0)
-            ta_words(1)
+            root(1)
             tb_quantise(0, 1)
             factor_mult("a", 1)
             tb_quantise(1, 1)
             factor_group("a", 0, "g", "gate1")
             factor_group("a", 1, "s", "gate2")
-            ta_turn(2)
-            ta_turn(3)
             xb_both(4)
             for b in range(5):
                 xb_add(b)
+            ta_turn(1)
+            ta_turn(2)
             xb_both(5)
             xb_both(6)
-            ta_words(2)
-            ta_words(3)
-            ta_turn(4)
+            ta_turn(3)
             xb_both(7)
+            for b in range(1, 4):
+                ta_words(b)
+            ta_turn(4)
             ta_turn(5)
-            root(1)
-            ta_words(4)
-            ta_words(5)
             root(2)
-            ta_quantise(0)
-            factor_quantise("a", 0)
+            ta_words(4)
+            root(3)
+            ta_words(5)
             xb_quantise(0)
+            factor_quantise("a", 0)
+            ta_quantise(0)
             ta_quantise(1)
             factor_quantise("a", 1)
             square_beside(1, "gate2")
             xa_mm(0)
             xa_mm(1)
-            ta_turn(6)
-            xa_mm(2)
             for b in range(5, 8):
                 xb_add(b)
+            xa_mm(2)
             xa_mm(3)
-            ta_turn(7)
-            root(3)
-            ta_words(6)
+            ta_turn(6)
             square(3)
-            ta_words(7)
             xa_add(0)
             xa_add(1)
             xa_turn(0)
+            ta_turn(7)
             ta_quantise(2)
             xa_mm(4)
             xa_mm(5)
+            ta_words(6)
             xa_words(0, "s", "gate3")
             root(4)
+            ta_words(7)
             xb_quantise(1)
             xa_add(2)
-            xa_add(3)
-            xa_turn(1)
-            ta_quantise(3)
-            xa_words(1)
-            square(4)
             xa_quantise(0)
             square_beside(2, "gate3")
+            xa_add(3)
+            xa_turn(1)
             product(0, 0)
             product(0, 1)
+            xa_words(1)
+            square(4)
             xa_add(4)
             xa_add(5)
             xa_turn(2)
@@ -448,32 +454,44 @@ def tile_opposedspindirectringamplitudeupdate_x1_kernel(tc, ta, tb, ba, bb, ga, 
             last = BLOCKS - 1
             rest = [(root, 6), (square, 5), (root, 7), (square, 6), (square, 7)]
             for i in range(BLOCKS):
-                if i >= 2:
+                if i in (2, 4):
                     p_turn(i - 2)
                 if i == 3:
                     xa_turn(3)
                 if i < last:
                     product(i + 1, 0)
                     product(i + 1, 1)
-                if i < 2:
-                    xa_mm(i + 6)
+                if i == 2:
+                    p_turn(1)
+                if i >= 5:
+                    p_turn(i - 2)
                 divide(i, 0)
                 divide(i, 1)
                 store_r(i)
-                if i >= 2:
-                    p_words(i - 2)
                 if i == 3:
                     xa_words(3)
                 for step, b in rest[i : i + 1]:
                     step(b)
+                if i >= 2 and i != 3:
+                    p_words(i - 2)
+                if i == 2:
+                    p_words(1)
                 if i in (0, 2, 4):
                     xa_quantise(i // 2 + 1)
-                if i == 5:
+                if i == 0:
+                    ta_quantise(3)
+                if i < 2:
+                    xa_mm(i + 6)
+                if i == 4:
                     p_quantise(0, 2, 0)
                     p_quantise(0, 2, 1)
                     store_codes(0, 2)
                 if i < last:
-                    narrow(i, 0, 2, "g" if i < 6 else "s")
+                    narrow(i, 0, 2 if i < 5 else 1, "g")
+                if i == 6:
+                    narrow(i, 1, 2, "s")
+                if i == 5:
+                    narrow(i, 1, 2, "s")
                 if i in (1, 2):
                     xa_add(i + 5)
             narrow(last, 0, 1, "v")

@@ -36,9 +36,9 @@ def tile_opposedspindirectringamplitudeupdate_x1_kernel(tc, ta, tb, ba, bb, ga, 
                 gscale[s, c] = keep_tile([128, P], U8, "gscale%s%d" % (s, c))
         rows1 = [keep_tile([128, 4, P], BF16, "rows1%d" % c) for c in range(2)]
         bbt = keep_tile([128, M, 4], BF16, "bbt")
-        tbr = [pool.tile([128, 4, M], BF16, name="tbr%d" % c, tag="big", align_bytes=64) for c in range(2)]
+        tbr = {}
         tar = {}
-        dr = [keep_tile([128, M], BF16, "dr%d" % b) for b in range(BLOCKS)]
+        dr = [pool.tile([128, M], BF16, name="dr%d" % b, tag="two", bufs=BLOCKS, align_bytes=64) for b in range(BLOCKS)]
         rec = {b: keep_tile([128, M], F32, "rec%d" % b) for b in (0, 3, 4, 5)}
         tbcodes = [keep_tile([128, M], U32, "tbcodes%d" % c) for c in range(2)]
         tbscale = [keep_tile([128, M], U8, "tbscale%d" % c) for c in range(2)]
@@ -53,6 +53,11 @@ def tile_opposedspindirectringamplitudeupdate_x1_kernel(tc, ta, tb, ba, bb, ga, 
         with tc.manual_schedule():
             factor = {"a": ba, "b": bb}
 
+            def input_tile(shape, name, shared):
+                if shared:
+                    return pool.tile(shape, BF16, name=name, tag="four", bufs=BLOCKS, align_bytes=64)
+                return keep_tile(shape, BF16, name)
+
             def load_gain(s, g, queue):
                 queue.dma_start(out=gain[s][:], in_=g.rearrange("(c p j) -> p c j", p=128, j=4))
 
@@ -60,7 +65,7 @@ def tile_opposedspindirectringamplitudeupdate_x1_kernel(tc, ta, tb, ba, bb, ga, 
                 src = factor[s][512 * c : 512 * (c + 1), :].rearrange("(p j) w -> p j w", j=4)
                 step = 4 // pieces
                 for j0 in range(0, 4, step):
-                    piece = keep_tile([128, step, P], BF16, "rows4%s%d%d" % (s, c, j0))
+                    piece = input_tile([128, step, P], "rows4%s%d%d" % (s, c, j0), step == 4)
                     nc.sync.dma_start(out=piece[:], in_=src[:, j0 : j0 + step, :])
                     for j in range(step):
                         rows4[s, c, j0 + j] = piece[:, j, :]
@@ -68,14 +73,17 @@ def tile_opposedspindirectringamplitudeupdate_x1_kernel(tc, ta, tb, ba, bb, ga, 
             def load_rows1(c):
                 nc.sync.dma_start(out=rows1[c][:], in_=ba[512 * c : 512 * (c + 1), :].rearrange("(b p) w -> p b w", p=128))
 
-            def load_tb(c):
-                nc.sync.dma_start(out=tbr[c][:], in_=tb[512 * c : 512 * (c + 1), :].rearrange("(p j) w -> p j w", j=4))
+            def load_tb(c, h0, h1):
+                rows = pool.tile([128, 4, 512 * (h1 - h0)], BF16, name="tbr", tag="big%d" % (h1 - h0), bufs=3 - (h1 - h0), align_bytes=64)
+                nc.sync.dma_start(out=rows[:], in_=tb[512 * c : 512 * (c + 1), 512 * h0 : 512 * h1].rearrange("(p j) w -> p j w", j=4))
+                for h in range(h0, h1):
+                    tbr[c, h] = rows[:, :, 512 * (h - h0) : 512 * (h - h0 + 1)]
 
             def load_delta(b):
                 nc.sync.dma_start(out=dr[b][:], in_=delta[128 * b : 128 * (b + 1), :])
 
             def load_ta(b0, b1):
-                rows = keep_tile([128, b1 - b0, N], BF16, "tar%d" % b0)
+                rows = input_tile([128, b1 - b0, N], "tar%d" % b0, b1 - b0 == 2)
                 nc.sync.dma_start(out=rows[:], in_=ta[128 * b0 : 128 * b1, :].rearrange("(b p) k -> p b k", p=128))
                 for b in range(b0, b1):
                     tar[b] = rows[:, b - b0, :]
@@ -97,7 +105,7 @@ def tile_opposedspindirectringamplitudeupdate_x1_kernel(tc, ta, tb, ba, bb, ga, 
 
             def interleave(engine, name, src, tag="grouped", c0=0, c1=512):
                 if c0 == 0:
-                    grouped[name] = pool.tile([128, 512, 4], BF16, name="grouped", tag=tag, bufs=3 if tag == "grouped" else 1, align_bytes=64)
+                    grouped[name] = pool.tile([128, 512, 4], BF16, name="grouped", tag=tag, bufs=5 if tag == "grouped" else 1, align_bytes=64)
                 out, src = grouped[name][:, c0:c1, :], src[:, :, c0:c1].rearrange("p j w -> p w j")
                 if engine == "g":
                     nc.gpsimd.tensor_scalar(out=out, in0=src, scalar1=1.0, scalar2=-0.0, op0=ALU.mult, op1=ALU.add)
@@ -108,7 +116,7 @@ def tile_opposedspindirectringamplitudeupdate_x1_kernel(tc, ta, tb, ba, bb, ga, 
                 if s == "a":
                     interleave(engine, (s, c), scaled[s, c][:], tag, c0, c1)
                 else:
-                    grouped[s, c] = pool.tile([128, 512, 4], BF16, name="grouped", bufs=3, align_bytes=64)
+                    grouped[s, c] = pool.tile([128, 512, 4], BF16, name="grouped", bufs=5, align_bytes=64)
                     copy_on(engine)(
                         out=grouped[s, c][:].rearrange("p (t m e) j -> p m t e j", t=4, e=2),
                         in_=scaled[s, c][:].rearrange("p j (m e t) -> p m t e j", t=4, e=2),
@@ -118,7 +126,7 @@ def tile_opposedspindirectringamplitudeupdate_x1_kernel(tc, ta, tb, ba, bb, ga, 
                 quantise(gcodes[s, c][:], gscale[s, c][:], grouped[s, c][:].rearrange("p w j -> p (w j)"))
 
             def tb_group(c, h, engine, tag="grouped"):
-                interleave(engine, ("t", c, h), tbr[c][:, :, 512 * h : 512 * (h + 1)], tag)
+                interleave(engine, ("t", c, h), tbr[c, h], tag)
 
             def tb_quantise(c, h):
                 cols = slice(512 * h, 512 * (h + 1))
@@ -142,7 +150,7 @@ def tile_opposedspindirectringamplitudeupdate_x1_kernel(tc, ta, tb, ba, bb, ga, 
             def ta_words(b):
                 half = slice(128 * (b % 2), 128 * (b % 2) + 128)
                 if b % 2 == 0:
-                    tat[b // 2] = pool.tile([128, 2, 256, 4], BF16, name="tat", bufs=2, align_bytes=64)
+                    tat[b // 2] = pool.tile([128, 2, 256, 4], BF16, name="tat", tag="tat%d" % (b // 2 % 2), bufs=1, align_bytes=64)
                 nc.scalar.copy(out=word_view(tat[b // 2][:])[:, :, half, :], in_=tabank[b][:].rearrange("p (c u) n -> p c n u", c=2))
 
             def ta_quantise(q):
@@ -236,9 +244,9 @@ def tile_opposedspindirectringamplitudeupdate_x1_kernel(tc, ta, tb, ba, bb, ga, 
                     for u in range(2):
                         nc.tensor.transpose(xbank[q][:, 2 * k + u, :], words[:, 128 * u : 128 * (u + 1)], ident[:])
 
-            def xa_words(q, engine="s", tag="xat"):
-                xt["a", q] = pool.tile([128, 2, 128, 4], BF16, name="xat", tag=tag, bufs=2 if tag == "xat" else 1, align_bytes=64)
-                copy_on(engine)(out=word_view(xt["a", q][:]), in_=xbank[q][:].rearrange("p (k u) n -> p k n u", u=2))
+            def xa_words(q):
+                xt["a", q] = pool.tile([128, 2, 128, 4], BF16, name="xat", tag="xat%d" % q, bufs=1, align_bytes=64)
+                nc.scalar.copy(out=word_view(xt["a", q][:]), in_=xbank[q][:].rearrange("p (k u) n -> p k n u", u=2))
 
             def xa_quantise(q):
                 cols = slice(256 * q, 256 * (q + 1))
@@ -248,7 +256,7 @@ def tile_opposedspindirectringamplitudeupdate_x1_kernel(tc, ta, tb, ba, bb, ga, 
 
             def root(b):
                 if b not in rec:
-                    rec[b] = pool.tile([128, M], F32, name="rec%d" % b, tag="big", align_bytes=64)
+                    rec[b] = pool.tile([128, M], F32, name="rec%d" % b, tag="big1", bufs=2, align_bytes=64)
                 roots[b] = rec[b]
                 nc.scalar.activation(out=roots[b][:], in_=dr[b][:], func=ACT.Abs_reciprocal_sqrt)
 
@@ -280,14 +288,17 @@ def tile_opposedspindirectringamplitudeupdate_x1_kernel(tc, ta, tb, ba, bb, ga, 
             def divide(b, h):
                 cols = slice(512 * h, 512 * (h + 1))
                 if h == 0:
-                    r[b] = pool.tile([128, M], F32, name="r", bufs=3)
+                    r[b] = pool.tile([128, M], F32, name="r", tag="four", bufs=BLOCKS, align_bytes=64)
                 nc.vector.scalar_tensor_tensor(
                     out=r[b][:, cols], in0=prod[b, h][:], scalar=-1.0, in1=rec[b][:, cols], op0=ALU.mult, op1=ALU.mult
                 )
 
             def narrow(b, g0, g1, engine):
                 if g0 == 0:
-                    rb[b] = pool.tile([128, M], BF16, name="rb", bufs=3)
+                    if b in (0, 2, 4):
+                        rb[b] = pool.tile([128, M], BF16, name="rb", tag={0: "tat1", 2: "xat2", 4: "xat3"}[b], bufs=1, align_bytes=64)
+                    else:
+                        rb[b] = pool.tile([128, M], BF16, name="rb", tag="two", bufs=BLOCKS, align_bytes=64)
                 pairs = slice(128 * g0, 128 * g1)
                 out = rb[b][:].rearrange("p (u w e) -> p u w e", u=2, e=2)[:, :, pairs, :]
                 src = r[b][:].rearrange("p (w u e) -> p u w e", u=2, e=2)[:, :, pairs, :]
@@ -310,7 +321,7 @@ def tile_opposedspindirectringamplitudeupdate_x1_kernel(tc, ta, tb, ba, bb, ga, 
             def p_words(b, g0=0, g1=2, engine="s"):
                 half = slice(128 * (b % 2), 128 * (b % 2) + 128)
                 if b % 2 == 0 and g0 == 0:
-                    pt[b // 2] = pool.tile([128, 2, 256, 4], BF16, name="pt", bufs=3, align_bytes=64)
+                    pt[b // 2] = pool.tile([128, 2, 256, 4], BF16, name="pt", bufs=4, align_bytes=64)
                 copy_on(engine)(
                     out=word_view(pt[b // 2][:])[:, g0:g1, half, :],
                     in_=pb[b, g0][:, 2 * g0 : 2 * g1, :].rearrange("p (c u) n -> p c n u", u=2),
@@ -342,9 +353,10 @@ def tile_opposedspindirectringamplitudeupdate_x1_kernel(tc, ta, tb, ba, bb, ga, 
             load_rows4("b", 0, 2)
             load_delta(0)
             load_rows4("b", 1)
-            load_tb(0)
+            load_tb(0, 0, 2)
+            load_tb(1, 0, 1)
             load_ta(0, 1)
-            load_tb(1)
+            load_tb(1, 1, 2)
             load_gain("a", ga, nc.sync)
             load_rows4("a", 0)
             load_rows4("a", 1)
@@ -383,13 +395,13 @@ def tile_opposedspindirectringamplitudeupdate_x1_kernel(tc, ta, tb, ba, bb, ga, 
                 xb_mm(b, 0)
             tb_group(1, 0, "v")
             tb_group(1, 1, "s", "gate1")
-            factor_mult("a", 0)
+            tb_quantise(0, 1)
             tb_quantise(1, 0)
             for b in range(4):
                 xb_mm(b, 1)
             ta_words(0)
             root(1)
-            tb_quantise(0, 1)
+            factor_mult("a", 0)
             factor_mult("a", 1)
             tb_quantise(1, 1)
             factor_group("a", 0, "g", "gate1")
@@ -400,8 +412,8 @@ def tile_opposedspindirectringamplitudeupdate_x1_kernel(tc, ta, tb, ba, bb, ga, 
             ta_turn(1)
             ta_turn(2)
             xb_both(5)
-            xb_both(6)
             ta_turn(3)
+            xb_both(6)
             xb_both(7)
             for b in range(1, 4):
                 ta_words(b)
@@ -419,11 +431,12 @@ def tile_opposedspindirectringamplitudeupdate_x1_kernel(tc, ta, tb, ba, bb, ga, 
             square_beside(1, "gate2")
             xa_mm(0)
             xa_mm(1)
+            ta_turn(6)
+            ta_words(6)
             for b in range(5, 8):
                 xb_add(b)
             xa_mm(2)
             xa_mm(3)
-            ta_turn(6)
             square(3)
             xa_add(0)
             xa_add(1)
@@ -432,20 +445,19 @@ def tile_opposedspindirectringamplitudeupdate_x1_kernel(tc, ta, tb, ba, bb, ga, 
             ta_quantise(2)
             xa_mm(4)
             xa_mm(5)
-            ta_words(6)
-            xa_words(0, "s", "gate3")
+            xa_words(0)
             root(4)
             ta_words(7)
             xb_quantise(1)
             xa_add(2)
             xa_quantise(0)
-            square_beside(2, "gate3")
-            xa_add(3)
-            xa_turn(1)
+            square_beside(2, "xat0")
             product(0, 0)
             product(0, 1)
-            xa_words(1)
+            xa_add(3)
+            xa_turn(1)
             square(4)
+            xa_words(1)
             xa_add(4)
             xa_add(5)
             xa_turn(2)
@@ -456,40 +468,44 @@ def tile_opposedspindirectringamplitudeupdate_x1_kernel(tc, ta, tb, ba, bb, ga, 
             for i in range(BLOCKS):
                 if i in (2, 4):
                     p_turn(i - 2)
-                if i == 3:
-                    xa_turn(3)
                 if i < last:
                     product(i + 1, 0)
                     product(i + 1, 1)
+                if i == 3:
+                    xa_turn(3)
                 if i == 2:
                     p_turn(1)
                 if i >= 5:
                     p_turn(i - 2)
                 divide(i, 0)
+                if i == 6:
+                    narrow(i, 0, 1, "g")
                 divide(i, 1)
                 store_r(i)
                 if i == 3:
                     xa_words(3)
                 for step, b in rest[i : i + 1]:
                     step(b)
+                if i == 6:
+                    narrow(i, 1, 2, "s")
                 if i >= 2 and i != 3:
                     p_words(i - 2)
                 if i == 2:
                     p_words(1)
-                if i in (0, 2, 4):
-                    xa_quantise(i // 2 + 1)
                 if i == 0:
                     ta_quantise(3)
+                if i == 4:
+                    narrow(3, 1, 2, "v")
+                if i in (0, 2, 4):
+                    xa_quantise(i // 2 + 1)
                 if i < 2:
                     xa_mm(i + 6)
                 if i == 4:
                     p_quantise(0, 2, 0)
                     p_quantise(0, 2, 1)
                     store_codes(0, 2)
-                if i < last:
-                    narrow(i, 0, 2 if i < 5 else 1, "g")
-                if i == 6:
-                    narrow(i, 1, 2, "s")
+                if i < 6:
+                    narrow(i, 0, 1 if i in (3, 5) else 2, "g")
                 if i == 5:
                     narrow(i, 1, 2, "s")
                 if i in (1, 2):

@@ -38,7 +38,7 @@ def tile_opposedspindirectringamplitudeupdate_x1_kernel(tc, ta, tb, ba, bb, ga, 
         bbt = keep_tile([128, M, 4], BF16, "bbt")
         tbr = {}
         tar = {}
-        dr = [pool.tile([128, M], BF16, name="dr%d" % b, tag="two", bufs=BLOCKS, align_bytes=64) for b in range(BLOCKS)]
+        dr = [keep_tile([128, M], BF16, "dr%d" % b) for b in range(BLOCKS)]
         rec = {b: keep_tile([128, M], F32, "rec%d" % b) for b in (0, 3, 4, 5)}
         tbcodes = [keep_tile([128, M], U32, "tbcodes%d" % c) for c in range(2)]
         tbscale = [keep_tile([128, M], U8, "tbscale%d" % c) for c in range(2)]
@@ -74,7 +74,7 @@ def tile_opposedspindirectringamplitudeupdate_x1_kernel(tc, ta, tb, ba, bb, ga, 
                 nc.sync.dma_start(out=rows1[c][:], in_=ba[512 * c : 512 * (c + 1), :].rearrange("(b p) w -> p b w", p=128))
 
             def load_tb(c, h0, h1):
-                rows = pool.tile([128, 4, 512 * (h1 - h0)], BF16, name="tbr", tag="big%d" % (h1 - h0), bufs=3 - (h1 - h0), align_bytes=64)
+                rows = pool.tile([128, 4, 512 * (h1 - h0)], BF16, name="tbr", tag="big", bufs=2, align_bytes=64)
                 nc.sync.dma_start(out=rows[:], in_=tb[512 * c : 512 * (c + 1), 512 * h0 : 512 * h1].rearrange("(p j) w -> p j w", j=4))
                 for h in range(h0, h1):
                     tbr[c, h] = rows[:, :, 512 * (h - h0) : 512 * (h - h0 + 1)]
@@ -105,7 +105,7 @@ def tile_opposedspindirectringamplitudeupdate_x1_kernel(tc, ta, tb, ba, bb, ga, 
 
             def interleave(engine, name, src, tag="grouped", c0=0, c1=512):
                 if c0 == 0:
-                    grouped[name] = pool.tile([128, 512, 4], BF16, name="grouped", tag=tag, bufs=5 if tag == "grouped" else 1, align_bytes=64)
+                    grouped[name] = pool.tile([128, 512, 4], BF16, name="grouped", tag=tag, bufs=4 if tag == "grouped" else 1, align_bytes=64)
                 out, src = grouped[name][:, c0:c1, :], src[:, :, c0:c1].rearrange("p j w -> p w j")
                 if engine == "g":
                     nc.gpsimd.tensor_scalar(out=out, in0=src, scalar1=1.0, scalar2=-0.0, op0=ALU.mult, op1=ALU.add)
@@ -116,7 +116,7 @@ def tile_opposedspindirectringamplitudeupdate_x1_kernel(tc, ta, tb, ba, bb, ga, 
                 if s == "a":
                     interleave(engine, (s, c), scaled[s, c][:], tag, c0, c1)
                 else:
-                    grouped[s, c] = pool.tile([128, 512, 4], BF16, name="grouped", bufs=5, align_bytes=64)
+                    grouped[s, c] = pool.tile([128, 512, 4], BF16, name="grouped", bufs=4, align_bytes=64)
                     copy_on(engine)(
                         out=grouped[s, c][:].rearrange("p (t m e) j -> p m t e j", t=4, e=2),
                         in_=scaled[s, c][:].rearrange("p j (m e t) -> p m t e j", t=4, e=2),
@@ -256,7 +256,7 @@ def tile_opposedspindirectringamplitudeupdate_x1_kernel(tc, ta, tb, ba, bb, ga, 
 
             def root(b):
                 if b not in rec:
-                    rec[b] = pool.tile([128, M], F32, name="rec%d" % b, tag="big1", bufs=2, align_bytes=64)
+                    rec[b] = pool.tile([128, M], F32, name="rec%d" % b, tag="big", bufs=2, align_bytes=64)
                 roots[b] = rec[b]
                 nc.scalar.activation(out=roots[b][:], in_=dr[b][:], func=ACT.Abs_reciprocal_sqrt)
 
@@ -295,17 +295,14 @@ def tile_opposedspindirectringamplitudeupdate_x1_kernel(tc, ta, tb, ba, bb, ga, 
 
             def narrow(b, g0, g1, engine):
                 if g0 == 0:
-                    if b in (0, 2, 4):
-                        rb[b] = pool.tile([128, M], BF16, name="rb", tag={0: "tat1", 2: "xat2", 4: "xat3"}[b], bufs=1, align_bytes=64)
-                    else:
-                        rb[b] = pool.tile([128, M], BF16, name="rb", tag="two", bufs=BLOCKS, align_bytes=64)
+                    rb[b] = pool.tile([128, M], BF16, name="rb", bufs=4, align_bytes=64)
                 pairs = slice(128 * g0, 128 * g1)
                 out = rb[b][:].rearrange("p (u w e) -> p u w e", u=2, e=2)[:, :, pairs, :]
                 src = r[b][:].rearrange("p (w u e) -> p u w e", u=2, e=2)[:, :, pairs, :]
                 if engine == "g":
                     nc.gpsimd.tensor_scalar(out=out, in0=src, scalar1=1.0, scalar2=-0.0, op0=ALU.mult, op1=ALU.add)
                 else:
-                    copy_on(engine)(out=out, in_=src)
+                    copy_on(engine)(out=out.rearrange("p u (a w) e -> p a u w e", w=4), in_=src.rearrange("p u (a w) e -> p a u w e", w=4))
 
             pb, pt = {}, {}
 
@@ -321,7 +318,7 @@ def tile_opposedspindirectringamplitudeupdate_x1_kernel(tc, ta, tb, ba, bb, ga, 
             def p_words(b, g0=0, g1=2, engine="s"):
                 half = slice(128 * (b % 2), 128 * (b % 2) + 128)
                 if b % 2 == 0 and g0 == 0:
-                    pt[b // 2] = pool.tile([128, 2, 256, 4], BF16, name="pt", bufs=4, align_bytes=64)
+                    pt[b // 2] = pool.tile([128, 2, 256, 4], BF16, name="pt", bufs=3, align_bytes=64)
                 copy_on(engine)(
                     out=word_view(pt[b // 2][:])[:, g0:g1, half, :],
                     in_=pb[b, g0][:, 2 * g0 : 2 * g1, :].rearrange("p (c u) n -> p c n u", u=2),
@@ -354,9 +351,8 @@ def tile_opposedspindirectringamplitudeupdate_x1_kernel(tc, ta, tb, ba, bb, ga, 
             load_delta(0)
             load_rows4("b", 1)
             load_tb(0, 0, 2)
-            load_tb(1, 0, 1)
             load_ta(0, 1)
-            load_tb(1, 1, 2)
+            load_tb(1, 0, 2)
             load_gain("a", ga, nc.sync)
             load_rows4("a", 0)
             load_rows4("a", 1)
@@ -496,12 +492,13 @@ def tile_opposedspindirectringamplitudeupdate_x1_kernel(tc, ta, tb, ba, bb, ga, 
                     ta_quantise(3)
                 if i == 4:
                     narrow(3, 1, 2, "v")
+                if i == 4:
+                    p_quantise(0, 2, 0)
                 if i in (0, 2, 4):
                     xa_quantise(i // 2 + 1)
                 if i < 2:
                     xa_mm(i + 6)
                 if i == 4:
-                    p_quantise(0, 2, 0)
                     p_quantise(0, 2, 1)
                     store_codes(0, 2)
                 if i < 6:

@@ -38,8 +38,8 @@ def tile_opposedspindirectringamplitudeupdate_x1_kernel(tc, ta, tb, ba, bb, ga, 
         bbt = keep_tile([128, M, 4], BF16, "bbt")
         tbr = {}
         tar = {}
-        dr = [keep_tile([128, M], BF16, "dr%d" % b) for b in range(BLOCKS)]
-        rec = {b: keep_tile([128, M], F32, "rec%d" % b) for b in (0, 3, 4, 5)}
+        dr = {}
+        rec = {b: keep_tile([128, M], F32, "rec%d" % b) for b in (0, 1, 3, 4, 5, 7)}
         tbcodes = [keep_tile([128, M], U32, "tbcodes%d" % c) for c in range(2)]
         tbscale = [keep_tile([128, M], U8, "tbscale%d" % c) for c in range(2)]
         tacodes = [keep_tile([128, 2, 256], U32, "tacodes%d" % q) for q in range(4)]
@@ -53,10 +53,6 @@ def tile_opposedspindirectringamplitudeupdate_x1_kernel(tc, ta, tb, ba, bb, ga, 
         with tc.manual_schedule():
             factor = {"a": ba, "b": bb}
 
-            def input_tile(shape, name, shared):
-                if shared:
-                    return pool.tile(shape, BF16, name=name, tag="four", bufs=BLOCKS, align_bytes=64)
-                return keep_tile(shape, BF16, name)
 
             def load_gain(s, g, queue):
                 queue.dma_start(out=gain[s][:], in_=g.rearrange("(c p j) -> p c j", p=128, j=4))
@@ -65,7 +61,7 @@ def tile_opposedspindirectringamplitudeupdate_x1_kernel(tc, ta, tb, ba, bb, ga, 
                 src = factor[s][512 * c : 512 * (c + 1), :].rearrange("(p j) w -> p j w", j=4)
                 step = 4 // pieces
                 for j0 in range(0, 4, step):
-                    piece = input_tile([128, step, P], "rows4%s%d%d" % (s, c, j0), step == 4)
+                    piece = keep_tile([128, step, P], BF16, "rows4%s%d%d" % (s, c, j0))
                     nc.sync.dma_start(out=piece[:], in_=src[:, j0 : j0 + step, :])
                     for j in range(step):
                         rows4[s, c, j0 + j] = piece[:, j, :]
@@ -79,11 +75,14 @@ def tile_opposedspindirectringamplitudeupdate_x1_kernel(tc, ta, tb, ba, bb, ga, 
                 for h in range(h0, h1):
                     tbr[c, h] = rows[:, :, 512 * (h - h0) : 512 * (h - h0 + 1)]
 
-            def load_delta(b):
-                nc.sync.dma_start(out=dr[b][:], in_=delta[128 * b : 128 * (b + 1), :])
+            def load_delta(b0, b1):
+                rows = keep_tile([128, b1 - b0, M], BF16, "dr%d" % b0)
+                nc.sync.dma_start(out=rows[:], in_=delta[128 * b0 : 128 * b1, :].rearrange("(b p) m -> p b m", p=128))
+                for b in range(b0, b1):
+                    dr[b] = rows[:, b - b0, :]
 
             def load_ta(b0, b1):
-                rows = input_tile([128, b1 - b0, N], "tar%d" % b0, b1 - b0 == 2)
+                rows = keep_tile([128, b1 - b0, N], BF16, "tar%d" % b0)
                 nc.sync.dma_start(out=rows[:], in_=ta[128 * b0 : 128 * b1, :].rearrange("(b p) k -> p b k", p=128))
                 for b in range(b0, b1):
                     tar[b] = rows[:, b - b0, :]
@@ -97,7 +96,7 @@ def tile_opposedspindirectringamplitudeupdate_x1_kernel(tc, ta, tb, ba, bb, ga, 
             scaled, grouped = {}, {}
 
             def factor_mult(s, c):
-                scaled[s, c] = pool.tile([128, 4, P], BF16, name="scaled", align_bytes=64)
+                scaled[s, c] = pool.tile([128, 4, P], BF16, name="scaled", bufs=2, align_bytes=64)
                 for j in range(4):
                     nc.vector.tensor_scalar(
                         out=scaled[s, c][:, j, :], in0=rows4[s, c, j], scalar1=gain[s][:, c, j : j + 1], scalar2=None, op0=ALU.mult
@@ -150,7 +149,7 @@ def tile_opposedspindirectringamplitudeupdate_x1_kernel(tc, ta, tb, ba, bb, ga, 
             def ta_words(b):
                 half = slice(128 * (b % 2), 128 * (b % 2) + 128)
                 if b % 2 == 0:
-                    tat[b // 2] = pool.tile([128, 2, 256, 4], BF16, name="tat", tag="tat%d" % (b // 2 % 2), bufs=1, align_bytes=64)
+                    tat[b // 2] = pool.tile([128, 2, 256, 4], BF16, name="tat", tag=("tat0", "gate2", "tat0", "tat1")[b // 2], bufs=1, align_bytes=64)
                 nc.scalar.copy(out=word_view(tat[b // 2][:])[:, :, half, :], in_=tabank[b][:].rearrange("p (c u) n -> p c n u", c=2))
 
             def ta_quantise(q):
@@ -197,7 +196,7 @@ def tile_opposedspindirectringamplitudeupdate_x1_kernel(tc, ta, tb, ba, bb, ga, 
                 xb_mm(b, 1)
 
             def xb_add(b):
-                if b % 4 == 0:
+                if ("b", b // 4) not in xt:
                     xt["b", b // 4] = pool.tile([128, 512, 4], BF16, name="xbt", tag="xbt%d" % (b // 4), bufs=1, align_bytes=64)
                 nc.vector.tensor_tensor(
                     out=xt["b", b // 4][:, 128 * (b % 4) : 128 * (b % 4) + 128, :],
@@ -258,7 +257,7 @@ def tile_opposedspindirectringamplitudeupdate_x1_kernel(tc, ta, tb, ba, bb, ga, 
                 if b not in rec:
                     rec[b] = pool.tile([128, M], F32, name="rec%d" % b, tag="big", bufs=2, align_bytes=64)
                 roots[b] = rec[b]
-                nc.scalar.activation(out=roots[b][:], in_=dr[b][:], func=ACT.Abs_reciprocal_sqrt)
+                nc.scalar.activation(out=roots[b][:], in_=dr[b], func=ACT.Abs_reciprocal_sqrt)
 
             def square(b):
                 nc.scalar.activation(out=rec[b][:], in_=roots[b][:], func=ACT.Square)
@@ -269,7 +268,7 @@ def tile_opposedspindirectringamplitudeupdate_x1_kernel(tc, ta, tb, ba, bb, ga, 
 
             prod = {}
 
-            def product(b, h):
+            def product_half(b, h):
                 own = slice(128 * b, 128 * (b + 1))
                 cols = slice(512 * h, 512 * (h + 1))
                 prod[b, h] = psum.tile([128, 512], F32, name="prod", tag="mm", bufs=5)
@@ -283,12 +282,17 @@ def tile_opposedspindirectringamplitudeupdate_x1_kernel(tc, ta, tb, ba, bb, ga, 
                     stop=True,
                 )
 
+            def product(b):
+                product_half(b, 1)
+                product_half(b, 0)
+
             r, rb = {}, {}
 
             def divide(b, h):
                 cols = slice(512 * h, 512 * (h + 1))
                 if h == 0:
-                    r[b] = pool.tile([128, M], F32, name="r", tag="four", bufs=BLOCKS, align_bytes=64)
+                    tag, bufs = ([("grouped", 4)] * 4 + [("xbt0", 1), ("xbt1", 1), ("gate1", 1), ("scaled", 2)])[b]
+                    r[b] = pool.tile([128, M], F32, name="r", tag=tag, bufs=bufs, align_bytes=64)
                 nc.vector.scalar_tensor_tensor(
                     out=r[b][:, cols], in0=prod[b, h][:], scalar=-1.0, in1=rec[b][:, cols], op0=ALU.mult, op1=ALU.mult
                 )
@@ -348,7 +352,7 @@ def tile_opposedspindirectringamplitudeupdate_x1_kernel(tc, ta, tb, ba, bb, ga, 
 
             load_gain("b", gb, nc.scalar)
             load_rows4("b", 0, 2)
-            load_delta(0)
+            load_delta(0, 1)
             load_rows4("b", 1)
             load_tb(0, 0, 2)
             load_ta(0, 1)
@@ -356,19 +360,16 @@ def tile_opposedspindirectringamplitudeupdate_x1_kernel(tc, ta, tb, ba, bb, ga, 
             load_gain("a", ga, nc.sync)
             load_rows4("a", 0)
             load_rows4("a", 1)
-            load_delta(1)
+            load_delta(1, 2)
             load_ta(1, 2)
             load_ta(2, 4)
             load_ta(4, 6)
-            load_delta(2)
-            load_rows1(0)
+            load_delta(2, 4)
             load_ta(6, 8)
-            load_delta(3)
-            load_delta(4)
+            load_rows1(0)
+            load_delta(4, 6)
             load_rows1(1)
-            load_delta(5)
-            load_delta(6)
-            load_delta(7)
+            load_delta(6, 8)
 
             root(0)
             for c in range(2):
@@ -393,7 +394,7 @@ def tile_opposedspindirectringamplitudeupdate_x1_kernel(tc, ta, tb, ba, bb, ga, 
             tb_group(1, 1, "s", "gate1")
             tb_quantise(0, 1)
             tb_quantise(1, 0)
-            for b in range(4):
+            for b in reversed(range(4)):
                 xb_mm(b, 1)
             ta_words(0)
             root(1)
@@ -401,20 +402,22 @@ def tile_opposedspindirectringamplitudeupdate_x1_kernel(tc, ta, tb, ba, bb, ga, 
             factor_mult("a", 1)
             tb_quantise(1, 1)
             factor_group("a", 0, "g", "gate1")
-            factor_group("a", 1, "s", "gate2")
+            factor_group("a", 1, "s")
             xb_both(4)
             for b in range(5):
                 xb_add(b)
             ta_turn(1)
             ta_turn(2)
             xb_both(5)
-            ta_turn(3)
             xb_both(6)
-            xb_both(7)
-            for b in range(1, 4):
-                ta_words(b)
+            ta_turn(3)
+            ta_words(1)
             ta_turn(4)
+            xb_both(7)
+            ta_words(2)
+            ta_words(3)
             ta_turn(5)
+            ta_turn(6)
             root(2)
             ta_words(4)
             root(3)
@@ -422,12 +425,11 @@ def tile_opposedspindirectringamplitudeupdate_x1_kernel(tc, ta, tb, ba, bb, ga, 
             xb_quantise(0)
             factor_quantise("a", 0)
             ta_quantise(0)
-            ta_quantise(1)
             factor_quantise("a", 1)
+            ta_quantise(1)
             square_beside(1, "gate2")
             xa_mm(0)
             xa_mm(1)
-            ta_turn(6)
             ta_words(6)
             for b in range(5, 8):
                 xb_add(b)
@@ -448,8 +450,7 @@ def tile_opposedspindirectringamplitudeupdate_x1_kernel(tc, ta, tb, ba, bb, ga, 
             xa_add(2)
             xa_quantise(0)
             square_beside(2, "xat0")
-            product(0, 0)
-            product(0, 1)
+            product(0)
             xa_add(3)
             xa_turn(1)
             square(4)
@@ -465,8 +466,7 @@ def tile_opposedspindirectringamplitudeupdate_x1_kernel(tc, ta, tb, ba, bb, ga, 
                 if i in (2, 4):
                     p_turn(i - 2)
                 if i < last:
-                    product(i + 1, 0)
-                    product(i + 1, 1)
+                    product(i + 1)
                 if i == 3:
                     xa_turn(3)
                 if i == 2:

@@ -336,10 +336,10 @@ def tile_opposedspindirectringamplitudeupdate_x1_kernel(tc, ta, tb, ba, bb, ga, 
             def store_r(b, c0=0, c1=M):
                 nc.sync.dma_start(out=out_0[128 * b : 128 * (b + 1), c0:c1], in_=r[b][:, c0:c1])
 
-            def store_codes(b0, b1):
+            def store_codes(b0, b1, g0=0, g1=2):
                 cols = slice(128 * b0, 128 * b1)
                 nc.sync.dma_start(
-                    out=out_1[:, :, cols, :].rearrange("g p n f -> p g (n f)").bitcast(I32), in_=pcodes[:, :, cols].bitcast(I32)
+                    out=out_1[g0:g1, :, cols, :].rearrange("g p n f -> p g (n f)").bitcast(I32), in_=pcodes[:, g0:g1, cols].bitcast(I32)
                 )
 
             def store_scales(b0, b1, queues):
@@ -518,7 +518,9 @@ def tile_opposedspindirectringamplitudeupdate_x1_kernel(tc, ta, tb, ba, bb, ga, 
             for g in range(2):
                 p_turn(last, g, g + 1)
                 p_words(last, g, g + 1)
-            p_quantise(6, 8, 0)
-            p_quantise(6, 8, 1)
-            store_codes(6, 8)
+            p_quantise(6, 7, 0)
+            p_quantise(6, 7, 1)
+            for g in range(2):
+                p_quantise(7, 8, g)
+                store_codes(6, 8, g, g + 1)
             store_scales(0, 8, (nc.scalar, nc.sync))

@@ -14,48 +14,50 @@ ACT = mybir.ActivationFunctionType
 
 N, M, P = 1024, 1024, 512
 FLOPS = 2 * N * N * P + 2 * M * M * P + 2 * N * M * P
-BLOCKS = N // 128
 
 
 def tile_opposedspindirectringamplitudeupdate_x1_kernel(tc, ta, tb, ba, bb, ga, gb, delta, out_0, out_1, out_2):
     nc = tc.nc
     with ExitStack() as ctx:
         keep = ctx.enter_context(tc.tile_pool(name="keep", bufs=1))
-        pool = ctx.enter_context(tc.tile_pool(name="work", bufs=2))
-        psum = ctx.enter_context(tc.psum_pool(name="psum", bufs=2))
+        psum = ctx.enter_context(tc.psum_pool(name="psum", bufs=1))
 
-        def keep_tile(shape, dtype, name):
-            return keep.tile(shape, dtype, name=name, align_bytes=64)
+        def keep_tile(shape, dtype, name, tag=None):
+            return keep.tile(shape, dtype, name=name, tag=tag or name, align_bytes=64)
 
         ident = keep_tile([128, 128], F32, "ident")
-        gain, rows4, rows1, gcodes, gscale = {}, {}, {}, {}, {}
-        for s in ("b", "a"):
+        factor = {"a": ba, "b": bb}
+        gain, rows4, gcodes, gscale, xt, xcodes, xscale = {}, {}, {}, {}, {}, {}, {}
+        for s in ("a", "b"):
             gain[s] = keep_tile([128, 2, 4], BF16, "gain" + s)
+            xcodes[s] = keep_tile([128, N], U32, "xcodes" + s)
+            xscale[s] = keep_tile([128, N], U8, "xscale" + s)
             for c in range(2):
                 gcodes[s, c] = keep_tile([128, P], U32, "gcodes%s%d" % (s, c))
                 gscale[s, c] = keep_tile([128, P], U8, "gscale%s%d" % (s, c))
-        rows1 = [keep_tile([128, 4, P], BF16, "rows1%d" % c) for c in range(2)]
-        bbt = keep_tile([128, M, 4], BF16, "bbt")
-        tbr = {}
-        tar = {}
-        dr = {}
-        rec = {b: keep_tile([128, M], F32, "rec%d" % b) for b in (0, 1, 3, 4, 5, 7)}
-        tbcodes = [keep_tile([128, M], U32, "tbcodes%d" % c) for c in range(2)]
-        tbscale = [keep_tile([128, M], U8, "tbscale%d" % c) for c in range(2)]
+                xt[s, c] = keep_tile([128, 512 * 4], BF16, "xt%s%d" % (s, c))
+        tbcodes, tbscale = {}, {}
+        for c in range(2):
+            for h in range(2):
+                tbcodes[c, h] = keep_tile([128, 512], U32, "tbcodes%d%d" % (c, h))
+                tbscale[c, h] = keep_tile([128, 512], U8, "tbscale%d%d" % (c, h))
         tacodes = [keep_tile([128, 2, 256], U32, "tacodes%d" % q) for q in range(4)]
         tascale = [keep_tile([128, 2, 256], U8, "tascale%d" % q) for q in range(4)]
-        xcodes = {s: keep_tile([128, M], U32, "xcodes" + s) for s in ("b", "a")}
-        xscale = {s: keep_tile([128, M], U8, "xscale" + s) for s in ("b", "a")}
-        pcodes = keep_tile([128, 2, N], U32, "pcodes")
+        rec = {(q, h): keep_tile([128, 2, 512], F32, "rec%d%d" % (q, h)) for q in range(4) for h in range(2)}
+        pcodes = [keep_tile([128, N], U32, "pcodes%d" % h) for h in range(2)]
         pscale = keep_tile([128, 2, N], U8, "pscale")
+        tar, tbr, dr = {}, {}, {}
 
+        grow = keep_tile([128, 512], BF16, "grow")
+        nc.gpsimd.memset(grow[:].bitcast(I32), 0)
         make_identity(nc, ident[:])
         with tc.manual_schedule():
-            factor = {"a": ba, "b": bb}
-
 
             def load_gain(s, g, queue):
                 queue.dma_start(out=gain[s][:], in_=g.rearrange("(c p j) -> p c j", p=128, j=4))
+
+            def load_gain_row(row, g, c, queue):
+                queue.dma_start(out=grow[row : row + 1, :], in_=g[512 * c : 512 * (c + 1)].rearrange("(r w) -> r w", r=1))
 
             def load_rows4(s, c, pieces=1):
                 src = factor[s][512 * c : 512 * (c + 1), :].rearrange("(p j) w -> p j w", j=4)
@@ -63,23 +65,22 @@ def tile_opposedspindirectringamplitudeupdate_x1_kernel(tc, ta, tb, ba, bb, ga, 
                 for j0 in range(0, 4, step):
                     piece = keep_tile([128, step, P], BF16, "rows4%s%d%d" % (s, c, j0))
                     nc.sync.dma_start(out=piece[:], in_=src[:, j0 : j0 + step, :])
+                    rows4[s, c] = piece
                     for j in range(step):
                         rows4[s, c, j0 + j] = piece[:, j, :]
 
-            def load_rows1(c):
-                nc.sync.dma_start(out=rows1[c][:], in_=ba[512 * c : 512 * (c + 1), :].rearrange("(b p) w -> p b w", p=128))
-
             def load_tb(c, h0, h1):
-                rows = pool.tile([128, 4, 512 * (h1 - h0)], BF16, name="tbr", tag="big", bufs=2, align_bytes=64)
+                rows = keep_tile([128, 4, 512 * (h1 - h0)], BF16, "tbr%d%d" % (c, h0))
                 nc.sync.dma_start(out=rows[:], in_=tb[512 * c : 512 * (c + 1), 512 * h0 : 512 * h1].rearrange("(p j) w -> p j w", j=4))
                 for h in range(h0, h1):
                     tbr[c, h] = rows[:, :, 512 * (h - h0) : 512 * (h - h0 + 1)]
 
-            def load_delta(b0, b1):
-                rows = keep_tile([128, b1 - b0, M], BF16, "dr%d" % b0)
-                nc.sync.dma_start(out=rows[:], in_=delta[128 * b0 : 128 * b1, :].rearrange("(b p) m -> p b m", p=128))
-                for b in range(b0, b1):
-                    dr[b] = rows[:, b - b0, :]
+            def load_delta(q, h0, h1, k0=0, k1=2, queue=nc.sync):
+                rows = keep_tile([128, k1 - k0, 512 * (h1 - h0)], BF16, "dr%d%d%d" % (q, h0, k0))
+                src = delta[256 * q + 128 * k0 : 256 * q + 128 * k1, 512 * h0 : 512 * h1]
+                queue.dma_start(out=rows[:], in_=src.rearrange("(k p) m -> p k m", p=128))
+                for h in range(h0, h1):
+                    dr[q, h, k0, k1] = rows[:, :, 512 * (h - h0) : 512 * (h - h0 + 1)]
 
             def load_ta(b0, b1):
                 rows = keep_tile([128, b1 - b0, N], BF16, "tar%d" % b0)
@@ -87,193 +88,142 @@ def tile_opposedspindirectringamplitudeupdate_x1_kernel(tc, ta, tb, ba, bb, ga, 
                 for b in range(b0, b1):
                     tar[b] = rows[:, b - b0, :]
 
+            def bank_tile(bank):
+                return psum.tile([128, 4, 128], F32, name="bank", tag="bank%d" % bank)
+
             def copy_on(engine):
                 return nc.vector.tensor_copy if engine == "v" else nc.scalar.copy
+
+            def move(engine, out, src):
+                if engine == "g":
+                    nc.gpsimd.tensor_scalar(out=out, in0=src, scalar1=1.0, scalar2=-0.0, op0=ALU.mult, op1=ALU.add)
+                else:
+                    copy_on(engine)(out=out, in_=src)
 
             def quantise(codes, scale, values):
                 nc.vector.quantize_mx(out=codes.bitcast(FP8X4), scales=scale, in_=values)
 
             scaled, grouped = {}, {}
 
-            def factor_mult(s, c):
-                scaled[s, c] = pool.tile([128, 4, P], BF16, name="scaled", bufs=2, align_bytes=64)
+            def factor_mult(s, c, slot):
+                scaled[s, c] = keep_tile([128, 4 * P], BF16, "scaled", slot)
                 for j in range(4):
                     nc.vector.tensor_scalar(
-                        out=scaled[s, c][:, j, :], in0=rows4[s, c, j], scalar1=gain[s][:, c, j : j + 1], scalar2=None, op0=ALU.mult
+                        out=scaled[s, c][:, P * j : P * (j + 1)], in0=rows4[s, c, j], scalar1=gain[s][:, c, j : j + 1], scalar2=None, op0=ALU.mult
                     )
 
-            def interleave(engine, name, src, tag="grouped", c0=0, c1=512):
-                if c0 == 0:
-                    grouped[name] = pool.tile([128, 512, 4], BF16, name="grouped", tag=tag, bufs=4 if tag == "grouped" else 1, align_bytes=64)
-                out, src = grouped[name][:, c0:c1, :], src[:, :, c0:c1].rearrange("p j w -> p w j")
-                if engine == "g":
-                    nc.gpsimd.tensor_scalar(out=out, in0=src, scalar1=1.0, scalar2=-0.0, op0=ALU.mult, op1=ALU.add)
-                else:
-                    copy_on(engine)(out=out, in_=src)
+            def factor_group(s, c, engine, slot):
+                grouped[s, c] = keep_tile([128, 4 * P], BF16, "grouped", slot)
+                copy_on(engine)(
+                    out=grouped[s, c][:].rearrange("p (t m e j) -> p m t e j", t=4, e=2, j=4),
+                    in_=scaled[s, c][:].rearrange("p (j m e t) -> p m t e j", t=4, e=2, j=4),
+                )
 
-            def factor_group(s, c, engine="v", tag="grouped", c0=0, c1=512):
-                if s == "a":
-                    interleave(engine, (s, c), scaled[s, c][:], tag, c0, c1)
-                else:
-                    grouped[s, c] = pool.tile([128, 512, 4], BF16, name="grouped", bufs=4, align_bytes=64)
-                    copy_on(engine)(
-                        out=grouped[s, c][:].rearrange("p (t m e) j -> p m t e j", t=4, e=2),
-                        in_=scaled[s, c][:].rearrange("p j (m e t) -> p m t e j", t=4, e=2),
-                    )
+            gbank = {}
+
+            def gain_turn(bank):
+                gbank[0] = bank_tile(bank)[:].rearrange("p a n -> p (a n)").rearrange("p (r x) -> p r x", x=4)
+                for u in range(2):
+                    nc.tensor.transpose(gbank[0][:, :, u], grow[:].bitcast(F32)[:, u::2], ident[:])
+
+            def factor_fused(s, c, row, slot):
+                grouped[s, c] = keep_tile([128, 4 * P], BF16, "grouped", slot)
+                four = gbank[0][:, row, 0:2].bitcast(BF16)
+                nc.vector.tensor_tensor(
+                    out=grouped[s, c][:].rearrange("p (t m j) -> p m t j", t=4, j=4),
+                    in0=rows4[s, c][:].rearrange("p j (m t) -> p m t j", t=4),
+                    in1=four.unsqueeze(1).unsqueeze(1).to_broadcast([128, 128, 4, 4]),
+                    op=ALU.mult,
+                )
 
             def factor_quantise(s, c):
-                quantise(gcodes[s, c][:], gscale[s, c][:], grouped[s, c][:].rearrange("p w j -> p (w j)"))
+                quantise(gcodes[s, c][:], gscale[s, c][:], grouped[s, c][:])
 
-            def tb_group(c, h, engine, tag="grouped"):
-                interleave(engine, ("t", c, h), tbr[c, h], tag)
+            def tb_group(c, h, engine, slot, w0=0, w1=512):
+                grouped["t", c, h, w0] = keep_tile([128, 4 * (w1 - w0)], BF16, "grouped", slot)
+                move(engine, grouped["t", c, h, w0][:].rearrange("p (w j) -> p w j", j=4), tbr[c, h][:, :, w0:w1].rearrange("p j w -> p w j"))
 
-            def tb_quantise(c, h):
-                cols = slice(512 * h, 512 * (h + 1))
-                quantise(tbcodes[c][:, cols], tbscale[c][:, cols], grouped["t", c, h][:].rearrange("p w j -> p (w j)"))
-
-            def turn_bank():
-                return psum.tile([128, 4, 128], F32, name="turn", bufs=3)
-
-            def word_view(tile_ap):
-                return tile_ap.rearrange("p c n f -> p (c n f)").bitcast(F32).rearrange("p (c n u) -> p c n u", c=2, u=2)
+            def tb_quantise(c, h, w0=0, w1=512):
+                quantise(tbcodes[c, h][:, w0:w1], tbscale[c, h][:, w0:w1], grouped["t", c, h, w0][:])
 
             tabank, tat = {}, {}
 
-            def ta_turn(b):
+            def ta_turn(b, bank):
                 words = tar[b].bitcast(F32)
-                tabank[b] = turn_bank()
+                tabank[b] = bank_tile(bank)
                 for c in range(2):
                     for u in range(2):
                         nc.tensor.transpose(tabank[b][:, 2 * c + u, :], words[:, 256 * c + u : 256 * (c + 1) : 2], ident[:])
 
-            def ta_words(b):
-                half = slice(128 * (b % 2), 128 * (b % 2) + 128)
+            def ta_words(b, slot=None, engine="s"):
                 if b % 2 == 0:
-                    tat[b // 2] = pool.tile([128, 2, 256, 4], BF16, name="tat", tag=("tat0", "gate2", "tat0", "tat1")[b // 2], bufs=1, align_bytes=64)
-                nc.scalar.copy(out=word_view(tat[b // 2][:])[:, :, half, :], in_=tabank[b][:].rearrange("p (c u) n -> p c n u", c=2))
+                    tat[b // 2] = keep_tile([128, 2 * 256 * 4], BF16, "tat", slot)
+                words = tat[b // 2][:].bitcast(F32).rearrange("p (c n u) -> p c n u", c=2, u=2)
+                copy_on(engine)(out=words[:, :, 128 * (b % 2) : 128 * (b % 2) + 128, :], in_=tabank[b][:].rearrange("p (c u) n -> p c n u", c=2))
 
             def ta_quantise(q):
-                quantise(
-                    tacodes[q][:].rearrange("p c n -> p (c n)"),
-                    tascale[q][:].rearrange("p c n -> p (c n)"),
-                    tat[q][:].rearrange("p c n f -> p (c n f)"),
-                )
+                quantise(tacodes[q][:].rearrange("p c n -> p (c n)"), tascale[q][:].rearrange("p c n -> p (c n)"), tat[q][:])
 
-            ybank, xrows, xbank, xt = {}, {}, {}, {}
+            fbank, ybank = {}, {}
 
-            bbank = {}
-
-            def bb_turn(c, h):
-                bbank[c, h] = turn_bank()
+            def factor_turn(s, c, h, bank):
+                fbank[s, c, h] = bank_tile(bank)
                 for jj in range(2):
-                    words = rows4["b", c, 2 * h + jj].bitcast(F32)
+                    words = rows4[s, c, 2 * h + jj].bitcast(F32)
                     for u in range(2):
-                        nc.tensor.transpose(bbank[c, h][:, 2 * jj + u, :], words[:, u::2], ident[:])
+                        nc.tensor.transpose(fbank[s, c, h][:, 2 * jj + u, :], words[:, u::2], ident[:])
 
-            def bb_words(c, h):
-                dst = bbt[:].rearrange("p n f -> p (n f)").bitcast(F32)
-                dst = dst[:, 1024 * c : 1024 * (c + 1)].rearrange("p (q r) -> p q r", r=8)[:, :, 4 * h : 4 * h + 4]
-                nc.scalar.copy(out=dst, in_=bbank[c, h][:].rearrange("p r q -> p q r"))
+            def factor_words(s, c, h, engine="s"):
+                dst = xt[s, c][:].bitcast(F32).rearrange("p (q r) -> p q r", r=8)[:, :, 4 * h : 4 * h + 4]
+                copy_on(engine)(out=dst, in_=fbank[s, c, h][:].rearrange("p r q -> p q r"))
 
-            def xb_mm(b, c):
+            def x_mm(s, b, c, bank=None):
                 if c == 0:
-                    ybank["b", b] = psum.tile([128, 4, 128], F32, name="dress", tag="mm", bufs=5)
-                own = slice(128 * b, 128 * (b + 1))
+                    ybank[s, b] = bank_tile(bank)
+                if s == "a":
+                    own = slice(128 * (b % 2), 128 * (b % 2) + 128)
+                    codes, scale = tacodes[b // 2][:, c, own], tascale[b // 2][:, c, own]
+                else:
+                    own = slice(128 * (b % 4), 128 * (b % 4) + 128)
+                    codes, scale = tbcodes[c, b // 4][:, own], tbscale[c, b // 4][:, own]
                 for t in range(4):
                     cols = slice(128 * t, 128 * (t + 1))
                     nc.tensor.matmul_mx(
-                        out=ybank["b", b][:, t, :],
-                        lhsT=gcodes["b", c][:, cols].bitcast(FP8X4),
-                        lhsT_scale=gscale["b", c][:, cols],
-                        rhs=tbcodes[c][:, own].bitcast(FP8X4),
-                        rhs_scale=tbscale[c][:, own],
+                        out=ybank[s, b][:, t, :],
+                        lhsT=gcodes[s, c][:, cols].bitcast(FP8X4),
+                        lhsT_scale=gscale[s, c][:, cols],
+                        rhs=codes.bitcast(FP8X4),
+                        rhs_scale=scale,
                         start=(c == 0 and t == 0),
                         stop=(c == 1 and t == 3),
                     )
 
-            def xb_both(b):
-                xb_mm(b, 0)
-                xb_mm(b, 1)
+            def x_both(s, b, bank):
+                x_mm(s, b, 0, bank)
+                x_mm(s, b, 1)
 
-            def xb_add(b):
-                if ("b", b // 4) not in xt:
-                    xt["b", b // 4] = pool.tile([128, 512, 4], BF16, name="xbt", tag="xbt%d" % (b // 4), bufs=1, align_bytes=64)
-                nc.vector.tensor_tensor(
-                    out=xt["b", b // 4][:, 128 * (b % 4) : 128 * (b % 4) + 128, :],
-                    in0=ybank["b", b][:].rearrange("p t n -> p n t"),
-                    in1=bbt[:, 128 * b : 128 * (b + 1), :],
-                    op=ALU.add,
-                )
+            def x_add(s, b):
+                own = xt[s, b // 4][:, 512 * (b % 4) : 512 * (b % 4 + 1)].rearrange("p (n t) -> p n t", t=4)
+                nc.vector.tensor_tensor(out=own, in0=ybank[s, b][:].rearrange("p t n -> p n t"), in1=own, op=ALU.add)
 
-            def xb_quantise(h):
+            def x_quantise(s, h):
                 cols = slice(512 * h, 512 * (h + 1))
-                quantise(xcodes["b"][:, cols], xscale["b"][:, cols], xt["b", h][:].rearrange("p n f -> p (n f)"))
+                quantise(xcodes[s][:, cols], xscale[s][:, cols], xt[s, h][:])
 
-            def xa_pass(b, c):
-                if c == 0:
-                    ybank["a", b] = psum.tile([128, P], F32, name="dress", tag="mm", bufs=5)
-                own = slice(128 * (b % 2), 128 * (b % 2) + 128)
-                nc.tensor.matmul_mx(
-                    out=ybank["a", b][:],
-                    lhsT=tacodes[b // 2][:, c, own].bitcast(FP8X4),
-                    lhsT_scale=tascale[b // 2][:, c, own],
-                    rhs=gcodes["a", c][:].bitcast(FP8X4),
-                    rhs_scale=gscale["a", c][:],
-                    start=(c == 0),
-                    stop=(c == 1),
-                )
+            def root(q, h, k0=0, k1=2):
+                nc.scalar.activation(out=rec[q, h][:, k0:k1, :], in_=dr[q, h, k0, k1], func=ACT.Abs_reciprocal_sqrt)
 
-            def xa_mm(b):
-                xa_pass(b, 0)
-                xa_pass(b, 1)
-
-            def xa_add(b):
-                xrows[b] = pool.tile([128, P], BF16, name="xrows", bufs=4, align_bytes=64)
-                nc.vector.tensor_tensor(
-                    out=xrows[b][:].rearrange("p (u w e) -> p u w e", u=2, e=2),
-                    in0=ybank["a", b][:].rearrange("p (w u e) -> p u w e", u=2, e=2),
-                    in1=rows1[b // 4][:, b % 4, :].rearrange("p (w u e) -> p u w e", u=2, e=2),
-                    op=ALU.add,
-                )
-
-            def xa_turn(q):
-                xbank[q] = turn_bank()
-                for k in range(2):
-                    words = xrows[2 * q + k][:].bitcast(F32)
-                    for u in range(2):
-                        nc.tensor.transpose(xbank[q][:, 2 * k + u, :], words[:, 128 * u : 128 * (u + 1)], ident[:])
-
-            def xa_words(q):
-                xt["a", q] = pool.tile([128, 2, 128, 4], BF16, name="xat", tag="xat%d" % q, bufs=1, align_bytes=64)
-                nc.scalar.copy(out=word_view(xt["a", q][:]), in_=xbank[q][:].rearrange("p (k u) n -> p k n u", u=2))
-
-            def xa_quantise(q):
-                cols = slice(256 * q, 256 * (q + 1))
-                quantise(xcodes["a"][:, cols], xscale["a"][:, cols], xt["a", q][:].rearrange("p k n f -> p (k n f)"))
-
-            roots = {}
-
-            def root(b):
-                if b not in rec:
-                    rec[b] = pool.tile([128, M], F32, name="rec%d" % b, tag="big", bufs=2, align_bytes=64)
-                roots[b] = rec[b]
-                nc.scalar.activation(out=roots[b][:], in_=dr[b], func=ACT.Abs_reciprocal_sqrt)
-
-            def square(b):
-                nc.scalar.activation(out=rec[b][:], in_=roots[b][:], func=ACT.Square)
-
-            def square_beside(b, tag):
-                rec[b] = pool.tile([128, M], F32, name="rec%d" % b, tag=tag, bufs=1, align_bytes=64)
-                nc.gpsimd.tensor_tensor(out=rec[b][:], in0=roots[b][:], in1=roots[b][:], op=ALU.mult)
+            def square(q, h):
+                nc.scalar.activation(out=rec[q, h][:], in_=rec[q, h][:], func=ACT.Square)
 
             prod = {}
 
-            def product_half(b, h):
+            def product(b, h, bank):
                 own = slice(128 * b, 128 * (b + 1))
                 cols = slice(512 * h, 512 * (h + 1))
-                prod[b, h] = psum.tile([128, 512], F32, name="prod", tag="mm", bufs=5)
+                prod[b, h] = bank_tile(bank)[:].rearrange("p t n -> p (t n)")
                 nc.tensor.matmul_mx(
-                    out=prod[b, h][:],
+                    out=prod[b, h],
                     lhsT=xcodes["a"][:, own].bitcast(FP8X4),
                     lhsT_scale=xscale["a"][:, own],
                     rhs=xcodes["b"][:, cols].bitcast(FP8X4),
@@ -282,245 +232,245 @@ def tile_opposedspindirectringamplitudeupdate_x1_kernel(tc, ta, tb, ba, bb, ga, 
                     stop=True,
                 )
 
-            def product(b):
-                product_half(b, 1)
-                product_half(b, 0)
-
-            r, rb = {}, {}
-
             def divide(b, h):
-                cols = slice(512 * h, 512 * (h + 1))
-                if h == 0:
-                    tag, bufs = ([("grouped", 4)] * 4 + [("xbt0", 1), ("xbt1", 1), ("gate1", 1), ("scaled", 2)])[b]
-                    r[b] = pool.tile([128, M], F32, name="r", tag=tag, bufs=bufs, align_bytes=64)
-                nc.vector.scalar_tensor_tensor(
-                    out=r[b][:, cols], in0=prod[b, h][:], scalar=-1.0, in1=rec[b][:, cols], op0=ALU.mult, op1=ALU.mult
-                )
+                own = rec[b // 2, h][:, b % 2, :]
+                nc.vector.scalar_tensor_tensor(out=own, in0=prod[b, h], scalar=-1.0, in1=own, op0=ALU.mult, op1=ALU.mult)
 
-            def narrow(b, g0, g1, engine):
-                if g0 == 0:
-                    rb[b] = pool.tile([128, M], BF16, name="rb", bufs=4, align_bytes=64)
-                pairs = slice(128 * g0, 128 * g1)
-                out = rb[b][:].rearrange("p (u w e) -> p u w e", u=2, e=2)[:, :, pairs, :]
-                src = r[b][:].rearrange("p (w u e) -> p u w e", u=2, e=2)[:, :, pairs, :]
-                if engine == "g":
-                    nc.gpsimd.tensor_scalar(out=out, in0=src, scalar1=1.0, scalar2=-0.0, op0=ALU.mult, op1=ALU.add)
-                else:
-                    copy_on(engine)(out=out.rearrange("p u (a w) e -> p a u w e", w=4), in_=src.rearrange("p u (a w) e -> p a u w e", w=4))
+            rb, pbank, pt = {}, {}, {}
 
-            pb, pt = {}, {}
+            def narrow(q, h, engine, slot, k0=0, k1=2):
+                if (q, h) not in rb:
+                    rb[q, h] = keep_tile([128, 1024], BF16, "rb", slot)
+                pairs = slice(128 * k0, 128 * k1)
+                out = rb[q, h][:].rearrange("p (u w e) -> p u w e", u=2, e=2)[:, :, pairs, :]
+                src = rec[q, h][:].rearrange("p k (w u e) -> p u (k w) e", u=2, e=2)[:, :, pairs, :]
+                if engine != "g":
+                    out, src = out.rearrange("p u (a w) e -> p a u w e", w=4), src.rearrange("p u (a w) e -> p a u w e", w=4)
+                move(engine, out, src)
 
-            def p_turn(b, g0=0, g1=2):
-                bank = turn_bank()
-                for g in range(g0, g1):
-                    pb[b, g] = bank
-                    words = rb[b][:].bitcast(F32)
+            def p_turn(q, h, bank, k0=0, k1=2):
+                bank = bank_tile(bank)
+                words = rb[q, h][:].bitcast(F32)
+                for k in range(k0, k1):
+                    pbank[q, h, k] = bank
                     for u in range(2):
-                        first = 256 * u + 128 * g
-                        nc.tensor.transpose(bank[:, 2 * g + u, :], words[:, first : first + 128], ident[:])
+                        first = 256 * u + 128 * k
+                        nc.tensor.transpose(bank[:, 2 * k + u, :], words[:, first : first + 128], ident[:])
 
-            def p_words(b, g0=0, g1=2, engine="s"):
-                half = slice(128 * (b % 2), 128 * (b % 2) + 128)
-                if b % 2 == 0 and g0 == 0:
-                    pt[b // 2] = pool.tile([128, 2, 256, 4], BF16, name="pt", bufs=3, align_bytes=64)
+            def p_words(q, h, slot, k0=0, k1=2, engine="s"):
+                if (q // 2, h) not in pt:
+                    pt[q // 2, h] = keep_tile([128, 2048], BF16, "pt", slot)
+                words = pt[q // 2, h][:].bitcast(F32).rearrange("p (k n u) -> p k n u", k=4, u=2)
+                first = 2 * (q % 2)
                 copy_on(engine)(
-                    out=word_view(pt[b // 2][:])[:, g0:g1, half, :],
-                    in_=pb[b, g0][:, 2 * g0 : 2 * g1, :].rearrange("p (c u) n -> p c n u", u=2),
+                    out=words[:, first + k0 : first + k1, :, :], in_=pbank[q, h, k0][:, 2 * k0 : 2 * k1, :].rearrange("p (k u) n -> p k n u", u=2)
                 )
 
-            def p_quantise(b0, b1, g):
+            def p_quantise(h, b0, b1):
                 cols = slice(128 * b0, 128 * b1)
-                own = slice(128 * (b0 % 2), 128 * (b0 % 2) + 128 * (b1 - b0))
-                quantise(pcodes[:, g, cols], pscale[:, g, cols], pt[b0 // 2][:, g, own, :].rearrange("p n f -> p (n f)"))
+                quantise(pcodes[h][:, cols], pscale[:, h, cols], pt[b0 // 4, h][:, 512 * (b0 % 4) : 512 * (b0 % 4 + b1 - b0)])
 
-            def store_r(b, c0=0, c1=M):
-                nc.sync.dma_start(out=out_0[128 * b : 128 * (b + 1), c0:c1], in_=r[b][:, c0:c1])
+            def store_r(q, h, k0=0, k1=2):
+                rows = out_0[256 * q + 128 * k0 : 256 * q + 128 * k1, 512 * h : 512 * (h + 1)]
+                nc.sync.dma_start(out=rows.rearrange("(k p) m -> p k m", p=128), in_=rec[q, h][:, k0:k1, :])
 
-            def store_codes(b0, b1, g0=0, g1=2):
+            def store_codes(h, b0, b1):
                 cols = slice(128 * b0, 128 * b1)
-                nc.sync.dma_start(
-                    out=out_1[g0:g1, :, cols, :].rearrange("g p n f -> p g (n f)").bitcast(I32), in_=pcodes[:, g0:g1, cols].bitcast(I32)
-                )
+                nc.sync.dma_start(out=out_1[h, :, cols, :].rearrange("p n f -> p (n f)").bitcast(I32), in_=pcodes[h][:, cols].bitcast(I32))
 
-            def store_scales(b0, b1, queues):
-                cols = slice(128 * b0, 128 * b1)
+            def store_scales(queues):
                 for quad in range(4):
                     queues[quad % 2].dma_start(
-                        out=out_2[:, 4 * quad : 4 * quad + 4, cols].rearrange("g r n -> r g n").bitcast(I32),
-                        in_=pscale[32 * quad : 32 * quad + 4, :, cols].bitcast(I32),
+                        out=out_2[:, 4 * quad : 4 * quad + 4, :].rearrange("g r n -> r g n").bitcast(I32),
+                        in_=pscale[32 * quad : 32 * quad + 4, :, :].bitcast(I32),
                     )
 
-            load_gain("b", gb, nc.scalar)
-            load_rows4("b", 0, 2)
-            load_delta(0, 1)
-            load_rows4("b", 1)
-            load_tb(0, 0, 2)
-            load_ta(0, 1)
-            load_tb(1, 0, 2)
-            load_gain("a", ga, nc.sync)
-            load_rows4("a", 0)
+            load_gain("a", ga, nc.scalar)
+            load_rows4("a", 0, 2)
+            load_gain_row(0, ga, 1, nc.scalar)
+            load_delta(0, 0, 1, 0, 1)
             load_rows4("a", 1)
-            load_delta(1, 2)
-            load_ta(1, 2)
+            load_tb(0, 0, 1)
+            load_delta(0, 0, 1, 1, 2)
+            load_ta(0, 2)
             load_ta(2, 4)
             load_ta(4, 6)
-            load_delta(2, 4)
+            load_rows4("b", 0)
+            load_gain("b", gb, nc.sync)
+            load_rows4("b", 1)
+            load_tb(1, 0, 1)
             load_ta(6, 8)
-            load_rows1(0)
-            load_delta(4, 6)
-            load_rows1(1)
-            load_delta(6, 8)
+            load_delta(1, 0, 2)
+            load_tb(0, 1, 2)
+            load_delta(2, 0, 2)
+            load_tb(1, 1, 2)
+            load_delta(3, 0, 2)
+            load_delta(0, 1, 2)
 
-            root(0)
-            for c in range(2):
-                for h in range(2):
-                    bb_turn(c, h)
-                    bb_words(c, h)
-                if c == 0:
-                    square(0)
-            ta_turn(0)
-            factor_mult("b", 0)
-            factor_group("b", 0)
-            factor_mult("b", 1)
-            factor_quantise("b", 0)
-            factor_group("b", 1)
-            tb_group(0, 1, "s")
-            tb_group(0, 0, "v")
-            factor_quantise("b", 1)
-            tb_quantise(0, 0)
-            for b in range(4):
-                xb_mm(b, 0)
-            tb_group(1, 0, "v")
-            tb_group(1, 1, "s", "gate1")
-            tb_quantise(0, 1)
-            tb_quantise(1, 0)
-            for b in reversed(range(4)):
-                xb_mm(b, 1)
-            ta_words(0)
-            root(1)
-            factor_mult("a", 0)
-            factor_mult("a", 1)
-            tb_quantise(1, 1)
-            factor_group("a", 0, "g", "gate1")
-            factor_group("a", 1, "s")
-            xb_both(4)
-            for b in range(5):
-                xb_add(b)
-            ta_turn(1)
-            ta_turn(2)
-            xb_both(5)
-            xb_both(6)
-            ta_turn(3)
-            ta_words(1)
-            ta_turn(4)
-            xb_both(7)
-            ta_words(2)
-            ta_words(3)
-            ta_turn(5)
-            ta_turn(6)
-            root(2)
-            ta_words(4)
-            root(3)
-            ta_words(5)
-            xb_quantise(0)
+            root(0, 0, 0, 1)
+            factor_turn("a", 0, 0, 0)
+            gain_turn(7)
+            factor_turn("a", 0, 1, 1)
+            factor_turn("a", 1, 0, 2)
+            factor_turn("a", 1, 1, 3)
+            factor_words("a", 0, 0)
+            factor_words("a", 0, 1)
+            factor_words("a", 1, 0)
+            root(0, 0, 1, 2)
+            factor_mult("a", 0, "s0")
+            factor_group("a", 0, "v", "g0")
+            tb_group(0, 0, "g", "g2")
+            factor_fused("a", 1, 0, "g1")
+            factor_words("a", 1, 1, "v")
+            for b in range(6):
+                ta_turn(b, (4, 5, 6, 0, 1, 7)[b])
+            square(0, 0)
+            for b in range(6):
+                ta_words(b, "t%d" % (b // 2))
             factor_quantise("a", 0)
-            ta_quantise(0)
             factor_quantise("a", 1)
+            ta_quantise(0)
+            tb_quantise(0, 0)
+            factor_mult("b", 0, "s0")
+            factor_mult("b", 1, "s1")
             ta_quantise(1)
-            square_beside(1, "gate2")
-            xa_mm(0)
-            xa_mm(1)
-            ta_words(6)
-            for b in range(5, 8):
-                xb_add(b)
-            xa_mm(2)
-            xa_mm(3)
-            square(3)
-            xa_add(0)
-            xa_add(1)
-            xa_turn(0)
-            ta_turn(7)
+            factor_group("b", 0, "s", "g0")
+            factor_group("b", 1, "s", "g1")
             ta_quantise(2)
-            xa_mm(4)
-            xa_mm(5)
-            xa_words(0)
-            root(4)
+            tb_group(1, 0, "g", "t1")
+            for b in range(5):
+                x_both("a", b, 2 + b)
+            ta_turn(6, 1)
+            ta_turn(7, 7)
+            x_both("a", 5, 0)
+            ta_words(6, "t0")
             ta_words(7)
-            xb_quantise(1)
-            xa_add(2)
-            xa_quantise(0)
-            square_beside(2, "xat0")
-            product(0)
-            xa_add(3)
-            xa_turn(1)
-            square(4)
-            xa_words(1)
-            xa_add(4)
-            xa_add(5)
-            xa_turn(2)
-            root(5)
-            xa_words(2)
-            last = BLOCKS - 1
-            rest = [(root, 6), (square, 5), (root, 7), (square, 6), (square, 7)]
-            for i in range(BLOCKS):
-                if i in (2, 4):
-                    p_turn(i - 2)
-                if i < last:
-                    product(i + 1)
-                if i == 3:
-                    xa_turn(3)
-                if i == 2:
-                    p_turn(1)
-                if i >= 5:
-                    p_turn(i - 2)
-                divide(i, 0)
-                if i == 6:
-                    narrow(i, 0, 1, "g")
-                divide(i, 1)
-                store_r(i)
-                if i == 3:
-                    xa_words(3)
-                for step, b in rest[i : i + 1]:
-                    step(b)
-                if i == 6:
-                    narrow(i, 1, 2, "s")
-                if i >= 2 and i != 3:
-                    p_words(i - 2)
-                if i == 2:
-                    p_words(1)
-                if i == 0:
-                    ta_quantise(3)
-                if i == 4:
-                    narrow(3, 1, 2, "v")
-                if i == 4:
-                    p_quantise(0, 2, 0)
-                if i in (0, 2, 4):
-                    xa_quantise(i // 2 + 1)
-                if i < 2:
-                    xa_mm(i + 6)
-                if i == 4:
-                    p_quantise(0, 2, 1)
-                    store_codes(0, 2)
-                if i < 6:
-                    narrow(i, 0, 1 if i in (3, 5) else 2, "g")
-                if i == 5:
-                    narrow(i, 1, 2, "s")
-                if i in (1, 2):
-                    xa_add(i + 5)
-            narrow(last, 0, 1, "v")
-            narrow(last, 1, 2, "v")
-            for q in (1, 2):
-                p_quantise(2 * q, 2 * q + 2, 0)
-                p_quantise(2 * q, 2 * q + 2, 1)
-                store_codes(2 * q, 2 * q + 2)
-            p_turn(6)
-            p_words(6)
-            for g in range(2):
-                p_turn(last, g, g + 1)
-                p_words(last, g, g + 1)
-            p_quantise(6, 7, 0)
-            p_quantise(6, 7, 1)
-            for g in range(2):
-                p_quantise(7, 8, g)
-                store_codes(6, 8, g, g + 1)
-            store_scales(0, 8, (nc.scalar, nc.sync))
+            for b in range(5):
+                x_add("a", b)
+            factor_turn("b", 0, 0, 2)
+            factor_turn("b", 0, 1, 3)
+            factor_words("b", 0, 0)
+            factor_words("b", 0, 1)
+            factor_quantise("b", 0)
+            tb_quantise(1, 0)
+            factor_quantise("b", 1)
+            x_quantise("a", 0)
+            ta_quantise(3)
+            tb_group(0, 1, "g", "xta0")
+            tb_group(1, 1, "g", "g0", 0, 256)
+            for b in range(3):
+                x_both("b", b, 4 + b)
+            x_both("a", 6, 1)
+            x_both("a", 7, 7)
+            x_both("b", 3, 2)
+            root(1, 0)
+            root(2, 0)
+            square(1, 0)
+            root(3, 0)
+            x_add("a", 5)
+            x_add("b", 0)
+            x_add("b", 1)
+            x_add("b", 2)
+            x_add("a", 6)
+            x_add("a", 7)
+            x_add("b", 3)
+            factor_turn("b", 1, 0, 3)
+            factor_turn("b", 1, 1, 0)
+            square(2, 0)
+            factor_words("b", 1, 0)
+            factor_words("b", 1, 1)
+            x_quantise("a", 1)
+            x_quantise("b", 0)
+            tb_quantise(0, 1)
+            tb_quantise(1, 1, 0, 256)
+            tb_group(1, 1, "g", "xta0", 256, 512)
+            for b in range(4):
+                product(b, 0, (4, 5, 6, 1)[b])
+            product(5, 0, 7)
+            product(4, 0, 2)
+            x_both("b", 5, 3)
+            x_both("b", 4, 0)
+            root(0, 1)
+            square(3, 0)
+            root(1, 1)
+            square(0, 1)
+            divide(0, 0)
+            divide(1, 0)
+            store_r(0, 0)
+            divide(2, 0)
+            tb_quantise(1, 1, 256, 512)
+            narrow(0, 0, "g", "xta0")
+            x_both("b", 7, 4)
+            x_both("b", 6, 5)
+            divide(3, 0)
+            store_r(1, 0)
+            narrow(1, 0, "g", "s1")
+            divide(4, 0)
+            divide(5, 0)
+            store_r(2, 0)
+            narrow(2, 0, "g", "t0")
+            p_turn(0, 0, 6)
+            for b in range(4, 8):
+                x_add("b", b)
+            product(7, 0, 0)
+            product(6, 0, 3)
+            root(2, 1)
+            p_words(0, 0, "g0")
+            p_turn(1, 0, 1)
+            square(1, 1)
+            p_words(1, 0, "g0")
+            divide(6, 0)
+            x_quantise("b", 1)
+            divide(7, 0)
+            p_quantise(0, 0, 4)
+            store_r(3, 0)
+            store_codes(0, 0, 4)
+            narrow(3, 0, "g", "t2")
+            p_turn(2, 0, 2)
+            for b in range(4):
+                product(b, 1, (7, 4, 5, 6)[b])
+            product(5, 1, 1)
+            product(4, 1, 3)
+            root(3, 1)
+            square(2, 1)
+            p_words(2, 0, "g2")
+            square(3, 1)
+            divide(0, 1)
+            divide(1, 1)
+            store_r(0, 1)
+            narrow(0, 1, "g", "xtb0")
+            p_turn(3, 0, 0)
+            p_words(3, 0, "g2")
+            product(7, 1, 7)
+            product(6, 1, 4)
+            divide(2, 1)
+            divide(3, 1)
+            store_r(1, 1)
+            narrow(1, 1, "g", "xtb1")
+            p_turn(0, 1, 2)
+            p_words(0, 1, "xta0")
+            divide(4, 1)
+            divide(5, 1)
+            store_r(2, 1)
+            narrow(2, 1, "g", "s0", 0, 1)
+            p_turn(1, 1, 5)
+            divide(6, 1)
+            store_r(3, 1, 0, 1)
+            narrow(3, 1, "s", "s1", 0, 1)
+            p_words(1, 1, "xta0")
+            divide(7, 1)
+            store_r(3, 1, 1, 2)
+            narrow(2, 1, "v", "s0", 1, 2)
+            narrow(3, 1, "v", "s1", 1, 2)
+            p_quantise(0, 4, 8)
+            store_codes(0, 4, 8)
+            p_turn(2, 1, 6)
+            p_words(2, 1, "t1")
+            p_turn(3, 1, 0)
+            p_words(3, 1, "t1")
+            p_quantise(1, 0, 4)
+            store_codes(1, 0, 4)
+            p_quantise(1, 4, 6)
+            p_quantise(1, 6, 8)
+            store_codes(1, 4, 8)
+            store_scales((nc.scalar, nc.sync))

@@ -43,7 +43,7 @@ def tile_opposedspindirectringamplitudeupdate_x1_kernel(tc, ta, tb, ba, bb, ga, 
                 tbscale[c, h] = keep_tile([128, 512], U8, "tbscale%d%d" % (c, h))
         tacodes = [keep_tile([128, 2, 256], U32, "tacodes%d" % q) for q in range(4)]
         tascale = [keep_tile([128, 2, 256], U8, "tascale%d" % q) for q in range(4)]
-        rec = {(q, h): keep_tile([128, 2, 512], F32, "rec%d%d" % (q, h)) for q in range(4) for h in range(2)}
+        rec = {(c, h): keep_tile([128, 4, 512], F32, "rec%d%d" % (c, h)) for c in range(2) for h in range(2)}
         pcodes = [keep_tile([128, N], U32, "pcodes%d" % h) for h in range(2)]
         pscale = keep_tile([128, 2, N], U8, "pscale")
         tar, tbr, dr = {}, {}, {}
@@ -75,12 +75,10 @@ def tile_opposedspindirectringamplitudeupdate_x1_kernel(tc, ta, tb, ba, bb, ga, 
                 for h in range(h0, h1):
                     tbr[c, h] = rows[:, :, 512 * (h - h0) : 512 * (h - h0 + 1)]
 
-            def load_delta(q, h0, h1, k0=0, k1=2, queue=nc.sync):
-                rows = keep_tile([128, k1 - k0, 512 * (h1 - h0)], BF16, "dr%d%d%d" % (q, h0, k0))
-                src = delta[256 * q + 128 * k0 : 256 * q + 128 * k1, 512 * h0 : 512 * h1]
-                queue.dma_start(out=rows[:], in_=src.rearrange("(k p) m -> p k m", p=128))
-                for h in range(h0, h1):
-                    dr[q, h, k0, k1] = rows[:, :, 512 * (h - h0) : 512 * (h - h0 + 1)]
+            def load_delta(h, b0, b1, w0=0, w1=512):
+                dr[h, b0, w0] = keep_tile([128, b1 - b0, w1 - w0], BF16, "dr%d%d%d" % (h, b0, w0))
+                src = delta[128 * b0 : 128 * b1, 512 * h + w0 : 512 * h + w1]
+                nc.sync.dma_start(out=dr[h, b0, w0][:], in_=src.rearrange("(k p) m -> p k m", p=128))
 
             def load_ta(b0, b1):
                 rows = keep_tile([128, b1 - b0, N], BF16, "tar%d" % b0)
@@ -112,11 +110,12 @@ def tile_opposedspindirectringamplitudeupdate_x1_kernel(tc, ta, tb, ba, bb, ga, 
                         out=scaled[s, c][:, P * j : P * (j + 1)], in0=rows4[s, c, j], scalar1=gain[s][:, c, j : j + 1], scalar2=None, op0=ALU.mult
                     )
 
-            def factor_group(s, c, engine, slot):
-                grouped[s, c] = keep_tile([128, 4 * P], BF16, "grouped", slot)
+            def factor_group(s, c, engine, slot, m0=0, m1=64):
+                if (s, c) not in grouped:
+                    grouped[s, c] = keep_tile([128, 4 * P], BF16, "grouped", slot)
                 copy_on(engine)(
-                    out=grouped[s, c][:].rearrange("p (t m e j) -> p m t e j", t=4, e=2, j=4),
-                    in_=scaled[s, c][:].rearrange("p (j m e t) -> p m t e j", t=4, e=2, j=4),
+                    out=grouped[s, c][:].rearrange("p (t m e j) -> p m t e j", t=4, e=2, j=4)[:, m0:m1],
+                    in_=scaled[s, c][:].rearrange("p (j m e t) -> p m t e j", t=4, e=2, j=4)[:, m0:m1],
                 )
 
             gbank = {}
@@ -210,11 +209,14 @@ def tile_opposedspindirectringamplitudeupdate_x1_kernel(tc, ta, tb, ba, bb, ga, 
                 cols = slice(512 * h, 512 * (h + 1))
                 quantise(xcodes[s][:, cols], xscale[s][:, cols], xt[s, h][:])
 
-            def root(q, h, k0=0, k1=2):
-                nc.scalar.activation(out=rec[q, h][:, k0:k1, :], in_=dr[q, h, k0, k1], func=ACT.Abs_reciprocal_sqrt)
+            def rec_rows(h, b0, b1):
+                return rec[b0 // 4, h][:, b0 % 4 : b0 % 4 + b1 - b0, :]
 
-            def square(q, h):
-                nc.scalar.activation(out=rec[q, h][:], in_=rec[q, h][:], func=ACT.Square)
+            def root(h, b0, b1, w0=0, w1=512):
+                nc.scalar.activation(out=rec_rows(h, b0, b1)[:, :, w0:w1], in_=dr[h, b0, w0][:], func=ACT.Abs_reciprocal_sqrt)
+
+            def square(h, b0, b1):
+                nc.scalar.activation(out=rec_rows(h, b0, b1), in_=rec_rows(h, b0, b1), func=ACT.Square)
 
             prod = {}
 
@@ -233,7 +235,7 @@ def tile_opposedspindirectringamplitudeupdate_x1_kernel(tc, ta, tb, ba, bb, ga, 
                 )
 
             def divide(b, h):
-                own = rec[b // 2, h][:, b % 2, :]
+                own = rec[b // 4, h][:, b % 4, :]
                 nc.vector.scalar_tensor_tensor(out=own, in0=prod[b, h], scalar=-1.0, in1=own, op0=ALU.mult, op1=ALU.mult)
 
             rb, pbank, pt = {}, {}, {}
@@ -243,7 +245,7 @@ def tile_opposedspindirectringamplitudeupdate_x1_kernel(tc, ta, tb, ba, bb, ga, 
                     rb[q, h] = keep_tile([128, 1024], BF16, "rb", slot)
                 pairs = slice(128 * k0, 128 * k1)
                 out = rb[q, h][:].rearrange("p (u w e) -> p u w e", u=2, e=2)[:, :, pairs, :]
-                src = rec[q, h][:].rearrange("p k (w u e) -> p u (k w) e", u=2, e=2)[:, :, pairs, :]
+                src = rec_rows(h, 2 * q, 2 * q + 2).rearrange("p k (w u e) -> p u (k w) e", u=2, e=2)[:, :, pairs, :]
                 if engine != "g":
                     out, src = out.rearrange("p u (a w) e -> p a u w e", w=4), src.rearrange("p u (a w) e -> p a u w e", w=4)
                 move(engine, out, src)
@@ -272,7 +274,7 @@ def tile_opposedspindirectringamplitudeupdate_x1_kernel(tc, ta, tb, ba, bb, ga, 
 
             def store_r(q, h, k0=0, k1=2):
                 rows = out_0[256 * q + 128 * k0 : 256 * q + 128 * k1, 512 * h : 512 * (h + 1)]
-                nc.sync.dma_start(out=rows.rearrange("(k p) m -> p k m", p=128), in_=rec[q, h][:, k0:k1, :])
+                nc.sync.dma_start(out=rows.rearrange("(k p) m -> p k m", p=128), in_=rec_rows(h, 2 * q + k0, 2 * q + k1))
 
             def store_codes(h, b0, b1):
                 cols = slice(128 * b0, 128 * b1)
@@ -288,10 +290,10 @@ def tile_opposedspindirectringamplitudeupdate_x1_kernel(tc, ta, tb, ba, bb, ga, 
             load_gain("a", ga, nc.scalar)
             load_rows4("a", 0, 2)
             load_gain_row(0, ga, 1, nc.scalar)
-            load_delta(0, 0, 1, 0, 1)
+            load_delta(0, 0, 1)
             load_rows4("a", 1)
             load_tb(0, 0, 1)
-            load_delta(0, 0, 1, 1, 2)
+            load_delta(0, 1, 2)
             load_ta(0, 2)
             load_ta(2, 4)
             load_ta(4, 6)
@@ -300,14 +302,14 @@ def tile_opposedspindirectringamplitudeupdate_x1_kernel(tc, ta, tb, ba, bb, ga, 
             load_rows4("b", 1)
             load_tb(1, 0, 1)
             load_ta(6, 8)
-            load_delta(1, 0, 2)
+            load_delta(0, 2, 4)
             load_tb(0, 1, 2)
-            load_delta(2, 0, 2)
+            load_delta(0, 4, 8)
             load_tb(1, 1, 2)
-            load_delta(3, 0, 2)
-            load_delta(0, 1, 2)
+            load_delta(1, 0, 4)
+            load_delta(1, 4, 8)
 
-            root(0, 0, 0, 1)
+            root(0, 0, 1)
             factor_turn("a", 0, 0, 0)
             gain_turn(7)
             factor_turn("a", 0, 1, 1)
@@ -316,7 +318,7 @@ def tile_opposedspindirectringamplitudeupdate_x1_kernel(tc, ta, tb, ba, bb, ga, 
             factor_words("a", 0, 0)
             factor_words("a", 0, 1)
             factor_words("a", 1, 0)
-            root(0, 0, 1, 2)
+            root(0, 1, 2)
             factor_mult("a", 0, "s0")
             factor_group("a", 0, "v", "g0")
             tb_group(0, 0, "g", "g2")
@@ -324,13 +326,13 @@ def tile_opposedspindirectringamplitudeupdate_x1_kernel(tc, ta, tb, ba, bb, ga, 
             factor_words("a", 1, 1, "v")
             for b in range(6):
                 ta_turn(b, (4, 5, 6, 0, 1, 7)[b])
-            square(0, 0)
+            square(0, 0, 2)
             for b in range(6):
                 ta_words(b, "t%d" % (b // 2))
-            factor_quantise("a", 0)
             factor_quantise("a", 1)
-            ta_quantise(0)
+            factor_quantise("a", 0)
             tb_quantise(0, 0)
+            ta_quantise(0)
             factor_mult("b", 0, "s0")
             factor_mult("b", 1, "s1")
             ta_quantise(1)
@@ -363,96 +365,90 @@ def tile_opposedspindirectringamplitudeupdate_x1_kernel(tc, ta, tb, ba, bb, ga, 
             x_both("a", 6, 1)
             x_both("a", 7, 7)
             x_both("b", 3, 2)
-            root(1, 0)
-            root(2, 0)
-            square(1, 0)
-            root(3, 0)
+            root(0, 2, 4)
+            root(0, 4, 8)
+            square(0, 2, 4)
             x_add("a", 5)
-            x_add("b", 0)
-            x_add("b", 1)
-            x_add("b", 2)
+            for b in range(3):
+                x_add("b", b)
             x_add("a", 6)
             x_add("a", 7)
             x_add("b", 3)
             factor_turn("b", 1, 0, 3)
             factor_turn("b", 1, 1, 0)
-            square(2, 0)
             factor_words("b", 1, 0)
             factor_words("b", 1, 1)
-            x_quantise("a", 1)
+            square(0, 4, 8)
             x_quantise("b", 0)
-            tb_quantise(0, 1)
+            x_quantise("a", 1)
             tb_quantise(1, 1, 0, 256)
-            tb_group(1, 1, "g", "xta0", 256, 512)
-            for b in range(4):
+            tb_quantise(0, 1)
+            tb_group(1, 1, "g", "g0", 256, 512)
+            for b in (0, 1, 3, 2):
                 product(b, 0, (4, 5, 6, 1)[b])
             product(5, 0, 7)
             product(4, 0, 2)
             x_both("b", 5, 3)
             x_both("b", 4, 0)
-            root(0, 1)
-            square(3, 0)
-            root(1, 1)
-            square(0, 1)
+            root(1, 0, 4)
+            root(1, 4, 8)
             divide(0, 0)
             divide(1, 0)
             store_r(0, 0)
             divide(2, 0)
             tb_quantise(1, 1, 256, 512)
-            narrow(0, 0, "g", "xta0")
+            narrow(0, 0, "g", "g0")
             x_both("b", 7, 4)
             x_both("b", 6, 5)
             divide(3, 0)
             store_r(1, 0)
             narrow(1, 0, "g", "s1")
             divide(4, 0)
-            divide(5, 0)
-            store_r(2, 0)
-            narrow(2, 0, "g", "t0")
             p_turn(0, 0, 6)
             for b in range(4, 8):
                 x_add("b", b)
             product(7, 0, 0)
             product(6, 0, 3)
-            root(2, 1)
-            p_words(0, 0, "g0")
+            p_words(0, 0, "g1")
+            square(1, 0, 2)
             p_turn(1, 0, 1)
-            square(1, 1)
-            p_words(1, 0, "g0")
-            divide(6, 0)
+            p_words(1, 0, "g1")
+            square(1, 2, 4)
+            square(1, 4, 6)
+            divide(5, 0)
             x_quantise("b", 1)
+            store_r(2, 0)
+            narrow(2, 0, "g", "t0")
+            divide(6, 0)
             divide(7, 0)
-            p_quantise(0, 0, 4)
             store_r(3, 0)
-            store_codes(0, 0, 4)
             narrow(3, 0, "g", "t2")
-            p_turn(2, 0, 2)
-            for b in range(4):
-                product(b, 1, (7, 4, 5, 6)[b])
+            for b in (0, 1, 3, 2):
+                product(b, 1, (2, 4, 5, 6)[b])
+            p_turn(2, 0, 7)
             product(5, 1, 1)
             product(4, 1, 3)
-            root(3, 1)
-            square(2, 1)
             p_words(2, 0, "g2")
-            square(3, 1)
             divide(0, 1)
             divide(1, 1)
             store_r(0, 1)
             narrow(0, 1, "g", "xtb0")
             p_turn(3, 0, 0)
+            square(1, 6, 8)
             p_words(3, 0, "g2")
-            product(7, 1, 7)
+            product(7, 1, 2)
             product(6, 1, 4)
             divide(2, 1)
             divide(3, 1)
             store_r(1, 1)
             narrow(1, 1, "g", "xtb1")
-            p_turn(0, 1, 2)
+            p_turn(0, 1, 7)
             p_words(0, 1, "xta0")
             divide(4, 1)
             divide(5, 1)
             store_r(2, 1)
             narrow(2, 1, "g", "s0", 0, 1)
+            narrow(2, 1, "s", "s0", 1, 2)
             p_turn(1, 1, 5)
             divide(6, 1)
             store_r(3, 1, 0, 1)
@@ -460,8 +456,9 @@ def tile_opposedspindirectringamplitudeupdate_x1_kernel(tc, ta, tb, ba, bb, ga, 
             p_words(1, 1, "xta0")
             divide(7, 1)
             store_r(3, 1, 1, 2)
-            narrow(2, 1, "v", "s0", 1, 2)
             narrow(3, 1, "v", "s1", 1, 2)
+            p_quantise(0, 0, 4)
+            store_codes(0, 0, 4)
             p_quantise(0, 4, 8)
             store_codes(0, 4, 8)
             p_turn(2, 1, 6)
@@ -471,6 +468,7 @@ def tile_opposedspindirectringamplitudeupdate_x1_kernel(tc, ta, tb, ba, bb, ga, 
             p_quantise(1, 0, 4)
             store_codes(1, 0, 4)
             p_quantise(1, 4, 6)
+            store_codes(1, 4, 6)
             p_quantise(1, 6, 8)
-            store_codes(1, 4, 8)
+            store_codes(1, 6, 8)
             store_scales((nc.scalar, nc.sync))

@@ -14,6 +14,13 @@ ACT = mybir.ActivationFunctionType
 
 N, M, P = 1024, 1024, 512
 FLOPS = 2 * N * N * P + 2 * M * M * P + 2 * N * M * P
+PARTS = 128
+PLACES = 4
+PASS = PARTS * PLACES
+PAIR = 2 * PARTS
+QUADRANT = 32
+LEFT, RIGHT = 0, 1
+VECTOR, SCALAR, GPSIMD = "v", "s", "g"
 
 
 def tile_opposedspindirectringamplitudeupdate_x1_kernel(tc, ta, tb, ba, bb, ga, gb, delta, out_0, out_1, out_2):
@@ -22,81 +29,82 @@ def tile_opposedspindirectringamplitudeupdate_x1_kernel(tc, ta, tb, ba, bb, ga, 
         keep = ctx.enter_context(tc.tile_pool(name="keep", bufs=1))
         psum = ctx.enter_context(tc.psum_pool(name="psum", bufs=1))
 
-        def keep_tile(shape, dtype, name, tag=None):
-            return keep.tile(shape, dtype, name=name, tag=tag or name, align_bytes=64)
+        def keep_tile(shape, dtype, name, slot=None):
+            return keep.tile(shape, dtype, name=name, tag=slot or name, align_bytes=64)
 
-        ident = keep_tile([128, 128], F32, "ident")
+        def bank_tile(bank):
+            return psum.tile([PARTS, PLACES, PARTS], F32, name="bank", tag="bank%d" % bank)
+
+        def span(i, width):
+            return slice(width * i, width * (i + 1))
+
+        ident = keep_tile([PARTS, PARTS], F32, "ident")
         factor = {"a": ba, "b": bb}
+        gain_passes = {"a": 1, "b": 2}
         gain, rows4, gcodes, gscale, xt, xcodes, xscale = {}, {}, {}, {}, {}, {}, {}
         for s in ("a", "b"):
-            gain[s] = keep_tile([128, 2, 4], BF16, "gain" + s)
-            xcodes[s] = keep_tile([128, N], U32, "xcodes" + s)
-            xscale[s] = keep_tile([128, N], U8, "xscale" + s)
+            gain[s] = keep_tile([PARTS, gain_passes[s], PLACES], BF16, "gain" + s)
+            xcodes[s] = keep_tile([PARTS, N], U32, "xcodes" + s)
+            xscale[s] = keep_tile([PARTS, N], U8, "xscale" + s)
             for c in range(2):
-                gcodes[s, c] = keep_tile([128, P], U32, "gcodes%s%d" % (s, c))
-                gscale[s, c] = keep_tile([128, P], U8, "gscale%s%d" % (s, c))
-                xt[s, c] = keep_tile([128, 512 * 4], BF16, "xt%s%d" % (s, c))
+                gcodes[s, c] = keep_tile([PARTS, P], U32, "gcodes%s%d" % (s, c))
+                gscale[s, c] = keep_tile([PARTS, P], U8, "gscale%s%d" % (s, c))
+                xt[s, c] = keep_tile([PARTS, PASS * PLACES], BF16, "xt%s%d" % (s, c))
         tbcodes, tbscale = {}, {}
         for c in range(2):
             for h in range(2):
-                tbcodes[c, h] = keep_tile([128, 512], U32, "tbcodes%d%d" % (c, h))
-                tbscale[c, h] = keep_tile([128, 512], U8, "tbscale%d%d" % (c, h))
-        tacodes = [keep_tile([128, 2, 256], U32, "tacodes%d" % q) for q in range(4)]
-        tascale = [keep_tile([128, 2, 256], U8, "tascale%d" % q) for q in range(4)]
-        rec = {(c, h): keep_tile([128, 4, 512], F32, "rec%d%d" % (c, h)) for c in range(2) for h in range(2)}
-        pcodes = [keep_tile([128, N], U32, "pcodes%d" % h) for h in range(2)]
-        pscale = keep_tile([128, 2, N], U8, "pscale")
-        tar, tbr, dr = {}, {}, {}
+                tbcodes[c, h] = keep_tile([PARTS, PASS], U32, "tbcodes%d%d" % (c, h))
+                tbscale[c, h] = keep_tile([PARTS, PASS], U8, "tbscale%d%d" % (c, h))
+        tacodes = [keep_tile([PARTS, 2, PAIR], U32, "tacodes%d" % q) for q in range(4)]
+        tascale = [keep_tile([PARTS, 2, PAIR], U8, "tascale%d" % q) for q in range(4)]
+        rec = {(four, h): keep_tile([PARTS, 4, PASS], F32, "rec%d%d" % (four, h)) for four in range(2) for h in range(2)}
+        pcodes = [keep_tile([PARTS, N], U32, "pcodes%d" % h) for h in range(2)]
+        pscale = keep_tile([PARTS, 2, N], U8, "pscale")
+        ta_rows, tb_rows, delta_rows = {}, {}, {}
 
-        grow = keep_tile([128, 512], BF16, "grow")
-        nc.gpsimd.memset(grow[:].bitcast(I32), 0)
+        gain_row = keep_tile([PARTS, PASS], BF16, "grow")
+        nc.gpsimd.memset(gain_row[:].bitcast(I32), 0)
         make_identity(nc, ident[:])
         with tc.manual_schedule():
 
             def load_gain(s, g, queue):
-                queue.dma_start(out=gain[s][:], in_=g.rearrange("(c p j) -> p c j", p=128, j=4))
+                queue.dma_start(out=gain[s][:], in_=g[0 : PASS * gain_passes[s]].rearrange("(c p j) -> p c j", p=PARTS, j=PLACES))
 
-            def load_gain_row(row, g, c, queue):
-                queue.dma_start(out=grow[row : row + 1, :], in_=g[512 * c : 512 * (c + 1)].rearrange("(r w) -> r w", r=1))
+            def load_gain_row():
+                nc.scalar.dma_start(out=gain_row[0:1, :], in_=ga[span(1, PASS)].rearrange("(r w) -> r w", r=1))
 
             def load_rows4(s, c, pieces=1):
-                src = factor[s][512 * c : 512 * (c + 1), :].rearrange("(p j) w -> p j w", j=4)
-                step = 4 // pieces
-                for j0 in range(0, 4, step):
-                    piece = keep_tile([128, step, P], BF16, "rows4%s%d%d" % (s, c, j0))
+                src = factor[s][span(c, PASS), :].rearrange("(p j) w -> p j w", j=PLACES)
+                step = PLACES // pieces
+                for j0 in range(0, PLACES, step):
+                    piece = keep_tile([PARTS, step, P], BF16, "rows4%s%d%d" % (s, c, j0))
                     nc.sync.dma_start(out=piece[:], in_=src[:, j0 : j0 + step, :])
                     rows4[s, c] = piece
                     for j in range(step):
                         rows4[s, c, j0 + j] = piece[:, j, :]
 
-            def load_tb(c, h0, h1):
-                rows = keep_tile([128, 4, 512 * (h1 - h0)], BF16, "tbr%d%d" % (c, h0))
-                nc.sync.dma_start(out=rows[:], in_=tb[512 * c : 512 * (c + 1), 512 * h0 : 512 * h1].rearrange("(p j) w -> p j w", j=4))
-                for h in range(h0, h1):
-                    tbr[c, h] = rows[:, :, 512 * (h - h0) : 512 * (h - h0 + 1)]
+            def load_tb(c, h):
+                tb_rows[c, h] = keep_tile([PARTS, PLACES, PASS], BF16, "tbr%d%d" % (c, h))
+                nc.sync.dma_start(out=tb_rows[c, h][:], in_=tb[span(c, PASS), span(h, PASS)].rearrange("(p j) w -> p j w", j=PLACES))
 
-            def load_delta(h, b0, b1, w0=0, w1=512):
-                dr[h, b0, w0] = keep_tile([128, b1 - b0, w1 - w0], BF16, "dr%d%d%d" % (h, b0, w0))
-                src = delta[128 * b0 : 128 * b1, 512 * h + w0 : 512 * h + w1]
-                nc.sync.dma_start(out=dr[h, b0, w0][:], in_=src.rearrange("(k p) m -> p k m", p=128))
+            def load_delta(h, b0, b1):
+                delta_rows[h, b0] = keep_tile([PARTS, b1 - b0, PASS], BF16, "dr%d%d" % (h, b0))
+                src = delta[PARTS * b0 : PARTS * b1, span(h, PASS)]
+                nc.sync.dma_start(out=delta_rows[h, b0][:], in_=src.rearrange("(k p) m -> p k m", p=PARTS))
 
-            def load_ta(b0, b1):
-                rows = keep_tile([128, b1 - b0, N], BF16, "tar%d" % b0)
-                nc.sync.dma_start(out=rows[:], in_=ta[128 * b0 : 128 * b1, :].rearrange("(b p) k -> p b k", p=128))
-                for b in range(b0, b1):
-                    tar[b] = rows[:, b - b0, :]
-
-            def bank_tile(bank):
-                return psum.tile([128, 4, 128], F32, name="bank", tag="bank%d" % bank)
-
-            def copy_on(engine):
-                return nc.vector.tensor_copy if engine == "v" else nc.scalar.copy
+            def load_ta(q):
+                rows = keep_tile([PARTS, 2, N], BF16, "tar%d" % q)
+                nc.sync.dma_start(out=rows[:], in_=ta[span(q, PAIR), :].rearrange("(k p) w -> p k w", p=PARTS))
+                for k in range(2):
+                    ta_rows[2 * q + k] = rows[:, k, :]
 
             def move(engine, out, src):
-                if engine == "g":
+                if engine == GPSIMD:
                     nc.gpsimd.tensor_scalar(out=out, in0=src, scalar1=1.0, scalar2=-0.0, op0=ALU.mult, op1=ALU.add)
+                elif engine == VECTOR:
+                    nc.vector.tensor_copy(out=out, in_=src)
                 else:
-                    copy_on(engine)(out=out, in_=src)
+                    nc.scalar.copy(out=out, in_=src)
 
             def quantise(codes, scale, values):
                 nc.vector.quantize_mx(out=codes.bitcast(FP8X4), scales=scale, in_=values)
@@ -104,116 +112,104 @@ def tile_opposedspindirectringamplitudeupdate_x1_kernel(tc, ta, tb, ba, bb, ga, 
             scaled, grouped = {}, {}
 
             def factor_mult(s, c, slot):
-                scaled[s, c] = keep_tile([128, 4 * P], BF16, "scaled", slot)
-                for j in range(4):
-                    nc.vector.tensor_scalar(
-                        out=scaled[s, c][:, P * j : P * (j + 1)], in0=rows4[s, c, j], scalar1=gain[s][:, c, j : j + 1], scalar2=None, op0=ALU.mult
-                    )
+                scaled[s, c] = keep_tile([PARTS, PLACES * P], BF16, "scaled", slot)
+                for j in range(PLACES):
+                    nc.vector.tensor_scalar(out=scaled[s, c][:, span(j, P)], in0=rows4[s, c, j], scalar1=gain[s][:, c, j : j + 1], scalar2=None, op0=ALU.mult)
 
-            def factor_group(s, c, engine, slot, m0=0, m1=64):
-                if (s, c) not in grouped:
-                    grouped[s, c] = keep_tile([128, 4 * P], BF16, "grouped", slot)
-                copy_on(engine)(
-                    out=grouped[s, c][:].rearrange("p (t m e j) -> p m t e j", t=4, e=2, j=4)[:, m0:m1],
-                    in_=scaled[s, c][:].rearrange("p (j m e t) -> p m t e j", t=4, e=2, j=4)[:, m0:m1],
+            def factor_group(s, c, engine, slot):
+                grouped[s, c] = keep_tile([PARTS, PLACES * P], BF16, "grouped", slot)
+                move(
+                    engine,
+                    grouped[s, c][:].rearrange("p (t m e j) -> p m t e j", t=PLACES, e=2, j=PLACES),
+                    scaled[s, c][:].rearrange("p (j m e t) -> p m t e j", t=PLACES, e=2, j=PLACES),
                 )
 
-            gbank = {}
-
             def gain_turn(bank):
-                gbank[0] = bank_tile(bank)[:].rearrange("p a n -> p (a n)").rearrange("p (r x) -> p r x", x=4)
+                turned = bank_tile(bank)[:].rearrange("p a n -> p (a n)").rearrange("p (r x) -> p r x", x=PLACES)
                 for u in range(2):
-                    nc.tensor.transpose(gbank[0][:, :, u], grow[:].bitcast(F32)[:, u::2], ident[:])
+                    nc.tensor.transpose(turned[:, :, u], gain_row[:].bitcast(F32)[:, u::2], ident[:])
+                return turned[:, 0, 0:2].bitcast(BF16)
 
-            def factor_fused(s, c, row, slot):
-                grouped[s, c] = keep_tile([128, 4 * P], BF16, "grouped", slot)
-                four = gbank[0][:, row, 0:2].bitcast(BF16)
+            def factor_fused(s, c, gains, slot):
+                grouped[s, c] = keep_tile([PARTS, PLACES * P], BF16, "grouped", slot)
                 nc.vector.tensor_tensor(
-                    out=grouped[s, c][:].rearrange("p (t m j) -> p m t j", t=4, j=4),
-                    in0=rows4[s, c][:].rearrange("p j (m t) -> p m t j", t=4),
-                    in1=four.unsqueeze(1).unsqueeze(1).to_broadcast([128, 128, 4, 4]),
+                    out=grouped[s, c][:].rearrange("p (t m j) -> p m t j", t=PLACES, j=PLACES),
+                    in0=rows4[s, c][:].rearrange("p j (m t) -> p m t j", t=PLACES),
+                    in1=gains.unsqueeze(1).unsqueeze(1).to_broadcast([PARTS, PARTS, PLACES, PLACES]),
                     op=ALU.mult,
                 )
 
             def factor_quantise(s, c):
                 quantise(gcodes[s, c][:], gscale[s, c][:], grouped[s, c][:])
 
-            def tb_group(c, h, engine, slot, w0=0, w1=512):
-                grouped["t", c, h, w0] = keep_tile([128, 4 * (w1 - w0)], BF16, "grouped", slot)
-                move(engine, grouped["t", c, h, w0][:].rearrange("p (w j) -> p w j", j=4), tbr[c, h][:, :, w0:w1].rearrange("p j w -> p w j"))
+            def tb_group(c, h, slot, w0=0, w1=PASS):
+                grouped["t", c, h, w0] = keep_tile([PARTS, PLACES * (w1 - w0)], BF16, "grouped", slot)
+                move(GPSIMD, grouped["t", c, h, w0][:].rearrange("p (w j) -> p w j", j=PLACES), tb_rows[c, h][:, :, w0:w1].rearrange("p j w -> p w j"))
 
-            def tb_quantise(c, h, w0=0, w1=512):
+            def tb_quantise(c, h, w0=0, w1=PASS):
                 quantise(tbcodes[c, h][:, w0:w1], tbscale[c, h][:, w0:w1], grouped["t", c, h, w0][:])
 
-            tabank, tat = {}, {}
+            ta_bank, ta_t = {}, {}
 
             def ta_turn(b, bank):
-                words = tar[b].bitcast(F32)
-                tabank[b] = bank_tile(bank)
+                words = ta_rows[b].bitcast(F32)
+                ta_bank[b] = bank_tile(bank)
                 for c in range(2):
                     for u in range(2):
-                        nc.tensor.transpose(tabank[b][:, 2 * c + u, :], words[:, 256 * c + u : 256 * (c + 1) : 2], ident[:])
+                        nc.tensor.transpose(ta_bank[b][:, 2 * c + u, :], words[:, PASS // 2 * c + u : PASS // 2 * (c + 1) : 2], ident[:])
 
-            def ta_words(b, slot=None, engine="s"):
-                if b % 2 == 0:
-                    tat[b // 2] = keep_tile([128, 2 * 256 * 4], BF16, "tat", slot)
-                words = tat[b // 2][:].bitcast(F32).rearrange("p (c n u) -> p c n u", c=2, u=2)
-                copy_on(engine)(out=words[:, :, 128 * (b % 2) : 128 * (b % 2) + 128, :], in_=tabank[b][:].rearrange("p (c u) n -> p c n u", c=2))
+            def ta_words(b, slot=None):
+                if slot:
+                    ta_t[b // 2] = keep_tile([PARTS, 2 * PAIR * PLACES], BF16, "tat", slot)
+                words = ta_t[b // 2][:].bitcast(F32).rearrange("p (c n u) -> p c n u", c=2, u=2)
+                move(SCALAR, words[:, :, span(b % 2, PARTS), :], ta_bank[b][:].rearrange("p (c u) n -> p c n u", c=2))
 
             def ta_quantise(q):
-                quantise(tacodes[q][:].rearrange("p c n -> p (c n)"), tascale[q][:].rearrange("p c n -> p (c n)"), tat[q][:])
+                quantise(tacodes[q][:].rearrange("p c n -> p (c n)"), tascale[q][:].rearrange("p c n -> p (c n)"), ta_t[q][:])
 
-            fbank, ybank = {}, {}
+            factor_bank, y_bank = {}, {}
 
-            def factor_turn(s, c, h, bank):
-                fbank[s, c, h] = bank_tile(bank)
-                for jj in range(2):
-                    words = rows4[s, c, 2 * h + jj].bitcast(F32)
+            def factor_turn(s, c, jj, bank):
+                factor_bank[s, c, jj] = bank_tile(bank)
+                for j in range(2):
+                    words = rows4[s, c, 2 * jj + j].bitcast(F32)
                     for u in range(2):
-                        nc.tensor.transpose(fbank[s, c, h][:, 2 * jj + u, :], words[:, u::2], ident[:])
+                        nc.tensor.transpose(factor_bank[s, c, jj][:, 2 * j + u, :], words[:, u::2], ident[:])
 
-            def factor_words(s, c, h, engine="s"):
-                dst = xt[s, c][:].bitcast(F32).rearrange("p (q r) -> p q r", r=8)[:, :, 4 * h : 4 * h + 4]
-                copy_on(engine)(out=dst, in_=fbank[s, c, h][:].rearrange("p r q -> p q r"))
+            def factor_words(s, c, jj, engine=SCALAR):
+                dst = xt[s, c][:].bitcast(F32).rearrange("p (q jj r) -> p q jj r", jj=2, r=4)[:, :, jj, :]
+                move(engine, dst, factor_bank[s, c, jj][:].rearrange("p r q -> p q r"))
 
-            def x_mm(s, b, c, bank=None):
-                if c == 0:
-                    ybank[s, b] = bank_tile(bank)
-                if s == "a":
-                    own = slice(128 * (b % 2), 128 * (b % 2) + 128)
-                    codes, scale = tacodes[b // 2][:, c, own], tascale[b // 2][:, c, own]
-                else:
-                    own = slice(128 * (b % 4), 128 * (b % 4) + 128)
-                    codes, scale = tbcodes[c, b // 4][:, own], tbscale[c, b // 4][:, own]
-                for t in range(4):
-                    cols = slice(128 * t, 128 * (t + 1))
-                    nc.tensor.matmul_mx(
-                        out=ybank[s, b][:, t, :],
-                        lhsT=gcodes[s, c][:, cols].bitcast(FP8X4),
-                        lhsT_scale=gscale[s, c][:, cols],
-                        rhs=codes.bitcast(FP8X4),
-                        rhs_scale=scale,
-                        start=(c == 0 and t == 0),
-                        stop=(c == 1 and t == 3),
-                    )
-
-            def x_both(s, b, bank):
-                x_mm(s, b, 0, bank)
-                x_mm(s, b, 1)
+            def dress(s, b, bank):
+                y_bank[s, b] = bank_tile(bank)
+                for c in range(2):
+                    if s == "a":
+                        codes, scale = tacodes[b // 2][:, c, span(b % 2, PARTS)], tascale[b // 2][:, c, span(b % 2, PARTS)]
+                    else:
+                        codes, scale = tbcodes[c, b // 4][:, span(b % 4, PARTS)], tbscale[c, b // 4][:, span(b % 4, PARTS)]
+                    for t in range(PLACES):
+                        nc.tensor.matmul_mx(
+                            out=y_bank[s, b][:, t, :],
+                            lhsT=gcodes[s, c][:, span(t, PARTS)].bitcast(FP8X4),
+                            lhsT_scale=gscale[s, c][:, span(t, PARTS)],
+                            rhs=codes.bitcast(FP8X4),
+                            rhs_scale=scale,
+                            start=(c == 0 and t == 0),
+                            stop=(c == 1 and t == PLACES - 1),
+                        )
 
             def x_add(s, b):
-                own = xt[s, b // 4][:, 512 * (b % 4) : 512 * (b % 4 + 1)].rearrange("p (n t) -> p n t", t=4)
-                nc.vector.tensor_tensor(out=own, in0=ybank[s, b][:].rearrange("p t n -> p n t"), in1=own, op=ALU.add)
+                own = xt[s, b // 4][:, span(b % 4, PASS)].rearrange("p (n t) -> p n t", t=PLACES)
+                nc.vector.tensor_tensor(out=own, in0=y_bank[s, b][:].rearrange("p t n -> p n t"), in1=own, op=ALU.add)
 
-            def x_quantise(s, h):
-                cols = slice(512 * h, 512 * (h + 1))
-                quantise(xcodes[s][:, cols], xscale[s][:, cols], xt[s, h][:])
+            def x_quantise(s, c):
+                quantise(xcodes[s][:, span(c, PASS)], xscale[s][:, span(c, PASS)], xt[s, c][:])
 
             def rec_rows(h, b0, b1):
                 return rec[b0 // 4, h][:, b0 % 4 : b0 % 4 + b1 - b0, :]
 
-            def root(h, b0, b1, w0=0, w1=512):
-                nc.scalar.activation(out=rec_rows(h, b0, b1)[:, :, w0:w1], in_=dr[h, b0, w0][:], func=ACT.Abs_reciprocal_sqrt)
+            def root(h, b0, b1):
+                nc.scalar.activation(out=rec_rows(h, b0, b1), in_=delta_rows[h, b0][:], func=ACT.Abs_reciprocal_sqrt)
 
             def square(h, b0, b1):
                 nc.scalar.activation(out=rec_rows(h, b0, b1), in_=rec_rows(h, b0, b1), func=ACT.Square)
@@ -221,15 +217,13 @@ def tile_opposedspindirectringamplitudeupdate_x1_kernel(tc, ta, tb, ba, bb, ga, 
             prod = {}
 
             def product(b, h, bank):
-                own = slice(128 * b, 128 * (b + 1))
-                cols = slice(512 * h, 512 * (h + 1))
                 prod[b, h] = bank_tile(bank)[:].rearrange("p t n -> p (t n)")
                 nc.tensor.matmul_mx(
                     out=prod[b, h],
-                    lhsT=xcodes["a"][:, own].bitcast(FP8X4),
-                    lhsT_scale=xscale["a"][:, own],
-                    rhs=xcodes["b"][:, cols].bitcast(FP8X4),
-                    rhs_scale=xscale["b"][:, cols],
+                    lhsT=xcodes["a"][:, span(b, PARTS)].bitcast(FP8X4),
+                    lhsT_scale=xscale["a"][:, span(b, PARTS)],
+                    rhs=xcodes["b"][:, span(h, PASS)].bitcast(FP8X4),
+                    rhs_scale=xscale["b"][:, span(h, PASS)],
                     start=True,
                     stop=True,
                 )
@@ -238,136 +232,132 @@ def tile_opposedspindirectringamplitudeupdate_x1_kernel(tc, ta, tb, ba, bb, ga, 
                 own = rec[b // 4, h][:, b % 4, :]
                 nc.vector.scalar_tensor_tensor(out=own, in0=prod[b, h], scalar=-1.0, in1=own, op0=ALU.mult, op1=ALU.mult)
 
-            rb, pbank, pt = {}, {}, {}
+            rounded, plane_bank, plane_t = {}, {}, {}
 
             def narrow(q, h, engine, slot, k0=0, k1=2):
-                if (q, h) not in rb:
-                    rb[q, h] = keep_tile([128, 1024], BF16, "rb", slot)
-                pairs = slice(128 * k0, 128 * k1)
-                out = rb[q, h][:].rearrange("p (u w e) -> p u w e", u=2, e=2)[:, :, pairs, :]
-                src = rec_rows(h, 2 * q, 2 * q + 2).rearrange("p k (w u e) -> p u (k w) e", u=2, e=2)[:, :, pairs, :]
-                if engine != "g":
+                if slot:
+                    rounded[q, h] = keep_tile([PARTS, 2 * PASS], BF16, "rb", slot)
+                words = slice(PARTS * k0, PARTS * k1)
+                out = rounded[q, h][:].rearrange("p (u w e) -> p u w e", u=2, e=2)[:, :, words, :]
+                src = rec_rows(h, 2 * q, 2 * q + 2).rearrange("p k (w u e) -> p u (k w) e", u=2, e=2)[:, :, words, :]
+                if engine != GPSIMD:
                     out, src = out.rearrange("p u (a w) e -> p a u w e", w=4), src.rearrange("p u (a w) e -> p a u w e", w=4)
                 move(engine, out, src)
 
-            def p_turn(q, h, bank, k0=0, k1=2):
-                bank = bank_tile(bank)
-                words = rb[q, h][:].bitcast(F32)
-                for k in range(k0, k1):
-                    pbank[q, h, k] = bank
+            def plane_turn(q, h, bank):
+                plane_bank[q, h] = bank_tile(bank)
+                words = rounded[q, h][:].bitcast(F32)
+                for k in range(2):
                     for u in range(2):
-                        first = 256 * u + 128 * k
-                        nc.tensor.transpose(bank[:, 2 * k + u, :], words[:, first : first + 128], ident[:])
+                        nc.tensor.transpose(plane_bank[q, h][:, 2 * k + u, :], words[:, span(2 * u + k, PARTS)], ident[:])
 
-            def p_words(q, h, slot, k0=0, k1=2, engine="s"):
-                if (q // 2, h) not in pt:
-                    pt[q // 2, h] = keep_tile([128, 2048], BF16, "pt", slot)
-                words = pt[q // 2, h][:].bitcast(F32).rearrange("p (k n u) -> p k n u", k=4, u=2)
-                first = 2 * (q % 2)
-                copy_on(engine)(
-                    out=words[:, first + k0 : first + k1, :, :], in_=pbank[q, h, k0][:, 2 * k0 : 2 * k1, :].rearrange("p (k u) n -> p k n u", u=2)
-                )
-
-            def p_quantise(h, b0, b1):
-                cols = slice(128 * b0, 128 * b1)
-                quantise(pcodes[h][:, cols], pscale[:, h, cols], pt[b0 // 4, h][:, 512 * (b0 % 4) : 512 * (b0 % 4 + b1 - b0)])
+            def plane_words(q, h, slot=None):
+                if slot:
+                    plane_t[q // 2, h] = keep_tile([PARTS, PLACES * PASS], BF16, "pt", slot)
+                words = plane_t[q // 2, h][:].bitcast(F32).rearrange("p (k n u) -> p k n u", k=4, u=2)
+                move(SCALAR, words[:, span(q % 2, 2), :, :], plane_bank[q, h][:].rearrange("p (k u) n -> p k n u", u=2))
 
             def store_r(q, h, k0=0, k1=2):
-                rows = out_0[256 * q + 128 * k0 : 256 * q + 128 * k1, 512 * h : 512 * (h + 1)]
-                nc.sync.dma_start(out=rows.rearrange("(k p) m -> p k m", p=128), in_=rec_rows(h, 2 * q + k0, 2 * q + k1))
+                rows = out_0[PAIR * q + PARTS * k0 : PAIR * q + PARTS * k1, span(h, PASS)]
+                nc.sync.dma_start(out=rows.rearrange("(k p) m -> p k m", p=PARTS), in_=rec_rows(h, 2 * q + k0, 2 * q + k1))
 
-            def store_codes(h, b0, b1):
-                cols = slice(128 * b0, 128 * b1)
+            def plane_out(h, b0, b1):
+                cols = slice(PARTS * b0, PARTS * b1)
+                quantise(pcodes[h][:, cols], pscale[:, h, cols], plane_t[b0 // 4, h][:, PASS * (b0 % 4) : PASS * (b0 % 4 + b1 - b0)])
                 nc.sync.dma_start(out=out_1[h, :, cols, :].rearrange("p n f -> p (n f)").bitcast(I32), in_=pcodes[h][:, cols].bitcast(I32))
 
-            def store_scales(queues):
-                for quad in range(4):
-                    queues[quad % 2].dma_start(
-                        out=out_2[:, 4 * quad : 4 * quad + 4, :].rearrange("g r n -> r g n").bitcast(I32),
-                        in_=pscale[32 * quad : 32 * quad + 4, :, :].bitcast(I32),
+            def store_scales():
+                for quad in range(PARTS // QUADRANT):
+                    (nc.scalar, nc.sync)[quad % 2].dma_start(
+                        out=out_2[:, span(quad, 4), :].rearrange("g r n -> r g n").bitcast(I32),
+                        in_=pscale[QUADRANT * quad : QUADRANT * quad + 4, :, :].bitcast(I32),
                     )
 
             load_gain("a", ga, nc.scalar)
-            load_rows4("a", 0, 2)
-            load_gain_row(0, ga, 1, nc.scalar)
-            load_delta(0, 0, 1)
+            load_rows4("a", 0, pieces=2)
+            load_gain_row()
+            load_delta(LEFT, 0, 1)
             load_rows4("a", 1)
-            load_tb(0, 0, 1)
-            load_delta(0, 1, 2)
-            load_ta(0, 2)
-            load_ta(2, 4)
-            load_ta(4, 6)
+            load_tb(0, LEFT)
+            load_delta(LEFT, 1, 2)
+            for q in range(3):
+                load_ta(q)
             load_rows4("b", 0)
             load_gain("b", gb, nc.sync)
             load_rows4("b", 1)
-            load_tb(1, 0, 1)
-            load_ta(6, 8)
-            load_delta(0, 2, 4)
-            load_tb(0, 1, 2)
-            load_delta(0, 4, 8)
-            load_tb(1, 1, 2)
-            load_delta(1, 0, 4)
-            load_delta(1, 4, 8)
+            load_tb(1, LEFT)
+            load_ta(3)
+            load_delta(LEFT, 2, 4)
+            load_tb(0, RIGHT)
+            load_delta(LEFT, 4, 8)
+            load_tb(1, RIGHT)
+            load_delta(RIGHT, 0, 4)
+            load_delta(RIGHT, 4, 8)
 
-            root(0, 0, 1)
+
+            root(LEFT, 0, 1)
             factor_turn("a", 0, 0, 0)
-            gain_turn(7)
+            gains = gain_turn(7)
             factor_turn("a", 0, 1, 1)
             factor_turn("a", 1, 0, 2)
             factor_turn("a", 1, 1, 3)
             factor_words("a", 0, 0)
             factor_words("a", 0, 1)
             factor_words("a", 1, 0)
-            root(0, 1, 2)
+            root(LEFT, 1, 2)
             factor_mult("a", 0, "s0")
-            factor_group("a", 0, "v", "g0")
-            tb_group(0, 0, "g", "g2")
-            factor_fused("a", 1, 0, "g1")
-            factor_words("a", 1, 1, "v")
-            for b in range(6):
-                ta_turn(b, (4, 5, 6, 0, 1, 7)[b])
-            square(0, 0, 2)
-            for b in range(6):
-                ta_words(b, "t%d" % (b // 2))
+            factor_group("a", 0, VECTOR, "g0")
+            tb_group(0, LEFT, "g2")
+            factor_fused("a", 1, gains, "g1")
+            factor_words("a", 1, 1, VECTOR)
+
+            for b, bank in enumerate((4, 5, 6, 0, 1, 7)):
+                ta_turn(b, bank)
+            square(LEFT, 0, 2)
+            for q in range(3):
+                ta_words(2 * q, "t%d" % q)
+                ta_words(2 * q + 1)
             factor_quantise("a", 1)
             factor_quantise("a", 0)
-            tb_quantise(0, 0)
+            tb_quantise(0, LEFT)
             ta_quantise(0)
             factor_mult("b", 0, "s0")
             factor_mult("b", 1, "s1")
             ta_quantise(1)
-            factor_group("b", 0, "s", "g0")
-            factor_group("b", 1, "s", "g1")
+            factor_group("b", 0, SCALAR, "g0")
+            factor_group("b", 1, SCALAR, "g1")
             ta_quantise(2)
-            tb_group(1, 0, "g", "t1")
+
+            tb_group(1, LEFT, "t1")
             for b in range(5):
-                x_both("a", b, 2 + b)
+                dress("a", b, 2 + b)
             ta_turn(6, 1)
             ta_turn(7, 7)
-            x_both("a", 5, 0)
+            dress("a", 5, 0)
             ta_words(6, "t0")
             ta_words(7)
             for b in range(5):
                 x_add("a", b)
-            factor_turn("b", 0, 0, 2)
-            factor_turn("b", 0, 1, 3)
-            factor_words("b", 0, 0)
-            factor_words("b", 0, 1)
+            for jj in range(2):
+                factor_turn("b", 0, jj, 2 + jj)
+            for jj in range(2):
+                factor_words("b", 0, jj)
             factor_quantise("b", 0)
-            tb_quantise(1, 0)
+            tb_quantise(1, LEFT)
             factor_quantise("b", 1)
             x_quantise("a", 0)
             ta_quantise(3)
-            tb_group(0, 1, "g", "xta0")
-            tb_group(1, 1, "g", "g0", 0, 256)
+
+            tb_group(0, RIGHT, "xta0")
+            tb_group(1, RIGHT, "g0", 0, PASS // 2)
             for b in range(3):
-                x_both("b", b, 4 + b)
-            x_both("a", 6, 1)
-            x_both("a", 7, 7)
-            x_both("b", 3, 2)
-            root(0, 2, 4)
-            root(0, 4, 8)
-            square(0, 2, 4)
+                dress("b", b, 4 + b)
+            dress("a", 6, 1)
+            dress("a", 7, 7)
+            dress("b", 3, 2)
+            root(LEFT, 2, 4)
+            root(LEFT, 4, 8)
+            square(LEFT, 2, 4)
             x_add("a", 5)
             for b in range(3):
                 x_add("b", b)
@@ -376,99 +366,96 @@ def tile_opposedspindirectringamplitudeupdate_x1_kernel(tc, ta, tb, ba, bb, ga, 
             x_add("b", 3)
             factor_turn("b", 1, 0, 3)
             factor_turn("b", 1, 1, 0)
-            factor_words("b", 1, 0)
-            factor_words("b", 1, 1)
-            square(0, 4, 8)
+            for jj in range(2):
+                factor_words("b", 1, jj)
+            square(LEFT, 4, 8)
             x_quantise("b", 0)
             x_quantise("a", 1)
-            tb_quantise(1, 1, 0, 256)
-            tb_quantise(0, 1)
-            tb_group(1, 1, "g", "g0", 256, 512)
-            for b in (0, 1, 3, 2):
-                product(b, 0, (4, 5, 6, 1)[b])
-            product(5, 0, 7)
-            product(4, 0, 2)
-            x_both("b", 5, 3)
-            x_both("b", 4, 0)
-            root(1, 0, 4)
-            root(1, 4, 8)
-            divide(0, 0)
-            divide(1, 0)
-            store_r(0, 0)
-            divide(2, 0)
-            tb_quantise(1, 1, 256, 512)
-            narrow(0, 0, "g", "g0")
-            x_both("b", 7, 4)
-            x_both("b", 6, 5)
-            divide(3, 0)
-            store_r(1, 0)
-            narrow(1, 0, "g", "s1")
-            divide(4, 0)
-            p_turn(0, 0, 6)
+            tb_quantise(1, RIGHT, 0, PASS // 2)
+            tb_quantise(0, RIGHT)
+
+            tb_group(1, RIGHT, "g0", PASS // 2, PASS)
+            for b, bank in ((0, 4), (1, 5), (3, 1), (2, 6), (5, 7), (4, 2)):
+                product(b, LEFT, bank)
+            dress("b", 5, 3)
+            dress("b", 4, 0)
+            root(RIGHT, 0, 4)
+            root(RIGHT, 4, 8)
+            divide(0, LEFT)
+            divide(1, LEFT)
+            store_r(0, LEFT)
+            divide(2, LEFT)
+            tb_quantise(1, RIGHT, PASS // 2, PASS)
+            narrow(0, LEFT, GPSIMD, "g0")
+            dress("b", 7, 4)
+            dress("b", 6, 5)
+            divide(3, LEFT)
+            store_r(1, LEFT)
+            narrow(1, LEFT, GPSIMD, "s1")
+            divide(4, LEFT)
+            plane_turn(0, LEFT, 6)
             for b in range(4, 8):
                 x_add("b", b)
-            product(7, 0, 0)
-            product(6, 0, 3)
-            p_words(0, 0, "g1")
-            square(1, 0, 2)
-            p_turn(1, 0, 1)
-            p_words(1, 0, "g1")
-            square(1, 2, 4)
-            square(1, 4, 6)
-            divide(5, 0)
+            product(7, LEFT, 0)
+            product(6, LEFT, 3)
+            plane_words(0, LEFT, "g1")
+            square(RIGHT, 0, 2)
+            plane_turn(1, LEFT, 1)
+            plane_words(1, LEFT)
+            square(RIGHT, 2, 4)
+            square(RIGHT, 4, 6)
+            divide(5, LEFT)
             x_quantise("b", 1)
-            store_r(2, 0)
-            narrow(2, 0, "g", "t0")
-            divide(6, 0)
-            divide(7, 0)
-            store_r(3, 0)
-            narrow(3, 0, "g", "t2")
-            for b in (0, 1, 3, 2):
-                product(b, 1, (2, 4, 5, 6)[b])
-            p_turn(2, 0, 7)
-            product(5, 1, 1)
-            product(4, 1, 3)
-            p_words(2, 0, "g2")
-            divide(0, 1)
-            divide(1, 1)
-            store_r(0, 1)
-            narrow(0, 1, "g", "xtb0")
-            p_turn(3, 0, 0)
-            square(1, 6, 8)
-            p_words(3, 0, "g2")
-            product(7, 1, 2)
-            product(6, 1, 4)
-            divide(2, 1)
-            divide(3, 1)
-            store_r(1, 1)
-            narrow(1, 1, "g", "xtb1")
-            p_turn(0, 1, 7)
-            p_words(0, 1, "xta0")
-            divide(4, 1)
-            divide(5, 1)
-            store_r(2, 1)
-            narrow(2, 1, "g", "s0", 0, 1)
-            narrow(2, 1, "s", "s0", 1, 2)
-            p_turn(1, 1, 5)
-            divide(6, 1)
-            store_r(3, 1, 0, 1)
-            narrow(3, 1, "s", "s1", 0, 1)
-            p_words(1, 1, "xta0")
-            divide(7, 1)
-            store_r(3, 1, 1, 2)
-            narrow(3, 1, "v", "s1", 1, 2)
-            p_quantise(0, 0, 4)
-            store_codes(0, 0, 4)
-            p_quantise(0, 4, 8)
-            store_codes(0, 4, 8)
-            p_turn(2, 1, 6)
-            p_words(2, 1, "t1")
-            p_turn(3, 1, 0)
-            p_words(3, 1, "t1")
-            p_quantise(1, 0, 4)
-            store_codes(1, 0, 4)
-            p_quantise(1, 4, 6)
-            store_codes(1, 4, 6)
-            p_quantise(1, 6, 8)
-            store_codes(1, 6, 8)
-            store_scales((nc.scalar, nc.sync))
+            store_r(2, LEFT)
+            narrow(2, LEFT, GPSIMD, "t0")
+            divide(6, LEFT)
+            divide(7, LEFT)
+            store_r(3, LEFT)
+            narrow(3, LEFT, GPSIMD, "t2")
+
+            for b, bank in ((0, 2), (1, 4), (3, 6), (2, 5)):
+                product(b, RIGHT, bank)
+            plane_turn(2, LEFT, 7)
+            product(5, RIGHT, 1)
+            product(4, RIGHT, 3)
+            plane_words(2, LEFT, "g2")
+            divide(0, RIGHT)
+            divide(1, RIGHT)
+            store_r(0, RIGHT)
+            narrow(0, RIGHT, GPSIMD, "xtb0")
+            plane_turn(3, LEFT, 0)
+            square(RIGHT, 6, 8)
+            plane_words(3, LEFT)
+            product(7, RIGHT, 2)
+            product(6, RIGHT, 4)
+            divide(2, RIGHT)
+            divide(3, RIGHT)
+            store_r(1, RIGHT)
+            narrow(1, RIGHT, GPSIMD, "xtb1")
+            plane_turn(0, RIGHT, 7)
+            plane_words(0, RIGHT, "xta0")
+            divide(4, RIGHT)
+            divide(5, RIGHT)
+            store_r(2, RIGHT)
+
+            narrow(2, RIGHT, GPSIMD, "s0", 0, 1)
+            narrow(2, RIGHT, SCALAR, None, 1, 2)
+            plane_turn(1, RIGHT, 5)
+            divide(6, RIGHT)
+            store_r(3, RIGHT, 0, 1)
+            narrow(3, RIGHT, SCALAR, "s1", 0, 1)
+            plane_words(1, RIGHT)
+            divide(7, RIGHT)
+            store_r(3, RIGHT, 1, 2)
+            narrow(3, RIGHT, VECTOR, None, 1, 2)
+
+            plane_out(LEFT, 0, 4)
+            plane_out(LEFT, 4, 8)
+            plane_turn(2, RIGHT, 6)
+            plane_words(2, RIGHT, "t1")
+            plane_turn(3, RIGHT, 0)
+            plane_words(3, RIGHT)
+            plane_out(RIGHT, 0, 4)
+            plane_out(RIGHT, 4, 6)
+            plane_out(RIGHT, 6, 8)
+            store_scales()

@@ -39,11 +39,11 @@ def tile_opposedspindirectringamplitudeupdate_x1_kernel(tc, ta, tb, ba, bb, ga, 
             return slice(width * i, width * (i + 1))
 
         ident = keep_tile([PARTS, PARTS], F32, "ident")
+        ident_bf = keep_tile([PARTS, PARTS], BF16, "identbf")
         factor = {"a": ba, "b": bb}
-        gain_passes = {"a": 1, "b": 2}
         gain, rows4, gcodes, gscale, xt, xcodes, xscale = {}, {}, {}, {}, {}, {}, {}
         for s in ("a", "b"):
-            gain[s] = keep_tile([PARTS, gain_passes[s], PLACES], BF16, "gain" + s)
+            gain[s] = keep_tile([PARTS, 2, PLACES], BF16, "gain" + s)
             xcodes[s] = keep_tile([PARTS, N], U32, "xcodes" + s)
             xscale[s] = keep_tile([PARTS, N], U8, "xscale" + s)
             for c in range(2):
@@ -62,16 +62,23 @@ def tile_opposedspindirectringamplitudeupdate_x1_kernel(tc, ta, tb, ba, bb, ga, 
         pscale = keep_tile([PARTS, 2, N], U8, "pscale")
         ta_rows, tb_rows, delta_rows = {}, {}, {}
 
-        gain_row = keep_tile([PARTS, PASS], BF16, "grow")
-        nc.gpsimd.memset(gain_row[:].bitcast(I32), 0)
+        ba_t = {1: keep_tile([PARTS, PLACES * P], BF16, "bat")}
+        ba_rows = {}
+        make_identity(nc, ident_bf[:])
         make_identity(nc, ident[:])
         with tc.manual_schedule():
 
             def load_gain(s, g, queue):
-                queue.dma_start(out=gain[s][:], in_=g[0 : PASS * gain_passes[s]].rearrange("(c p j) -> p c j", p=PARTS, j=PLACES))
+                queue.dma_start(out=gain[s][:], in_=g.rearrange("(c p j) -> p c j", p=PARTS, j=PLACES))
 
-            def load_gain_row():
-                nc.scalar.dma_start(out=gain_row[0:1, :], in_=ga[span(1, PASS)].rearrange("(r w) -> r w", r=1))
+            def load_ba(r0, r1):
+                rows = keep_tile([PARTS, r1 - r0, P], BF16, "bar%d" % r0)
+                nc.sync.dma_start(out=rows[:], in_=ba[PARTS * r0 : PARTS * r1, :].rearrange("(r i) w -> i r w", i=PARTS))
+                for r in range(r0, r1):
+                    ba_rows[r] = rows[:, r - r0, :]
+
+            def dealt(x, b0, b1, cols):
+                return x[span(b0 // 4, PASS), cols].rearrange("(p j) w -> p j w", j=PLACES)[:, b0 % 4 : b0 % 4 + b1 - b0, :]
 
             def load_rows4(s, c, pieces=1):
                 src = factor[s][span(c, PASS), :].rearrange("(p j) w -> p j w", j=PLACES)
@@ -87,14 +94,13 @@ def tile_opposedspindirectringamplitudeupdate_x1_kernel(tc, ta, tb, ba, bb, ga, 
                 tb_rows[c, h] = keep_tile([PARTS, PLACES, PASS], BF16, "tbr%d%d" % (c, h))
                 nc.sync.dma_start(out=tb_rows[c, h][:], in_=tb[span(c, PASS), span(h, PASS)].rearrange("(p j) w -> p j w", j=PLACES))
 
-            def load_delta(h, b0, b1):
-                delta_rows[h, b0] = keep_tile([PARTS, b1 - b0, PASS], BF16, "dr%d%d" % (h, b0))
-                src = delta[PARTS * b0 : PARTS * b1, span(h, PASS)]
-                nc.sync.dma_start(out=delta_rows[h, b0][:], in_=src.rearrange("(k p) m -> p k m", p=PARTS))
+            def load_delta(h, b0, b1, w0=0, w1=PASS, queue=nc.sync):
+                delta_rows[h, b0, w0] = keep_tile([PARTS, b1 - b0, w1 - w0], BF16, "dr%d%d%d" % (h, b0, w0))
+                queue.dma_start(out=delta_rows[h, b0, w0][:], in_=dealt(delta, b0, b1, slice(PASS * h + w0, PASS * h + w1)))
 
             def load_ta(q):
                 rows = keep_tile([PARTS, 2, N], BF16, "tar%d" % q)
-                nc.sync.dma_start(out=rows[:], in_=ta[span(q, PAIR), :].rearrange("(k p) w -> p k w", p=PARTS))
+                nc.sync.dma_start(out=rows[:], in_=dealt(ta, 2 * q, 2 * q + 2, slice(0, N)))
                 for k in range(2):
                     ta_rows[2 * q + k] = rows[:, k, :]
 
@@ -124,30 +130,51 @@ def tile_opposedspindirectringamplitudeupdate_x1_kernel(tc, ta, tb, ba, bb, ga, 
                     scaled[s, c][:].rearrange("p (j m e t) -> p m t e j", t=PLACES, e=2, j=PLACES),
                 )
 
-            def gain_turn(bank):
-                turned = bank_tile(bank)[:].rearrange("p a n -> p (a n)").rearrange("p (r x) -> p r x", x=PLACES)
-                for u in range(2):
-                    nc.tensor.transpose(turned[:, :, u], gain_row[:].bitcast(F32)[:, u::2], ident[:])
-                return turned[:, 0, 0:2].bitcast(BF16)
+            ba_bank, ga_bank = {}, {}
 
-            def factor_fused(s, c, gains, slot):
-                grouped[s, c] = keep_tile([PARTS, PLACES * P], BF16, "grouped", slot)
+            def ba_turn(r, banks=None):
+                c = r // 4
+                for lo in range(2):
+                    if banks:
+                        ba_bank[c, lo] = bank_tile(banks[lo])
+                    out = ba_bank[c, lo][:].rearrange("p a n -> p (a n)").bitcast(BF16)
+                    for hi in range(2):
+                        nc.tensor.transpose(out[:, span(4 * hi + r % 4, PARTS)], ba_rows[r][:, 2 * hi + lo :: PLACES], ident_bf[:])
+
+            def ba_words(c, lo, engine):
+                dst = ba_t[c][:].bitcast(F32).rearrange("p (u lo q hi) -> p u lo q hi", u=2, lo=2, hi=2)[:, :, lo, :, :]
+                move(engine, dst, ba_bank[c, lo][:].rearrange("p a n -> p (a n)").rearrange("p (hi q u) -> p u q hi", hi=2, u=2))
+
+            def ba_turn_back(c, lo, bank):
+                ga_bank[c, lo] = bank_tile(bank)
+                words = ba_t[c][:].bitcast(F32)
+                for u in range(2):
+                    for hi in range(2):
+                        start = PAIR * (2 * u + lo) + hi
+                        nc.tensor.transpose(ga_bank[c, lo][:, 2 * u + hi, :], words[:, start : PAIR * (2 * u + lo + 1) : 2], ident[:])
+
+            def ga_mult(c, lo, slot=None):
+                if slot:
+                    grouped["a", c] = keep_tile([PARTS, PLACES * P], BF16, "grouped", slot)
+                src = ga_bank[c, lo][:].rearrange("p a n -> p (a n)").bitcast(BF16)
                 nc.vector.tensor_tensor(
-                    out=grouped[s, c][:].rearrange("p (t m j) -> p m t j", t=PLACES, j=PLACES),
-                    in0=rows4[s, c][:].rearrange("p j (m t) -> p m t j", t=PLACES),
-                    in1=gains.unsqueeze(1).unsqueeze(1).to_broadcast([PARTS, PARTS, PLACES, PLACES]),
+                    out=grouped["a", c][:, span(lo, 2 * P)].rearrange("p (w u e) -> p w u e", u=2, e=2),
+                    in0=src.rearrange("p (u w e) -> p w u e", u=2, e=2),
+                    in1=gain["a"][:, c, :].rearrange("p (u e) -> p u e", e=2).unsqueeze(1).to_broadcast([PARTS, PAIR, 2, 2]),
                     op=ALU.mult,
                 )
 
             def factor_quantise(s, c):
                 quantise(gcodes[s, c][:], gscale[s, c][:], grouped[s, c][:])
 
-            def tb_group(c, h, slot, w0=0, w1=PASS):
-                grouped["t", c, h, w0] = keep_tile([PARTS, PLACES * (w1 - w0)], BF16, "grouped", slot)
-                move(GPSIMD, grouped["t", c, h, w0][:].rearrange("p (w j) -> p w j", j=PLACES), tb_rows[c, h][:, :, w0:w1].rearrange("p j w -> p w j"))
+            def tb_group(c, h, slot, w0=0, w1=PASS, engine=GPSIMD):
+                if slot:
+                    grouped["t", c, h] = keep_tile([PARTS, PLACES * PASS], BF16, "grouped", slot)
+                out = grouped["t", c, h][:].rearrange("p (w j) -> p w j", j=PLACES)[:, w0:w1, :]
+                move(engine, out, tb_rows[c, h][:, :, w0:w1].rearrange("p j w -> p w j"))
 
             def tb_quantise(c, h, w0=0, w1=PASS):
-                quantise(tbcodes[c, h][:, w0:w1], tbscale[c, h][:, w0:w1], grouped["t", c, h, w0][:])
+                quantise(tbcodes[c, h][:, w0:w1], tbscale[c, h][:, w0:w1], grouped["t", c, h][:, PLACES * w0 : PLACES * w1])
 
             ta_bank, ta_t = {}, {}
 
@@ -158,11 +185,11 @@ def tile_opposedspindirectringamplitudeupdate_x1_kernel(tc, ta, tb, ba, bb, ga, 
                     for u in range(2):
                         nc.tensor.transpose(ta_bank[b][:, 2 * c + u, :], words[:, PASS // 2 * c + u : PASS // 2 * (c + 1) : 2], ident[:])
 
-            def ta_words(b, slot=None):
+            def ta_words(b, slot=None, engine=SCALAR):
                 if slot:
                     ta_t[b // 2] = keep_tile([PARTS, 2 * PAIR * PLACES], BF16, "tat", slot)
                 words = ta_t[b // 2][:].bitcast(F32).rearrange("p (c n u) -> p c n u", c=2, u=2)
-                move(SCALAR, words[:, :, span(b % 2, PARTS), :], ta_bank[b][:].rearrange("p (c u) n -> p c n u", c=2))
+                move(engine, words[:, :, span(b % 2, PARTS), :], ta_bank[b][:].rearrange("p (c u) n -> p c n u", c=2))
 
             def ta_quantise(q):
                 quantise(tacodes[q][:].rearrange("p c n -> p (c n)"), tascale[q][:].rearrange("p c n -> p (c n)"), ta_t[q][:])
@@ -177,21 +204,26 @@ def tile_opposedspindirectringamplitudeupdate_x1_kernel(tc, ta, tb, ba, bb, ga, 
                         nc.tensor.transpose(factor_bank[s, c, jj][:, 2 * j + u, :], words[:, u::2], ident[:])
 
             def factor_words(s, c, jj, engine=SCALAR):
-                dst = xt[s, c][:].bitcast(F32).rearrange("p (q jj r) -> p q jj r", jj=2, r=4)[:, :, jj, :]
-                move(engine, dst, factor_bank[s, c, jj][:].rearrange("p r q -> p q r"))
+                words, src = xt[s, c][:].bitcast(F32), factor_bank[s, c, jj][:]
+                if s == "a":
+                    move(engine, words[:, span(jj, PASS)].rearrange("p (j q u) -> p j q u", j=2, u=2), src.rearrange("p (j u) q -> p j q u", u=2))
+                else:
+                    move(engine, words.rearrange("p (q jj r) -> p q jj r", jj=2, r=4)[:, :, jj, :], src.rearrange("p r q -> p q r"))
 
-            def dress(s, b, bank):
-                y_bank[s, b] = bank_tile(bank)
-                for c in range(2):
+            def dress(s, b, bank, c0=0, c1=2):
+                if c0 == 0:
+                    y_bank[s, b] = bank_tile(bank)
+                for c in range(c0, c1):
                     if s == "a":
                         codes, scale = tacodes[b // 2][:, c, span(b % 2, PARTS)], tascale[b // 2][:, c, span(b % 2, PARTS)]
                     else:
                         codes, scale = tbcodes[c, b // 4][:, span(b % 4, PARTS)], tbscale[c, b // 4][:, span(b % 4, PARTS)]
                     for t in range(PLACES):
+                        group = span(2 * (t % 2) + t // 2 if (s, c) == ("a", 1) else t, PARTS)
                         nc.tensor.matmul_mx(
                             out=y_bank[s, b][:, t, :],
-                            lhsT=gcodes[s, c][:, span(t, PARTS)].bitcast(FP8X4),
-                            lhsT_scale=gscale[s, c][:, span(t, PARTS)],
+                            lhsT=gcodes[s, c][:, group].bitcast(FP8X4),
+                            lhsT_scale=gscale[s, c][:, group],
                             rhs=codes.bitcast(FP8X4),
                             rhs_scale=scale,
                             start=(c == 0 and t == 0),
@@ -200,16 +232,23 @@ def tile_opposedspindirectringamplitudeupdate_x1_kernel(tc, ta, tb, ba, bb, ga, 
 
             def x_add(s, b):
                 own = xt[s, b // 4][:, span(b % 4, PASS)].rearrange("p (n t) -> p n t", t=PLACES)
-                nc.vector.tensor_tensor(out=own, in0=y_bank[s, b][:].rearrange("p t n -> p n t"), in1=own, op=ALU.add)
+                addend = own
+                if s == "a" and b >= 4:
+                    own = own.rearrange("p n (hi lo) -> p n hi lo", lo=2)
+                    addend = ba_t[b // 4][:].rearrange("p (u lo n hi e) -> p u e n hi lo", u=2, lo=2, hi=2, e=2)[:, b % 4 // 2, b % 2]
+                    nc.vector.tensor_tensor(out=own, in0=y_bank[s, b][:].rearrange("p (hi lo) n -> p n hi lo", lo=2), in1=addend, op=ALU.add)
+                else:
+                    nc.vector.tensor_tensor(out=own, in0=y_bank[s, b][:].rearrange("p t n -> p n t"), in1=addend, op=ALU.add)
 
-            def x_quantise(s, c):
-                quantise(xcodes[s][:, span(c, PASS)], xscale[s][:, span(c, PASS)], xt[s, c][:])
+            def x_quantise(s, c, k0=0, k1=4):
+                cols = slice(PASS * c + PARTS * k0, PASS * c + PARTS * k1)
+                quantise(xcodes[s][:, cols], xscale[s][:, cols], xt[s, c][:, PASS * k0 : PASS * k1])
 
             def rec_rows(h, b0, b1):
                 return rec[b0 // 4, h][:, b0 % 4 : b0 % 4 + b1 - b0, :]
 
-            def root(h, b0, b1):
-                nc.scalar.activation(out=rec_rows(h, b0, b1), in_=delta_rows[h, b0][:], func=ACT.Abs_reciprocal_sqrt)
+            def root(h, b0, b1, w0=0, w1=PASS):
+                nc.scalar.activation(out=rec_rows(h, b0, b1)[:, :, w0:w1], in_=delta_rows[h, b0, w0][:], func=ACT.Abs_reciprocal_sqrt)
 
             def square(h, b0, b1):
                 nc.scalar.activation(out=rec_rows(h, b0, b1), in_=rec_rows(h, b0, b1), func=ACT.Square)
@@ -251,20 +290,26 @@ def tile_opposedspindirectringamplitudeupdate_x1_kernel(tc, ta, tb, ba, bb, ga, 
                     for u in range(2):
                         nc.tensor.transpose(plane_bank[q, h][:, 2 * k + u, :], words[:, span(2 * u + k, PARTS)], ident[:])
 
-            def plane_words(q, h, slot=None):
+            def plane_words(q, h, slot=None, p0=0, p1=PARTS):
                 if slot:
                     plane_t[q // 2, h] = keep_tile([PARTS, PLACES * PASS], BF16, "pt", slot)
-                words = plane_t[q // 2, h][:].bitcast(F32).rearrange("p (k n u) -> p k n u", k=4, u=2)
-                move(SCALAR, words[:, span(q % 2, 2), :, :], plane_bank[q, h][:].rearrange("p (k u) n -> p k n u", u=2))
+                words = plane_t[q // 2, h][:].bitcast(F32).rearrange("p (n jj r) -> p n jj r", jj=2, r=4)
+                move(SCALAR, words[:, p0:p1, q % 2, :], plane_bank[q, h][:, :, p0:p1].rearrange("p r n -> p n r"))
 
             def store_r(q, h, k0=0, k1=2):
-                rows = out_0[PAIR * q + PARTS * k0 : PAIR * q + PARTS * k1, span(h, PASS)]
-                nc.sync.dma_start(out=rows.rearrange("(k p) m -> p k m", p=PARTS), in_=rec_rows(h, 2 * q + k0, 2 * q + k1))
+                nc.sync.dma_start(out=dealt(out_0, 2 * q + k0, 2 * q + k1, span(h, PASS)), in_=rec_rows(h, 2 * q + k0, 2 * q + k1))
 
-            def plane_out(h, b0, b1):
+            def plane_quantise(h, b0, b1):
                 cols = slice(PARTS * b0, PARTS * b1)
                 quantise(pcodes[h][:, cols], pscale[:, h, cols], plane_t[b0 // 4, h][:, PASS * (b0 % 4) : PASS * (b0 % 4 + b1 - b0)])
+
+            def plane_store(h, b0, b1):
+                cols = slice(PARTS * b0, PARTS * b1)
                 nc.sync.dma_start(out=out_1[h, :, cols, :].rearrange("p n f -> p (n f)").bitcast(I32), in_=pcodes[h][:, cols].bitcast(I32))
+
+            def plane_out(h, b0, b1):
+                plane_quantise(h, b0, b1)
+                plane_store(h, b0, b1)
 
             def store_scales():
                 for quad in range(PARTS // QUADRANT):
@@ -273,101 +318,106 @@ def tile_opposedspindirectringamplitudeupdate_x1_kernel(tc, ta, tb, ba, bb, ga, 
                         in_=pscale[QUADRANT * quad : QUADRANT * quad + 4, :, :].bitcast(I32),
                     )
 
+
             load_gain("a", ga, nc.scalar)
+            load_gain("b", gb, nc.scalar)
             load_rows4("a", 0, pieces=2)
-            load_gain_row()
             load_delta(LEFT, 0, 1)
-            load_rows4("a", 1)
-            load_tb(0, LEFT)
-            load_delta(LEFT, 1, 2)
-            for q in range(3):
-                load_ta(q)
+            load_ba(4, 6)
+            load_ba(6, 8)
             load_rows4("b", 0)
-            load_gain("b", gb, nc.sync)
+            load_ta(0)
+            load_delta(LEFT, 1, 2)
+            load_tb(0, LEFT)
+            load_ta(1)
+            load_ta(2)
             load_rows4("b", 1)
             load_tb(1, LEFT)
-            load_ta(3)
             load_delta(LEFT, 2, 4)
-            load_tb(0, RIGHT)
+            load_ta(3)
             load_delta(LEFT, 4, 8)
+            load_tb(0, RIGHT)
             load_tb(1, RIGHT)
             load_delta(RIGHT, 0, 4)
             load_delta(RIGHT, 4, 8)
 
-
             root(LEFT, 0, 1)
             factor_turn("a", 0, 0, 0)
-            gains = gain_turn(7)
             factor_turn("a", 0, 1, 1)
-            factor_turn("a", 1, 0, 2)
-            factor_turn("a", 1, 1, 3)
-            factor_words("a", 0, 0)
-            factor_words("a", 0, 1)
-            factor_words("a", 1, 0)
-            root(LEFT, 1, 2)
             factor_mult("a", 0, "s0")
             factor_group("a", 0, VECTOR, "g0")
-            tb_group(0, LEFT, "g2")
-            factor_fused("a", 1, gains, "g1")
-            factor_words("a", 1, 1, VECTOR)
-
-            for b, bank in enumerate((4, 5, 6, 0, 1, 7)):
-                ta_turn(b, bank)
-            square(LEFT, 0, 2)
-            for q in range(3):
-                ta_words(2 * q, "t%d" % q)
-                ta_words(2 * q + 1)
-            factor_quantise("a", 1)
+            factor_words("a", 0, 0)
+            factor_words("a", 0, 1)
+            square(LEFT, 0, 1)
+            ba_turn(4, (2, 3))
+            for r in range(5, 8):
+                ba_turn(r)
             factor_quantise("a", 0)
-            tb_quantise(0, LEFT)
-            ta_quantise(0)
-            factor_mult("b", 0, "s0")
-            factor_mult("b", 1, "s1")
-            ta_quantise(1)
-            factor_group("b", 0, SCALAR, "g0")
-            factor_group("b", 1, SCALAR, "g1")
-            ta_quantise(2)
-
-            tb_group(1, LEFT, "t1")
-            for b in range(5):
-                dress("a", b, 2 + b)
-            ta_turn(6, 1)
-            ta_turn(7, 7)
-            dress("a", 5, 0)
-            ta_words(6, "t0")
-            ta_words(7)
-            for b in range(5):
-                x_add("a", b)
+            factor_mult("b", 0, "s1")
+            ba_words(1, 0, SCALAR)
+            ba_words(1, 1, SCALAR)
             for jj in range(2):
-                factor_turn("b", 0, jj, 2 + jj)
+                factor_turn("b", 0, jj, 4 + jj)
+            ba_turn_back(1, 0, 6)
+            ba_turn_back(1, 1, 7)
+            factor_group("b", 0, VECTOR, "g3")
             for jj in range(2):
                 factor_words("b", 0, jj)
+            tb_group(0, LEFT, "g2", 0, 256)
+            ga_mult(1, 0, "g1")
+            ga_mult(1, 1)
+            for b in range(6):
+                ta_turn(b, b)
+            root(LEFT, 1, 2)
+            ta_words(0, "t0", VECTOR)
+            ta_words(1)
+            for q in range(1, 3):
+                ta_words(2 * q, "t%d" % q)
+                ta_words(2 * q + 1)
+            tb_group(0, LEFT, None, 256, 512, SCALAR)
+            factor_quantise("a", 1)
+            ta_quantise(0)
             factor_quantise("b", 0)
-            tb_quantise(1, LEFT)
+            ta_quantise(1)
+            factor_mult("b", 1, "s1")
+            factor_group("b", 1, SCALAR, "g1")
+            ta_quantise(2)
+            tb_quantise(0, LEFT, 0, 256)
+
+            tb_group(1, LEFT, "t2")
+            for b, bank in enumerate((6, 7, 0, 1, 2)):
+                dress("a", b, bank)
+            ta_turn(6, 3)
+            ta_turn(7, 4)
+            dress("a", 5, 5)
+            ta_words(6, "t0")
+            ta_words(7)
+            root(LEFT, 2, 4)
+            for b in range(5):
+                x_add("a", b)
+            factor_turn("b", 1, 0, 6)
+            factor_turn("b", 1, 1, 7)
             factor_quantise("b", 1)
+            tb_quantise(1, LEFT)
+            tb_quantise(0, LEFT, 256, 512)
             x_quantise("a", 0)
             ta_quantise(3)
+            for jj in range(2):
+                factor_words("b", 1, jj)
 
             tb_group(0, RIGHT, "xta0")
             tb_group(1, RIGHT, "g0", 0, PASS // 2)
-            for b in range(3):
-                dress("b", b, 4 + b)
-            dress("a", 6, 1)
-            dress("a", 7, 7)
-            dress("b", 3, 2)
-            root(LEFT, 2, 4)
+            for b, bank in enumerate((0, 1, 2, 3)):
+                dress("b", b, bank)
+            dress("a", 6, 4)
+            dress("a", 7, 6)
             root(LEFT, 4, 8)
-            square(LEFT, 2, 4)
+            square(LEFT, 1, 4)
             x_add("a", 5)
-            for b in range(3):
+            for b in range(4):
                 x_add("b", b)
             x_add("a", 6)
             x_add("a", 7)
-            x_add("b", 3)
-            factor_turn("b", 1, 0, 3)
-            factor_turn("b", 1, 1, 0)
-            for jj in range(2):
-                factor_words("b", 1, jj)
             square(LEFT, 4, 8)
             x_quantise("b", 0)
             x_quantise("a", 1)
@@ -375,10 +425,10 @@ def tile_opposedspindirectringamplitudeupdate_x1_kernel(tc, ta, tb, ba, bb, ga, 
             tb_quantise(0, RIGHT)
 
             tb_group(1, RIGHT, "g0", PASS // 2, PASS)
-            for b, bank in ((0, 4), (1, 5), (3, 1), (2, 6), (5, 7), (4, 2)):
+            for b, bank in ((0, 7), (1, 5), (3, 1), (2, 0), (4, 2)):
                 product(b, LEFT, bank)
+            dress("b", 4, 4)
             dress("b", 5, 3)
-            dress("b", 4, 0)
             root(RIGHT, 0, 4)
             root(RIGHT, 4, 8)
             divide(0, LEFT)
@@ -387,24 +437,25 @@ def tile_opposedspindirectringamplitudeupdate_x1_kernel(tc, ta, tb, ba, bb, ga, 
             divide(2, LEFT)
             tb_quantise(1, RIGHT, PASS // 2, PASS)
             narrow(0, LEFT, GPSIMD, "g0")
-            dress("b", 7, 4)
-            dress("b", 6, 5)
+            dress("b", 6, 7)
+            dress("b", 7, 6)
             divide(3, LEFT)
             store_r(1, LEFT)
             narrow(1, LEFT, GPSIMD, "s1")
             divide(4, LEFT)
-            plane_turn(0, LEFT, 6)
+            product(5, LEFT, 5)
+            plane_turn(0, LEFT, 0)
             for b in range(4, 8):
                 x_add("b", b)
-            product(7, LEFT, 0)
-            product(6, LEFT, 3)
-            plane_words(0, LEFT, "g1")
             square(RIGHT, 0, 2)
-            plane_turn(1, LEFT, 1)
-            plane_words(1, LEFT)
+            plane_words(0, LEFT, "g1")
+            plane_turn(1, LEFT, 4)
             square(RIGHT, 2, 4)
+            plane_words(1, LEFT)
             square(RIGHT, 4, 6)
+            product(6, LEFT, 6)
             divide(5, LEFT)
+            product(7, LEFT, 5)
             x_quantise("b", 1)
             store_r(2, LEFT)
             narrow(2, LEFT, GPSIMD, "t0")
@@ -413,49 +464,48 @@ def tile_opposedspindirectringamplitudeupdate_x1_kernel(tc, ta, tb, ba, bb, ga, 
             store_r(3, LEFT)
             narrow(3, LEFT, GPSIMD, "t2")
 
-            for b, bank in ((0, 2), (1, 4), (3, 6), (2, 5)):
+            for b, bank in enumerate((2, 3, 7, 1)):
                 product(b, RIGHT, bank)
-            plane_turn(2, LEFT, 7)
-            product(5, RIGHT, 1)
-            product(4, RIGHT, 3)
+            plane_turn(2, LEFT, 0)
+            product(4, RIGHT, 6)
+            product(5, RIGHT, 5)
             plane_words(2, LEFT, "g2")
+            square(RIGHT, 6, 8)
             divide(0, RIGHT)
             divide(1, RIGHT)
             store_r(0, RIGHT)
             narrow(0, RIGHT, GPSIMD, "xtb0")
-            plane_turn(3, LEFT, 0)
-            square(RIGHT, 6, 8)
+            plane_turn(3, LEFT, 4)
+            product(6, RIGHT, 2)
+            product(7, RIGHT, 3)
             plane_words(3, LEFT)
-            product(7, RIGHT, 2)
-            product(6, RIGHT, 4)
             divide(2, RIGHT)
             divide(3, RIGHT)
             store_r(1, RIGHT)
             narrow(1, RIGHT, GPSIMD, "xtb1")
             plane_turn(0, RIGHT, 7)
-            plane_words(0, RIGHT, "xta0")
             divide(4, RIGHT)
             divide(5, RIGHT)
             store_r(2, RIGHT)
-
-            narrow(2, RIGHT, GPSIMD, "s0", 0, 1)
-            narrow(2, RIGHT, SCALAR, None, 1, 2)
-            plane_turn(1, RIGHT, 5)
+            narrow(2, RIGHT, SCALAR, "s0")
+            plane_words(0, RIGHT, "xta0")
+            plane_turn(1, RIGHT, 1)
+            plane_words(1, RIGHT)
+            plane_turn(2, RIGHT, 0)
             divide(6, RIGHT)
             store_r(3, RIGHT, 0, 1)
-            narrow(3, RIGHT, SCALAR, "s1", 0, 1)
-            plane_words(1, RIGHT)
             divide(7, RIGHT)
             store_r(3, RIGHT, 1, 2)
+            narrow(3, RIGHT, VECTOR, "s1", 0, 1)
             narrow(3, RIGHT, VECTOR, None, 1, 2)
-
             plane_out(LEFT, 0, 4)
             plane_out(LEFT, 4, 8)
-            plane_turn(2, RIGHT, 6)
             plane_words(2, RIGHT, "t1")
-            plane_turn(3, RIGHT, 0)
-            plane_words(3, RIGHT)
+            plane_turn(3, RIGHT, 6)
+            plane_words(3, RIGHT, None, 0, 64)
+            plane_words(3, RIGHT, None, 64, 128)
             plane_out(RIGHT, 0, 4)
-            plane_out(RIGHT, 4, 6)
-            plane_out(RIGHT, 6, 8)
+            plane_quantise(RIGHT, 4, 6)
+            plane_quantise(RIGHT, 6, 8)
+            plane_store(RIGHT, 4, 8)
             store_scales()

from contextlib import ExitStack

import concourse.mybir as mybir
from concourse.masks import make_identity

F32 = mybir.dt.float32
BF16 = mybir.dt.bfloat16
I32 = mybir.dt.int32
U32 = mybir.dt.uint32
U8 = mybir.dt.uint8
FP8X4 = mybir.dt.float8_e4m3fn_x4
ALU = mybir.AluOpType
ACT = mybir.ActivationFunctionType

N, M, P = 1024, 1024, 512
FLOPS = 2 * N * N * P + 2 * M * M * P + 2 * N * M * P
PARTS = 128
PLACES = 4
PASS = PARTS * PLACES
PAIR = 2 * PARTS
QUADRANT = 32
LEFT, RIGHT = 0, 1
VECTOR, SCALAR, GPSIMD = "v", "s", "g"


def tile_opposedspindirectringamplitudeupdate_x1_kernel(tc, ta, tb, ba, bb, ga, gb, delta, out_0, out_1, out_2):
    nc = tc.nc
    with ExitStack() as ctx:
        keep = ctx.enter_context(tc.tile_pool(name="keep", bufs=1))
        psum = ctx.enter_context(tc.psum_pool(name="psum", bufs=1))

        def keep_tile(shape, dtype, name, slot=None):
            return keep.tile(shape, dtype, name=name, tag=slot or name, align_bytes=64)

        def bank_tile(bank):
            return psum.tile([PARTS, PLACES, PARTS], F32, name="bank", tag="bank%d" % bank)

        def span(i, width):
            return slice(width * i, width * (i + 1))

        ident = keep_tile([PARTS, PARTS], F32, "ident")
        ident_bf = keep_tile([PARTS, PARTS], BF16, "identbf")
        factor = {"a": ba, "b": bb}
        gain, rows4, gcodes, gscale, xt, xcodes, xscale = {}, {}, {}, {}, {}, {}, {}
        for s in ("a", "b"):
            gain[s] = keep_tile([PARTS, 2, PLACES], BF16, "gain" + s)
            xcodes[s] = keep_tile([PARTS, N], U32, "xcodes" + s)
            xscale[s] = keep_tile([PARTS, N], U8, "xscale" + s)
            for c in range(2):
                gcodes[s, c] = keep_tile([PARTS, P], U32, "gcodes%s%d" % (s, c))
                gscale[s, c] = keep_tile([PARTS, P], U8, "gscale%s%d" % (s, c))
                xt[s, c] = keep_tile([PARTS, PASS * PLACES], BF16, "xt%s%d" % (s, c))
        tbcodes, tbscale = {}, {}
        for c in range(2):
            for h in range(2):
                tbcodes[c, h] = keep_tile([PARTS, PASS], U32, "tbcodes%d%d" % (c, h))
                tbscale[c, h] = keep_tile([PARTS, PASS], U8, "tbscale%d%d" % (c, h))
        tacodes = [keep_tile([PARTS, 2, PAIR], U32, "tacodes%d" % q) for q in range(4)]
        tascale = [keep_tile([PARTS, 2, PAIR], U8, "tascale%d" % q) for q in range(4)]
        rec = {(four, h): keep_tile([PARTS, 4, PASS], F32, "rec%d%d" % (four, h)) for four in range(2) for h in range(2)}
        pcodes = [keep_tile([PARTS, N], U32, "pcodes%d" % h) for h in range(2)]
        pscale = keep_tile([PARTS, 2, N], U8, "pscale")
        ta_rows, tb_rows, delta_rows = {}, {}, {}

        ba_t = {1: keep_tile([PARTS, PLACES * P], BF16, "bat")}
        ba_rows = {}
        make_identity(nc, ident_bf[:])
        make_identity(nc, ident[:])
        with tc.manual_schedule():

            def load_gain(s, g, queue):
                queue.dma_start(out=gain[s][:], in_=g.rearrange("(c p j) -> p c j", p=PARTS, j=PLACES))

            def load_ba(r0, r1):
                rows = keep_tile([PARTS, r1 - r0, P], BF16, "bar%d" % r0)
                nc.sync.dma_start(out=rows[:], in_=ba[PARTS * r0 : PARTS * r1, :].rearrange("(r i) w -> i r w", i=PARTS))
                for r in range(r0, r1):
                    ba_rows[r] = rows[:, r - r0, :]

            def dealt(x, b0, b1, cols):
                return x[span(b0 // 4, PASS), cols].rearrange("(p j) w -> p j w", j=PLACES)[:, b0 % 4 : b0 % 4 + b1 - b0, :]

            def load_rows4(s, c, pieces=1):
                src = factor[s][span(c, PASS), :].rearrange("(p j) w -> p j w", j=PLACES)
                step = PLACES // pieces
                for j0 in range(0, PLACES, step):
                    piece = keep_tile([PARTS, step, P], BF16, "rows4%s%d%d" % (s, c, j0))
                    nc.sync.dma_start(out=piece[:], in_=src[:, j0 : j0 + step, :])
                    rows4[s, c] = piece
                    for j in range(step):
                        rows4[s, c, j0 + j] = piece[:, j, :]

            def load_tb(c, h):
                tb_rows[c, h] = keep_tile([PARTS, PLACES, PASS], BF16, "tbr%d%d" % (c, h))
                nc.sync.dma_start(out=tb_rows[c, h][:], in_=tb[span(c, PASS), span(h, PASS)].rearrange("(p j) w -> p j w", j=PLACES))

            def load_delta(h, b0, b1, w0=0, w1=PASS, queue=nc.sync):
                delta_rows[h, b0, w0] = keep_tile([PARTS, b1 - b0, w1 - w0], BF16, "dr%d%d%d" % (h, b0, w0))
                queue.dma_start(out=delta_rows[h, b0, w0][:], in_=dealt(delta, b0, b1, slice(PASS * h + w0, PASS * h + w1)))

            def load_ta(q):
                rows = keep_tile([PARTS, 2, N], BF16, "tar%d" % q)
                nc.sync.dma_start(out=rows[:], in_=dealt(ta, 2 * q, 2 * q + 2, slice(0, N)))
                for k in range(2):
                    ta_rows[2 * q + k] = rows[:, k, :]

            def move(engine, out, src):
                if engine == GPSIMD:
                    nc.gpsimd.tensor_scalar(out=out, in0=src, scalar1=1.0, scalar2=-0.0, op0=ALU.mult, op1=ALU.add)
                elif engine == VECTOR:
                    nc.vector.tensor_copy(out=out, in_=src)
                else:
                    nc.scalar.copy(out=out, in_=src)

            def quantise(codes, scale, values):
                nc.vector.quantize_mx(out=codes.bitcast(FP8X4), scales=scale, in_=values)

            scaled, grouped = {}, {}

            def factor_mult(s, c, slot):
                scaled[s, c] = keep_tile([PARTS, PLACES * P], BF16, "scaled", slot)
                for j in range(PLACES):
                    nc.vector.tensor_scalar(out=scaled[s, c][:, span(j, P)], in0=rows4[s, c, j], scalar1=gain[s][:, c, j : j + 1], scalar2=None, op0=ALU.mult)

            def factor_group(s, c, engine, slot):
                grouped[s, c] = keep_tile([PARTS, PLACES * P], BF16, "grouped", slot)
                move(
                    engine,
                    grouped[s, c][:].rearrange("p (t m e j) -> p m t e j", t=PLACES, e=2, j=PLACES),
                    scaled[s, c][:].rearrange("p (j m e t) -> p m t e j", t=PLACES, e=2, j=PLACES),
                )

            ba_bank, ga_bank = {}, {}

            def ba_turn(r, banks=None):
                c = r // 4
                for lo in range(2):
                    if banks:
                        ba_bank[c, lo] = bank_tile(banks[lo])
                    out = ba_bank[c, lo][:].rearrange("p a n -> p (a n)").bitcast(BF16)
                    for hi in range(2):
                        nc.tensor.transpose(out[:, span(4 * hi + r % 4, PARTS)], ba_rows[r][:, 2 * hi + lo :: PLACES], ident_bf[:])

            def ba_words(c, lo, engine):
                dst = ba_t[c][:].bitcast(F32).rearrange("p (u lo q hi) -> p u lo q hi", u=2, lo=2, hi=2)[:, :, lo, :, :]
                move(engine, dst, ba_bank[c, lo][:].rearrange("p a n -> p (a n)").rearrange("p (hi q u) -> p u q hi", hi=2, u=2))

            def ba_turn_back(c, lo, bank):
                ga_bank[c, lo] = bank_tile(bank)
                words = ba_t[c][:].bitcast(F32)
                for u in range(2):
                    for hi in range(2):
                        start = PAIR * (2 * u + lo) + hi
                        nc.tensor.transpose(ga_bank[c, lo][:, 2 * u + hi, :], words[:, start : PAIR * (2 * u + lo + 1) : 2], ident[:])

            def ga_mult(c, lo, slot=None):
                if slot:
                    grouped["a", c] = keep_tile([PARTS, PLACES * P], BF16, "grouped", slot)
                src = ga_bank[c, lo][:].rearrange("p a n -> p (a n)").bitcast(BF16)
                nc.vector.tensor_tensor(
                    out=grouped["a", c][:, span(lo, 2 * P)].rearrange("p (w u e) -> p w u e", u=2, e=2),
                    in0=src.rearrange("p (u w e) -> p w u e", u=2, e=2),
                    in1=gain["a"][:, c, :].rearrange("p (u e) -> p u e", e=2).unsqueeze(1).to_broadcast([PARTS, PAIR, 2, 2]),
                    op=ALU.mult,
                )

            def factor_quantise(s, c):
                quantise(gcodes[s, c][:], gscale[s, c][:], grouped[s, c][:])

            def tb_group(c, h, slot, w0=0, w1=PASS, engine=GPSIMD):
                if slot:
                    grouped["t", c, h] = keep_tile([PARTS, PLACES * PASS], BF16, "grouped", slot)
                out = grouped["t", c, h][:].rearrange("p (w j) -> p w j", j=PLACES)[:, w0:w1, :]
                move(engine, out, tb_rows[c, h][:, :, w0:w1].rearrange("p j w -> p w j"))

            def tb_quantise(c, h, w0=0, w1=PASS):
                quantise(tbcodes[c, h][:, w0:w1], tbscale[c, h][:, w0:w1], grouped["t", c, h][:, PLACES * w0 : PLACES * w1])

            ta_bank, ta_t = {}, {}

            def ta_turn(b, bank):
                words = ta_rows[b].bitcast(F32)
                ta_bank[b] = bank_tile(bank)
                for c in range(2):
                    for u in range(2):
                        nc.tensor.transpose(ta_bank[b][:, 2 * c + u, :], words[:, PASS // 2 * c + u : PASS // 2 * (c + 1) : 2], ident[:])

            def ta_words(b, slot=None, engine=SCALAR):
                if slot:
                    ta_t[b // 2] = keep_tile([PARTS, 2 * PAIR * PLACES], BF16, "tat", slot)
                words = ta_t[b // 2][:].bitcast(F32).rearrange("p (c n u) -> p c n u", c=2, u=2)
                move(engine, words[:, :, span(b % 2, PARTS), :], ta_bank[b][:].rearrange("p (c u) n -> p c n u", c=2))

            def ta_quantise(q):
                quantise(tacodes[q][:].rearrange("p c n -> p (c n)"), tascale[q][:].rearrange("p c n -> p (c n)"), ta_t[q][:])

            factor_bank, y_bank = {}, {}

            def factor_turn(s, c, jj, bank):
                factor_bank[s, c, jj] = bank_tile(bank)
                for j in range(2):
                    words = rows4[s, c, 2 * jj + j].bitcast(F32)
                    for u in range(2):
                        nc.tensor.transpose(factor_bank[s, c, jj][:, 2 * j + u, :], words[:, u::2], ident[:])

            def factor_words(s, c, jj, engine=SCALAR):
                words, src = xt[s, c][:].bitcast(F32), factor_bank[s, c, jj][:]
                if s == "a":
                    move(engine, words[:, span(jj, PASS)].rearrange("p (j q u) -> p j q u", j=2, u=2), src.rearrange("p (j u) q -> p j q u", u=2))
                else:
                    move(engine, words.rearrange("p (q jj r) -> p q jj r", jj=2, r=4)[:, :, jj, :], src.rearrange("p r q -> p q r"))

            def dress(s, b, bank, c0=0, c1=2):
                if c0 == 0:
                    y_bank[s, b] = bank_tile(bank)
                for c in range(c0, c1):
                    if s == "a":
                        codes, scale = tacodes[b // 2][:, c, span(b % 2, PARTS)], tascale[b // 2][:, c, span(b % 2, PARTS)]
                    else:
                        codes, scale = tbcodes[c, b // 4][:, span(b % 4, PARTS)], tbscale[c, b // 4][:, span(b % 4, PARTS)]
                    for t in range(PLACES):
                        group = span(2 * (t % 2) + t // 2 if (s, c) == ("a", 1) else t, PARTS)
                        nc.tensor.matmul_mx(
                            out=y_bank[s, b][:, t, :],
                            lhsT=gcodes[s, c][:, group].bitcast(FP8X4),
                            lhsT_scale=gscale[s, c][:, group],
                            rhs=codes.bitcast(FP8X4),
                            rhs_scale=scale,
                            start=(c == 0 and t == 0),
                            stop=(c == 1 and t == PLACES - 1),
                        )

            def x_add(s, b):
                own = xt[s, b // 4][:, span(b % 4, PASS)].rearrange("p (n t) -> p n t", t=PLACES)
                addend = own
                if s == "a" and b >= 4:
                    own = own.rearrange("p n (hi lo) -> p n hi lo", lo=2)
                    addend = ba_t[b // 4][:].rearrange("p (u lo n hi e) -> p u e n hi lo", u=2, lo=2, hi=2, e=2)[:, b % 4 // 2, b % 2]
                    nc.vector.tensor_tensor(out=own, in0=y_bank[s, b][:].rearrange("p (hi lo) n -> p n hi lo", lo=2), in1=addend, op=ALU.add)
                else:
                    nc.vector.tensor_tensor(out=own, in0=y_bank[s, b][:].rearrange("p t n -> p n t"), in1=addend, op=ALU.add)

            def x_quantise(s, c, k0=0, k1=4):
                cols = slice(PASS * c + PARTS * k0, PASS * c + PARTS * k1)
                quantise(xcodes[s][:, cols], xscale[s][:, cols], xt[s, c][:, PASS * k0 : PASS * k1])

            def rec_rows(h, b0, b1):
                return rec[b0 // 4, h][:, b0 % 4 : b0 % 4 + b1 - b0, :]

            def root(h, b0, b1, w0=0, w1=PASS):
                nc.scalar.activation(out=rec_rows(h, b0, b1)[:, :, w0:w1], in_=delta_rows[h, b0, w0][:], func=ACT.Abs_reciprocal_sqrt)

            def square(h, b0, b1):
                nc.scalar.activation(out=rec_rows(h, b0, b1), in_=rec_rows(h, b0, b1), func=ACT.Square)

            prod = {}

            def product(b, h, bank):
                prod[b, h] = bank_tile(bank)[:].rearrange("p t n -> p (t n)")
                nc.tensor.matmul_mx(
                    out=prod[b, h],
                    lhsT=xcodes["a"][:, span(b, PARTS)].bitcast(FP8X4),
                    lhsT_scale=xscale["a"][:, span(b, PARTS)],
                    rhs=xcodes["b"][:, span(h, PASS)].bitcast(FP8X4),
                    rhs_scale=xscale["b"][:, span(h, PASS)],
                    start=True,
                    stop=True,
                )

            def divide(b, h):
                own = rec[b // 4, h][:, b % 4, :]
                nc.vector.scalar_tensor_tensor(out=own, in0=prod[b, h], scalar=-1.0, in1=own, op0=ALU.mult, op1=ALU.mult)

            rounded, plane_bank, plane_t = {}, {}, {}

            def narrow(q, h, engine, slot, k0=0, k1=2):
                if slot:
                    rounded[q, h] = keep_tile([PARTS, 2 * PASS], BF16, "rb", slot)
                words = slice(PARTS * k0, PARTS * k1)
                out = rounded[q, h][:].rearrange("p (u w e) -> p u w e", u=2, e=2)[:, :, words, :]
                src = rec_rows(h, 2 * q, 2 * q + 2).rearrange("p k (w u e) -> p u (k w) e", u=2, e=2)[:, :, words, :]
                if engine != GPSIMD:
                    out, src = out.rearrange("p u (a w) e -> p a u w e", w=4), src.rearrange("p u (a w) e -> p a u w e", w=4)
                move(engine, out, src)

            def plane_turn(q, h, bank):
                plane_bank[q, h] = bank_tile(bank)
                words = rounded[q, h][:].bitcast(F32)
                for k in range(2):
                    for u in range(2):
                        nc.tensor.transpose(plane_bank[q, h][:, 2 * k + u, :], words[:, span(2 * u + k, PARTS)], ident[:])

            def plane_words(q, h, slot=None, p0=0, p1=PARTS):
                if slot:
                    plane_t[q // 2, h] = keep_tile([PARTS, PLACES * PASS], BF16, "pt", slot)
                words = plane_t[q // 2, h][:].bitcast(F32).rearrange("p (n jj r) -> p n jj r", jj=2, r=4)
                move(SCALAR, words[:, p0:p1, q % 2, :], plane_bank[q, h][:, :, p0:p1].rearrange("p r n -> p n r"))

            def store_r(q, h, k0=0, k1=2):
                nc.sync.dma_start(out=dealt(out_0, 2 * q + k0, 2 * q + k1, span(h, PASS)), in_=rec_rows(h, 2 * q + k0, 2 * q + k1))

            def plane_quantise(h, b0, b1):
                cols = slice(PARTS * b0, PARTS * b1)
                quantise(pcodes[h][:, cols], pscale[:, h, cols], plane_t[b0 // 4, h][:, PASS * (b0 % 4) : PASS * (b0 % 4 + b1 - b0)])

            def plane_store(h, b0, b1):
                cols = slice(PARTS * b0, PARTS * b1)
                nc.sync.dma_start(out=out_1[h, :, cols, :].rearrange("p n f -> p (n f)").bitcast(I32), in_=pcodes[h][:, cols].bitcast(I32))

            def plane_out(h, b0, b1):
                plane_quantise(h, b0, b1)
                plane_store(h, b0, b1)

            def store_scales():
                for quad in range(PARTS // QUADRANT):
                    (nc.scalar, nc.sync)[quad % 2].dma_start(
                        out=out_2[:, span(quad, 4), :].rearrange("g r n -> r g n").bitcast(I32),
                        in_=pscale[QUADRANT * quad : QUADRANT * quad + 4, :, :].bitcast(I32),
                    )


            load_gain("a", ga, nc.scalar)
            load_gain("b", gb, nc.scalar)
            load_rows4("a", 0, pieces=2)
            load_delta(LEFT, 0, 1)
            load_ba(4, 6)
            load_ba(6, 8)
            load_rows4("b", 0)
            load_ta(0)
            load_delta(LEFT, 1, 2)
            load_tb(0, LEFT)
            load_ta(1)
            load_ta(2)
            load_rows4("b", 1)
            load_tb(1, LEFT)
            load_delta(LEFT, 2, 4)
            load_ta(3)
            load_delta(LEFT, 4, 8)
            load_tb(0, RIGHT)
            load_tb(1, RIGHT)
            load_delta(RIGHT, 0, 4)
            load_delta(RIGHT, 4, 8)

            root(LEFT, 0, 1)
            factor_turn("a", 0, 0, 0)
            factor_turn("a", 0, 1, 1)
            factor_mult("a", 0, "s0")
            factor_group("a", 0, VECTOR, "g0")
            factor_words("a", 0, 0)
            factor_words("a", 0, 1)
            square(LEFT, 0, 1)
            ba_turn(4, (2, 3))
            for r in range(5, 8):
                ba_turn(r)
            factor_quantise("a", 0)
            factor_mult("b", 0, "s1")
            ba_words(1, 0, SCALAR)
            ba_words(1, 1, SCALAR)
            for jj in range(2):
                factor_turn("b", 0, jj, 4 + jj)
            ba_turn_back(1, 0, 6)
            ba_turn_back(1, 1, 7)
            factor_group("b", 0, VECTOR, "g3")
            for jj in range(2):
                factor_words("b", 0, jj)
            tb_group(0, LEFT, "g2", 0, 256)
            ga_mult(1, 0, "g1")
            ga_mult(1, 1)
            for b in range(6):
                ta_turn(b, b)
            root(LEFT, 1, 2)
            ta_words(0, "t0", VECTOR)
            ta_words(1)
            for q in range(1, 3):
                ta_words(2 * q, "t%d" % q)
                ta_words(2 * q + 1)
            tb_group(0, LEFT, None, 256, 512, SCALAR)
            factor_quantise("a", 1)
            ta_quantise(0)
            factor_quantise("b", 0)
            ta_quantise(1)
            factor_mult("b", 1, "s1")
            factor_group("b", 1, SCALAR, "g1")
            ta_quantise(2)
            tb_quantise(0, LEFT, 0, 256)

            tb_group(1, LEFT, "t2")
            for b, bank in enumerate((6, 7, 0, 1, 2)):
                dress("a", b, bank)
            ta_turn(6, 3)
            ta_turn(7, 4)
            dress("a", 5, 5)
            ta_words(6, "t0")
            ta_words(7)
            root(LEFT, 2, 4)
            for b in range(5):
                x_add("a", b)
            factor_turn("b", 1, 0, 6)
            factor_turn("b", 1, 1, 7)
            factor_quantise("b", 1)
            tb_quantise(1, LEFT)
            tb_quantise(0, LEFT, 256, 512)
            x_quantise("a", 0)
            ta_quantise(3)
            for jj in range(2):
                factor_words("b", 1, jj)

            tb_group(0, RIGHT, "xta0")
            tb_group(1, RIGHT, "g0", 0, PASS // 2)
            for b, bank in enumerate((0, 1, 2, 3)):
                dress("b", b, bank)
            dress("a", 6, 4)
            dress("a", 7, 6)
            root(LEFT, 4, 8)
            square(LEFT, 1, 4)
            x_add("a", 5)
            for b in range(4):
                x_add("b", b)
            x_add("a", 6)
            x_add("a", 7)
            square(LEFT, 4, 8)
            x_quantise("b", 0)
            x_quantise("a", 1)
            tb_quantise(1, RIGHT, 0, PASS // 2)
            tb_quantise(0, RIGHT)

            tb_group(1, RIGHT, "g0", PASS // 2, PASS)
            for b, bank in ((0, 7), (1, 5), (3, 1), (2, 0), (4, 2)):
                product(b, LEFT, bank)
            dress("b", 4, 4)
            dress("b", 5, 3)
            root(RIGHT, 0, 4)
            root(RIGHT, 4, 8)
            divide(0, LEFT)
            divide(1, LEFT)
            store_r(0, LEFT)
            divide(2, LEFT)
            tb_quantise(1, RIGHT, PASS // 2, PASS)
            narrow(0, LEFT, GPSIMD, "g0")
            dress("b", 6, 7)
            dress("b", 7, 6)
            divide(3, LEFT)
            store_r(1, LEFT)
            narrow(1, LEFT, GPSIMD, "s1")
            divide(4, LEFT)
            product(5, LEFT, 5)
            plane_turn(0, LEFT, 0)
            for b in range(4, 8):
                x_add("b", b)
            square(RIGHT, 0, 2)
            plane_words(0, LEFT, "g1")
            plane_turn(1, LEFT, 4)
            square(RIGHT, 2, 4)
            plane_words(1, LEFT)
            square(RIGHT, 4, 6)
            product(6, LEFT, 6)
            divide(5, LEFT)
            product(7, LEFT, 5)
            x_quantise("b", 1)
            store_r(2, LEFT)
            narrow(2, LEFT, GPSIMD, "t0")
            divide(6, LEFT)
            divide(7, LEFT)
            store_r(3, LEFT)
            narrow(3, LEFT, GPSIMD, "t2")

            for b, bank in enumerate((2, 3, 7, 1)):
                product(b, RIGHT, bank)
            plane_turn(2, LEFT, 0)
            product(4, RIGHT, 6)
            product(5, RIGHT, 5)
            plane_words(2, LEFT, "g2")
            square(RIGHT, 6, 8)
            divide(0, RIGHT)
            divide(1, RIGHT)
            store_r(0, RIGHT)
            narrow(0, RIGHT, GPSIMD, "xtb0")
            plane_turn(3, LEFT, 4)
            product(6, RIGHT, 2)
            product(7, RIGHT, 3)
            plane_words(3, LEFT)
            divide(2, RIGHT)
            divide(3, RIGHT)
            store_r(1, RIGHT)
            narrow(1, RIGHT, GPSIMD, "xtb1")
            plane_turn(0, RIGHT, 7)
            divide(4, RIGHT)
            divide(5, RIGHT)
            store_r(2, RIGHT)
            narrow(2, RIGHT, SCALAR, "s0")
            plane_words(0, RIGHT, "xta0")
            plane_turn(1, RIGHT, 1)
            plane_words(1, RIGHT)
            plane_turn(2, RIGHT, 0)
            divide(6, RIGHT)
            store_r(3, RIGHT, 0, 1)
            divide(7, RIGHT)
            store_r(3, RIGHT, 1, 2)
            narrow(3, RIGHT, VECTOR, "s1", 0, 1)
            narrow(3, RIGHT, VECTOR, None, 1, 2)
            plane_out(LEFT, 0, 4)
            plane_out(LEFT, 4, 8)
            plane_words(2, RIGHT, "t1")
            plane_turn(3, RIGHT, 6)
            plane_words(3, RIGHT, None, 0, 64)
            plane_words(3, RIGHT, None, 64, 128)
            plane_out(RIGHT, 0, 4)
            plane_quantise(RIGHT, 4, 6)
            plane_quantise(RIGHT, 6, 8)
            plane_store(RIGHT, 4, 8)
            store_scales()
